import numpy as np, ml_dtypes
CORES = [3,11,19,27,35,43,51,59]
N = 8
BF = ml_dtypes.bfloat16
def gentries(a):
    return np.ascontiguousarray(a.reshape(8, 16, -1).transpose(0, 2, 1)).reshape(8, -1)
def gtable(e):
    e = np.asarray(e); return np.ascontiguousarray(e.reshape(8, -1, 16).transpose(0, 2, 1)).reshape(128, -1).astype(np.int32)
I, W, PL, RO, CNT, B, AS = 192, 3072, 2048, 8, 12, 24, 64
def records(x, s):
    return np.take_along_axis(x, s.transpose(0, 1, 3, 2).reshape(N, 8, 1, 16 * I), 3).reshape(N, 8, 16, I, 16)
def dist(xs, z):
    return np.sum(np.abs(xs - z[..., None]), axis=2).transpose(0, 1, 3, 2)
def parts(rng):
    x = (256 * rng.random((N, 8, 16, W)) * rng.choice(np.array([1.0, 1.0, 0.5, 0.25]), (N, 8, 1, W))).astype(np.int64)
    z = rng.integers(0, 256, (N, 8, 16, I)); f = rng.integers(0, 256, (N, 8, 16, I))
    s = rng.integers(0, W, (N, 8, 16, I)); pl = rng.integers(0, W, (N, 8, 16, PL)); p = rng.integers(0, PL, (N, 8, I))
    th = rng.integers(300, 1300, (N, 8, 1, I)) + rng.integers(0, 200, (N, 8, 16, I))
    return x, z, f, s, pl, p, th
def pack(x, z, f, s, pl, p, th):
    return {"x0": x.reshape(N, 128, W).astype(np.float32).astype(BF), "z0": z.reshape(N, 128, I).astype(np.float32).astype(BF), "f0": f.reshape(N, 128, I).astype(np.float32).astype(BF),
            "s0": s.reshape(N, 128, I).astype(np.int32), "pl": pl.reshape(N, 128, PL).astype(np.int32), "p0": np.stack([gtable(a) for a in p]), "th": th.reshape(N, 128, I).astype(np.int32)}
def setup_inputs(rng):
    return pack(*parts(rng))
def setup_inputs_spread(rng):
    x = (np.exp2(8 * rng.random((N, 8, 1, W))) * rng.random((N, 8, 16, W))).astype(np.int64)
    z = (np.exp2(8 * rng.random((N, 8, 1, I))) * rng.random((N, 8, 16, I))).astype(np.int64)
    f = (np.exp2(8 * rng.random((N, 8, 1, I))) * rng.random((N, 8, 16, I))).astype(np.int64)
    s = (W * rng.random((N, 8, 16, I)) ** 3).astype(np.int64); pl = (W * rng.random((N, 8, 16, PL)) ** 2).astype(np.int64); p = (PL * rng.random((N, 8, I)) ** 3).astype(np.int64)
    th = np.minimum((np.exp2(5 + 7 * rng.random((N, 8, 1, I))) * (0.5 + 0.5 * rng.random((N, 8, 16, I)))).astype(np.int64), 4080)
    return pack(np.minimum(x, 255), np.minimum(z, 255), np.minimum(f, 255), np.minimum(s, W - 1), np.minimum(pl, W - 1), np.minimum(p, PL - 1), th)
def setup_inputs_ends(rng):
    def mix(n):
        return np.where(rng.random((N, 8, 1, n)) < 0.5, rng.integers(0, 2, (N, 8, 16, n)), rng.integers(0, 2, (N, 8, 1, n)))
    x = 255 * mix(W); z = 255 * mix(I); f = 255 * mix(I); th = 4080 * mix(I)
    s = (W - 1) * rng.integers(0, 2, (N, 8, 16, I)); pl = (W - 1) * rng.integers(0, 2, (N, 8, 16, PL)); p = (PL - 1) * rng.integers(0, 2, (N, 8, I))
    x[:, 1::2, :, W - 1] = 255; x[:, 1::2, :, 0] = 0; x[:, 0:4:2, :, W - 1] = 0; x[:, 0:4:2, :, 0] = 255
    pl[:, 7, :, PL - 1] = W - 1; pl[:, 7, :, 0] = 0; pl[:, 7, 0, 768] = 0
    for i in (0, 1, I - 2, I - 1):
        z[:, 7, :, i] = 0; f[:, 7, :, i] = 0; s[:, 7, :, i] = W - 1; th[:, 7, :, i] = 4080; p[:, 7, i] = PL - 1
    for i in (2, 3, I - 4, I - 3):
        z[:, 7, :, i] = 255; f[:, 7, :, i] = 255; s[:, 7, :, i] = 0; th[:, 7, :, i] = 4080; p[:, 7, i] = 0
    return pack(x, z, f, s, pl, p, th)
def setup_inputs_ties(rng):
    x, z, f, s, pl, p, th = parts(rng)
    x = 64 * rng.integers(0, 4, (N, 8, 16, W)); z = 64 * rng.integers(0, 4, (N, 8, 16, I))
    few = np.take_along_axis(rng.integers(0, W, (N, 8, 3, I)), rng.integers(0, 3, (N, 8, 16, I)), 2)
    s = np.where(rng.random((N, 8, 1, I)) < 0.5, few, s)
    ds = dist(records(x, s), z); dp = dist(records(x, np.take_along_axis(pl, p[:, :, None, :], 3)), z)
    one = (rng.random((N, 8, 16, I)) < 0.08).astype(np.int64); k = rng.integers(0, 3, (N, 8, 1, I))
    th = np.where(k == 0, ds + one, np.where(k == 1, np.minimum(dp + one, ds), np.minimum(dp, ds)))
    return pack(x, z, f, s, pl, p, np.minimum(th, 4080))
def setup_inputs_odd(rng):
    x, z, f, s, pl, p, th = parts(rng); h = W // 2
    o = np.argsort(rng.random((N, 8, W)), axis=-1)
    hi = np.zeros((N, 8, W), np.int64); np.put_along_axis(hi, o[:, :, h:], 1, 2)
    x = rng.integers(0, 56, (N, 8, 16, W)) + 200 * hi[:, :, None, :]; x[:, :, 15] ^= np.sum(x, axis=2) & 1
    kz = rng.integers(0, 2, (N, 8, 1, I)); z = rng.integers(0, 56, (N, 8, 16, I)) + 200 * kz; z[:, :, 15] ^= (np.sum(z, axis=2) & 1) ^ 1
    s = np.take_along_axis(o, (rng.integers(0, h, (N, 8, 16, I)) + h * (1 - kz)).reshape(N, 8, 16 * I), 2).reshape(N, 8, 16, I)
    pl = np.take_along_axis(o, (rng.integers(0, h, (N, 8, 16, PL)) + h * (np.arange(PL) & 1)).reshape(N, 8, 16 * PL), 2).reshape(N, 8, 16, PL)
    p = 2 * rng.integers(0, PL // 2, (N, 8, I)) + 1 - kz[:, :, 0]
    x[:, :, :, W - 1] = 255; x[:, ::2, :, W - 3] = 0; x[:, 1::2, :, 1] = 0
    pl[:, :, 0, PL - 1] = W - 1; pl[:, ::2, 0, 0] = W - 3; pl[:, 1::2, 0, 0] = 1
    ds = dist(records(x, s), z); dp = dist(records(x, np.take_along_axis(pl, p[:, :, None, :], 3)), z)
    one = (rng.random((N, 8, 16, I)) < 0.08).astype(np.int64); k = rng.integers(0, 3, (N, 8, 1, I))
    th = np.where(k == 0, ds + one, np.where(k == 1, np.minimum(dp + one, ds), np.minimum(dp, ds)))
    th = np.minimum(th, 4080)
    for i in (0, 1, I - 2, I - 1):
        z[:, :, :, i] = 0; f[:, :, :, i] = 0; s[:, :, 0, i] = W - 1; p[:, :, i] = PL - 1; th[:, :, :, i] = 0; th[:, :, 0, i] = 4080
    return pack(x, z, f, s, pl, p, th)
def setup_inputs_corners(rng):
    x, z, f, s, pl, p, th = parts(rng)
    k = rng.integers(0, 8, (N, 8, I)); k[:, :, I - 8:] = np.arange(8); k = k[:, :, None, :]; row = np.arange(16)[:, None]
    th = 4080 * ((((k == 1) | (k == 4) | (k == 5)) & (row == 15)) | ((k == 2) & (row == 0)) | (k == 3)).astype(np.int64)
    th = np.where(k == 7, rng.integers(0, 4081, (N, 8, 16, I)), th)
    z = np.where(k == 4, 255, np.where((k == 5) | (k == 7) | ((k == 0) & (rng.random((N, 8, 1, I)) < 0.5)), 0, z))
    z = np.where(k == 6, np.where(row == 1, 100, 15), z)
    s = np.where(k == 2, (W - 1) * rng.integers(0, 2, s.shape), s); s = np.where(k == 3, rng.integers(0, W, (N, 8, 1, I)), s)
    s = np.where(k == 7, 16 * np.arange(I) + rng.integers(0, 16, s.shape), s); s = np.where((k == 5) & (row == 15), W - 1, s)
    x[:, :, :, W - 1] = 255
    pl[:, :, :, 0] = rng.integers(0, W - 1, (N, 8, 1)); pl[:, :, :, PL - 1] = W - 1; pl[:, :, 15, :] = rng.integers(0, W - 1, (N, 8, PL))
    e = rng.integers(0, 4, (N, 8, I)); p = np.where(e == 0, 0, np.where(e == 1, PL - 1, p))
    return pack(x, z, f, s, pl, p, th)
def check_inputs(d):
    bad = []
    for k, lo, hi in (("x0", 0, 255), ("z0", 0, 255), ("f0", 0, 255), ("s0", 0, W - 1), ("pl", 0, W - 1), ("p0", 0, PL - 1), ("th", 0, 4080)):
        v = np.asarray(d[k]).astype(np.float64)
        if not np.all((v >= lo) & (v <= hi) & (v == np.floor(v))): bad.append("range of " + k)
    return bad
def reference(x0, z0, f0, s0, pl, p0, th):
    X = x0.astype(np.float32).astype(np.int32).reshape(N, 8, 16, W); z = z0.astype(np.float32).astype(np.int32).reshape(N, 8, 16, I); f = f0.astype(np.float32).astype(np.int32).reshape(N, 8, 16, I)
    S = s0.astype(np.int32).reshape(N, 8, 16, I); plans = pl.astype(np.int32).reshape(N, 8, 16, PL); lim = th.astype(np.int32).reshape(N, 8, 16, I)
    P = np.stack([gentries(a) for a in p0]).astype(np.int32); A = np.zeros((N, 8, I), np.int32)
    row = np.arange(16)[:, None]; wt = (2 * np.arange(16) + 1)[:, None]
    for t in range(RO):
        e = np.take_along_axis(plans, P[:, :, None, :], 3)
        xs = records(X, S); xe = records(X, e); bound = lim + AS * A[:, :, None, :]
        rs = dist(xs, z) < bound; rp = dist(xe, z) < bound
        c1 = np.any(rs, axis=2); c2 = ~c1 & np.any(rp, axis=2); c3 = ~c1 & ~c2
        j = np.argmax(rs, axis=2); jp = np.argmax(rp, axis=2)
        u = np.sum(wt * z, axis=2) & 4095; A = A + c3; P = np.where(c3, ((u * u >> 5) + 37 * u) & (PL - 1), P).astype(np.int32)
        low = np.sum(xs <= z[..., None], axis=2).transpose(0, 1, 3, 2)
        R = np.where(c1[:, :, None, :] & (low >= CNT) & (row != j[:, :, None, :]), e, S)
        t1 = np.take_along_axis(S, j[:, :, None, :], 2)[:, :, 0]; t2 = np.take_along_axis(e, jp[:, :, None, :], 2)[:, :, 0]; t3 = np.take_along_axis(plans[:, :, 0], P, 2)
        top = np.where(c1, t1, np.where(c2, t2, t3)); last = np.where(c1, j, 15)
        S = np.where(row <= last[:, :, None, :], np.concatenate([top[:, :, None, :], R[:, :, :15]], axis=2), R).astype(np.int32)
        f = (f + z) >> 1
        y = np.abs(np.take_along_axis(X, S[:, :, :1, :], 3) - f)
        place = 16 * np.arange(I) + (np.sum(y, axis=2) & 15)
        np.put_along_axis(X, place[:, :, None, :], (y + z) >> 1, 3)
        if t < RO - 1:
            z = np.concatenate([np.roll(y[..., b * B:(b + 1) * B], b + t, axis=0) for b in range(N)], axis=3)
    yx = np.sum(X.reshape(N, 8, 16, I, 16) * np.arange(1, 17), axis=4)
    return {"ys": S.reshape(N, 128, I).astype(np.float32), "yp": np.stack([gtable(a) for a in P + PL * A]).astype(np.float32),
            "yf": f.reshape(N, 128, I).astype(np.float32).astype(BF), "yx": yx.reshape(N, 128, I).astype(np.float32)}

@@ -1,0 +1,583 @@
+import numpy as np
+from concourse.bass import DstId, RemoteDMATransfer
+from concourse.mybir import dt, AluOpType, AxisListType, ActivationFunctionType
+
+A = AluOpType
+F = ActivationFunctionType
+I, W, PLN, TURNS, BLK, N = 192, 3072, 2048, 8, 24, 8
+NK = 2
+NQ = 0
+NF = 0
+NS = 2
+CSPL = 152
+XC = 3
+TR = 0.5
+NC = 16 // NK
+CW = NK * I
+CEN = 1536.0
+MAGIC = 12582912.0
+MAGIC16 = 201326592.0
+
+SCRATCH = {
+    "X": ("sbuf", [128, W], "bfloat16"),
+    "XS": ("sbuf", [128, W], "bfloat16"), "XE": ("sbuf", [128, W], "bfloat16"),
+    "D": ("sbuf", [128, W], "bfloat16"), "AB": ("sbuf", [128, W], "bfloat16"),
+    "SG": ("sbuf", [128, W], "bfloat16"), "MX": ("sbuf", [128, W], "bfloat16"),
+    "PLT": ("sbuf", [128, PLN], "int32"), "SI": ("sbuf", [128, I], "int32"), "THI": ("sbuf", [128, I], "int32"),
+    "PI": ("sbuf", [128, 12], "int32"), "PF": ("sbuf", [128, 12], "float32"),
+    "BND": ("sbuf", [128, I], "float32"), "C64": ("sbuf", [128, I], "float32"), "KK": ("sbuf", [128, I], "float32"),
+    "RS": ("sbuf", [128, I], "bfloat16"), "RP": ("sbuf", [128, I], "bfloat16"), "FI": ("sbuf", [128, I], "bfloat16"),
+    "CR": ("sbuf", [128, I], "bfloat16"), "DES": ("sbuf", [128, I], "float32"), "WD": ("sbuf", [128, I], "float32"),
+    "RR": ("sbuf", [128, I], "float16"), "QQ": ("sbuf", [128, I], "float16"), "FF": ("sbuf", [128, I], "float16"),
+    "GG": ("sbuf", [128, I], "float16"), "HH": ("sbuf", [128, I], "float16"), "HF": ("sbuf", [128, I], "float16"),
+    "E16": ("sbuf", [128, I], "float16"), "CAND": ("sbuf", [128, I], "float16"),
+    "SU": ("sbuf", [128, I], "uint16"), "EU": ("sbuf", [128, I], "uint16"),
+    "TU": ("sbuf", [128, 12], "uint16"), "PU": ("sbuf", [128, 12], "uint16"), "MU": ("sbuf", [128, 12], "uint16"),
+    "FA": ("sbuf", [128, I], "bfloat16"), "FB": ("sbuf", [128, I], "bfloat16"),
+    "YD": ("sbuf", [128, I], "bfloat16"), "WR": ("sbuf", [128, I], "bfloat16"),
+    "H1": ("sbuf", [128, 12], "int32"), "H2": ("sbuf", [128, 12], "int32"), "H3": ("sbuf", [128, 12], "int32"),
+    "H4": ("sbuf", [128, 12], "int32"),
+    "H7": ("sbuf", [128, 12], "int32"), "DP": ("sbuf", [128, 12], "float32"), "DQ": ("sbuf", [128, 12], "float32"),
+    "QF": ("sbuf", [128, 12], "float32"), "RF": ("sbuf", [128, 12], "float32"), "MF": ("sbuf", [128, 12], "float32"),
+    "YPF": ("sbuf", [128, 12], "float32"),
+    "ip": ("sbuf", [128, 1], "int32"), "ig": ("sbuf", [128, 1], "int32"), "irow": ("sbuf", [128, 144], "int32"),
+    "igrow": ("sbuf", [128, 128], "int32"), "ibase": ("sbuf", [128, 12], "int32"),
+    "pf": ("sbuf", [128, 1], "float32"), "p1": ("sbuf", [128, 1], "float32"), "gf": ("sbuf", [128, 1], "float32"),
+    "g16": ("sbuf", [128, 1], "float32"), "g15": ("sbuf", [128, 1], "float32"), "lf": ("sbuf", [128, 1], "float32"),
+    "l21": ("sbuf", [128, 1], "float32"), "l0": ("sbuf", [128, 1], "float32"), "nl0": ("sbuf", [128, 1], "float32"),
+    "nl15": ("sbuf", [128, 1], "float32"), "r16": ("sbuf", [128, 1], "float32"),
+    "row": ("sbuf", [128, 144], "float32"), "grow": ("sbuf", [128, 128], "float32"), "base": ("sbuf", [128, 12], "float32"),
+    "W1": ("sbuf", [128, 144], "bfloat16"), "W2": ("sbuf", [128, 144], "bfloat16"), "Wm": ("sbuf", [128, 144], "bfloat16"),
+    "Wu": ("sbuf", [128, 144], "bfloat16"), "Wh": ("sbuf", [128, 144], "float16"),
+    "OB": ("sbuf", [128, 128], "bfloat16"), "OBm": ("sbuf", [128, 128], "bfloat16"), "Ib": ("sbuf", [128, 128], "bfloat16"),
+    "Im": ("sbuf", [128, 128], "bfloat16"), "im8": ("sbuf", [128, 128], "int32"), "mk": ("sbuf", [128, 128], "float32"),
+    "Ihf": ("sbuf", [128, 128], "bfloat16"), "I100": ("sbuf", [128, 128], "bfloat16"), "GT": ("sbuf", [128, 128], "bfloat16"),
+    "Ls": ("sbuf", [128, 128], "bfloat16"), "Li": ("sbuf", [128, 128], "bfloat16"),
+    "Ih": ("sbuf", [128, 128], "float16"), "Sh": ("sbuf", [128, 128], "float16"),
+    "ShI": ("sbuf", [128, 128], "float16"), "Tp": ("sbuf", [128, 128], "float16"), "TpI": ("sbuf", [128, 128], "float16"),
+    "cq": ("sbuf", [128, I], "bfloat16"), "zz": ("sbuf", [128, I], "bfloat16"), "c75": ("sbuf", [128, 16], "bfloat16"),
+    "IC": ("sbuf", [128, 16 * 128], "bfloat16"),
+    "OS": ("sbuf", [128, I], "float32"), "OX": ("sbuf", [128, I], "float32"),
+}
+for _t in range(8):
+    SCRATCH["L%d" % _t] = ("sbuf", [128, I], "bfloat16")
+    SCRATCH["Y%d" % _t] = ("sbuf", [128, I], "bfloat16")
+for _t in range(8):
+    SCRATCH["b%d" % _t] = ("psum", [128, 512], "float32")
+NDMA = 12
+SEMAPHORES = ["qV", "qS", "qT", "qG", "sent"] + ["arr%d" % t for t in range(8)] + ["dm%d" % k for k in range(NDMA)]
+
+LAT = 0.08
+HOLD = 0.15
+BONUS = {}
+
+
+def _build():
+    ops = []
+
+    def add(q, fn, rd, wr, cost, **kw):
+        ops.append([q, fn, [(r if len(r) == 3 else (r[0], 0, 1 << 20)) for r in rd], [(r if len(r) == 3 else (r[0], 0, 1 << 20)) for r in wr], cost, kw])
+
+    def al(*names):
+        return [(n,) for n in names]
+
+    CY = 0.00083
+
+    def V(fn, rd, wr, n, f=1.0):
+        add("V", fn, rd, wr, 0.055 + max(64, n * f) * CY)
+
+    def S(fn, rd, wr, n, f=1.0):
+        add("S", fn, rd, wr, 0.15 + n * f * CY)
+
+    def MM(out, lhsT, rhs, start, stop, rd, wr, n):
+        add("T", lambda g, T: g.tensor.matmul(out(T), lhsT(T), rhs(T), start, stop), rd, wr, max(64, n) * CY * TR)
+
+    def tt(o, a, b, op):
+        return lambda g, T: g.vector.tensor_tensor(o(T), a(T), b(T), op)
+
+    def ts(o, a, s1, s2, op0, op1=None):
+        def fn(g, T):
+            x1 = s1(T) if callable_(s1) else s1
+            x2 = s2(T) if callable_(s2) else s2
+            if op1 is None:
+                return g.vector.tensor_scalar(o(T), a(T), x1, x2, op0)
+            return g.vector.tensor_scalar(o(T), a(T), x1, x2, op0, op1)
+        return fn
+
+    def callable_(x):
+        return x is not None and not isinstance(x, (int, float))
+
+    def tc(o, a):
+        return lambda g, T: g.vector.tensor_copy(o(T), a(T))
+
+    def act(o, a, f, **kw):
+        return lambda g, T: g.scalar.activation(o(T), a(T), f, **{k: (v(T) if callable_(v) else v) for k, v in kw.items()})
+
+    def B(name, a=None, b=None, st=None):
+        if a is None:
+            return lambda T: T[name][:]
+        if st is None:
+            return lambda T: T[name][:, a:b]
+        return lambda T: T[name][:, a:b:st]
+
+    def slide(name, k):
+        return lambda T: T[name][:, 15 - k:15 - k + 128]
+
+    nd = [0]
+
+    def load(q, dst, src, cost):
+        k = nd[0]
+        nd[0] += 1
+        add(q, lambda g, T: (g.sync if q == "Y" else g.scalar).dma_start(T[dst][:], T[src][:]), [], al(dst), cost, dma=k)
+
+    load("Y", "SI", "s0", 2.5)
+    load("S", "PI", "p0", 2.5)
+    load("Y", "X", "x0", 6.0)
+    load("S", "PLT", "pl", 6.0)
+    load("Y", "L0", "z0", 6.0)
+    load("Y", "THI", "th", 6.0)
+    load("S", "FA", "f0", 6.0)
+
+    def G(fn, wr, n):
+        add("G", fn, [], wr, 0.15 + 2 * n * CY)
+    G(lambda g, T: g.iota(T.ip[:], [[0, 1]], 0, 1), al("ip"), 1)
+    G(lambda g, T: g.iota(T.irow[:], [[1, 144]], 0, 0), al("irow"), 144)
+    G(lambda g, T: g.iota(T.ibase[:], [[256, 12]], 0, 0), al("ibase"), 12)
+    V(ts(B("ig"), B("ip"), 4, None, A.arith_shift_right), al("ip"), al("ig"), 1)
+    V(tc(B("pf"), B("ip")), al("ip"), al("pf"), 1)
+    V(tc(B("gf"), B("ig")), al("ig"), al("gf"), 1)
+    V(tc(B("row"), B("irow")), al("irow"), al("row"), 144)
+    V(ts(B("igrow"), B("irow", 0, 128), 4, None, A.arith_shift_right), al("irow"), al("igrow"), 128)
+    V(tc(B("grow"), B("igrow")), al("igrow"), al("grow"), 128)
+    V(ts(B("g16"), B("gf"), 16.0, None, A.mult), al("gf"), al("g16"), 1)
+    V(ts(B("g15"), B("gf"), 16.0, 15.0, A.mult, A.add), al("gf"), al("g15"), 1)
+    V(ts(B("p1"), B("pf"), 1.0, None, A.add), al("pf"), al("p1"), 1)
+    V(tt(B("lf"), B("pf"), B("g16"), A.subtract), al("pf", "g16"), al("lf"), 1)
+    V(ts(B("l21"), B("lf"), 2.0, 1.0, A.mult, A.add), al("lf"), al("l21"), 1)
+    V(ts(B("l0"), B("lf"), 0.0, None, A.is_equal), al("lf"), al("l0"), 1)
+    V(ts(B("nl0"), B("l0"), -1.0, None, A.mult), al("l0"), al("nl0"), 1)
+    V(ts(B("nl15"), B("lf"), 15.0, None, A.not_equal), al("lf"), al("nl15"), 1)
+    V(ts(B("r16"), B("lf"), 16.0, 7.5, A.mult, A.add), al("lf"), al("r16"), 1)
+    V(ts(B("base"), B("ibase"), B("r16"), None, A.add), al("ibase", "r16"), al("base"), 12)
+    V(ts(B("W1"), B("row"), B("g15"), None, A.is_equal), al("row", "g15"), al("W1"), 144)
+    V(ts(B("Wm"), B("row"), B("g15"), -1.0, A.is_equal, A.mult), al("row", "g15"), al("Wm"), 144)
+    V(ts(B("W2"), B("row"), B("g15"), 2.0, A.is_equal, A.mult), al("row", "g15"), al("W2"), 144)
+    V(ts(B("Wu"), B("row"), B("g15"), B("l21"), A.is_equal, A.mult), al("row", "g15", "l21"), al("Wu"), 144)
+    V(ts(B("Wh"), B("row"), B("g15"), None, A.is_equal), al("row", "g15"), al("Wh"), 144)
+    R128 = B("row", 0, 128)
+    V(ts(B("Ib"), R128, B("pf"), None, A.is_equal), al("row", "pf"), al("Ib"), 128)
+    V(ts(B("Ihf"), R128, B("pf"), 0.5, A.is_equal, A.mult), al("row", "pf"), al("Ihf"), 128)
+    V(ts(B("I100"), R128, B("pf"), -100.0, A.is_equal, A.mult), al("row", "pf"), al("I100"), 128)
+    V(ts(B("Ih"), R128, B("pf"), None, A.is_equal), al("row", "pf"), al("Ih"), 128)
+    V(ts(B("OB"), B("grow"), B("gf"), None, A.is_equal), al("grow", "gf"), al("OB"), 128)
+    V(ts(B("im8"), B("irow", 0, 128), NC - 1, None, A.bitwise_and), al("irow"), al("im8"), 128)
+    V(ts(B("mk"), B("im8"), NC - NQ - 0.5, -1.0, A.is_lt, A.mult), al("im8"), al("mk"), 128)
+    V(tt(B("OBm"), B("mk"), B("OB"), A.mult), al("mk", "OB"), al("OBm"), 128, 2)
+    V(ts(B("Im"), R128, B("pf"), -1.0, A.is_equal, A.mult), al("row", "pf"), al("Im"), 128)
+    V(ts(B("GT"), R128, B("pf"), None, A.is_gt), al("row", "pf"), al("GT"), 128)
+    V(tt(B("Ls"), B("GT"), B("OB"), A.mult), al("GT", "OB"), al("Ls"), 128, 2)
+    V(tt(B("Li"), B("Ls"), B("Ib"), A.add), al("Ls", "Ib"), al("Li"), 128, 2)
+    V(ts(B("Tp"), R128, B("g16"), None, A.is_equal), al("row", "g16"), al("Tp"), 128)
+    V(tt(B("TpI"), B("Tp"), B("Ih"), A.subtract), al("Tp", "Ih"), al("TpI"), 128, 2)
+    V(ts(B("Sh"), R128, B("p1"), B("nl15"), A.is_equal, A.mult), al("row", "p1", "nl15"), al("Sh"), 128)
+    V(tt(B("ShI"), B("Sh"), B("Ih"), A.subtract), al("Sh", "Ih"), al("ShI"), 128, 2)
+    V(lambda g, T: g.vector.memset(T.zz[:], 0.0), [], al("zz"), I)
+    V(lambda g, T: g.vector.memset(T.cq[:], -0.5), [], al("cq"), I)
+    V(lambda g, T: g.vector.memset(T.c75[:], -7.5), [], al("c75"), 16)
+
+    V(tc(B("PU"), B("PI")), al("PI"), al("PU"), 12)
+    V(tc(B("SU"), B("SI")), al("SI"), al("SU"), I)
+    V(ts(B("E16"), lambda T: T.PLT[:, :].indirect(T.PU[:, 0:12]), -CEN, None, A.add), al("PLT", "PU"), al("E16"), I, 1.6)
+    V(ts(B("EU"), B("E16"), CEN, None, A.add), al("E16"), al("EU"), I)
+    V(ts(B("b5", 0, I), B("SI"), -CEN, None, A.add), al("SI"), [("b5", 0, I)], I)
+    V(tc(B("PF"), B("PI")), al("PI"), al("PF"), 12)
+    V(tc(B("BND"), B("THI")), al("THI"), al("BND"), I)
+
+    def gathers():
+        cs = CSPL
+        V(lambda g, T: g.vector.tensor_copy(T.XS[:, 0:16 * cs], T.X[:, :].indirect(T.SU[:, 0:cs])), al("X", "SU"), [("XS", 0, 16 * cs)], 16 * cs, 1.5)
+        if cs < I:
+            S(lambda g, T: g.scalar.activation(T.XS[:, 16 * cs:W], T.X[:, :].indirect(T.SU[:, cs:I]), F.Copy), al("X", "SU"), [("XS", 16 * cs, W)], 16 * (I - cs), 1.5)
+        for c in range(XC):
+            a, b = I // XC * c, I // XC * (c + 1)
+            S(lambda g, T, a=a, b=b: g.scalar.activation(T.XE[:, 16 * a:16 * b], T.X[:, :].indirect(T.EU[:, a:b]), F.Copy), al("X", "EU"), [("XE", 16 * a, 16 * b)], 16 * (b - a), 1.5)
+
+    gathers()
+
+    def mixed(n):
+        fast, slow = list(range(NC - n)), list(range(NC - n, NC))
+        res = []
+        while fast or slow:
+            if slow and (not fast or len(slow) * (NC - n) >= len(fast) * n):
+                res.append(slow.pop(0))
+            else:
+                res.append(fast.pop(0))
+        return res
+
+    turn_bank = [0]
+
+    def bank():
+        turn_bank[0] += 1
+        return "b4" if turn_bank[0] % 2 else "b6"
+
+    for t in range(TURNS):
+        L, Y = "L%d" % t, "Y%d" % t
+        f0, f1 = ("FA", "FB") if t % 2 == 0 else ("FB", "FA")
+        s0, s1 = (0, I) if t % 2 == 0 else (I, 0)
+        if t == 0:
+            for c in range(16):
+                S(act(B("IC", 128 * c, 128 * c + 128), B("Ib"), F.Copy, scale=float(c + 1)), al("Ib"), [("IC", 128 * c, 128 * c + 128)], 128)
+        MM(B("b3", 0, I), B("Ib"), B("zz"), True, False, al("Ib", "zz"), [("b3", 0, I)], I)
+        for c in range(XC):
+            p, q = I // XC * c, I // XC * (c + 1)
+            for k in [k for k in range(16) if k % NC < NC - NQ]:
+                MM(B("b3", p, q), slide("Wm", k), B("XE", 16 * p + k, 16 * q, 16), False, False, al("Wm") + [("XE", 16 * p, 16 * q)], [("b3", p, q)], q - p)
+        for m in range(NK):
+            MM(B("b0", m, CW, NK), B("Ib"), B(L), True, True, al("Ib", L), [("b0", 0, CW)], I)
+        MM(B("b3", 0, I), B("OBm"), B(L), False, False, al("OBm", L), [("b3", 0, I)], I)
+        for r in range(16):
+            MM(B("b7", 0, 12), slide("Wu", r), B(L, r, I, 16), r == 0, r == 15, al("Wu", L), [("b7", 0, 12)], 12)
+        MM(B("b7", 256, 256 + I), B("Ihf"), B(L), True, False, al("Ihf", L), [("b7", 256, 256 + I)], I)
+        MM(B("b7", 256, 256 + I), B("Ihf"), B(f0), False, False, al("Ihf", f0), [("b7", 256, 256 + I)], I)
+        MM(B("b7", 256, 256 + I), B("Ihf"), B("cq"), False, True, al("Ihf", "cq"), [("b7", 256, 256 + I)], I)
+        V(ts(B(f1), B("b7", 256, 256 + I), MAGIC, MAGIC, A.add, A.subtract), [("b7", 256, 256 + I)], al(f1), I)
+        V(tc(B("H1"), B("b7", 0, 12)), [("b7", 0, 12)], al("H1"), 12)
+        V(ts(B("H2"), B("H1"), 4095, None, A.bitwise_and), al("H1"), al("H2"), 12)
+        V(ts(B("H3"), B("H2"), 1184.0, None, A.add), al("H2"), al("H3"), 12)
+        V(tt(B("H4"), B("H2"), B("H3"), A.mult), al("H2", "H3"), al("H4"), 12)
+        V(ts(B("H7"), B("H4"), 5, PLN - 1, A.arith_shift_right, A.bitwise_and), al("H4"), al("H7"), 12)
+        V(tc(B("PU"), B("H7")), al("H7"), al("PU"), 12)
+        V(ts(B("CAND"), lambda T: T.PLT[:, :].indirect(T.PU[:, 0:12]), -CEN, None, A.add), al("PLT", "PU"), al("CAND"), I, 1.6)
+        V(tt(B("DES"), B("E16"), B("b5", s0, s0 + I), A.subtract), al("E16") + [("b5", s0, s0 + I)], al("DES"), I)
+        def tensor_diff(X, q, bk):
+            for m in range(NK):
+                k = q + NC * m
+                MM(B(bk, I * m, I * m + I), B("Ib"), lambda T, k=k: T[X][:, k:W:16], True, False, al("Ib", X), [(bk, I * m, I * m + I)], I)
+                MM(B(bk, I * m, I * m + I), B("Im"), B(L), False, True, al("Im", L), [(bk, I * m, I * m + I)], I)
+
+        VQ = NC - NS
+        for q in range(VQ):
+            V(tt(B("D", CW * q, CW * q + CW), lambda T, q=q: T.XS[:, q:W:NC], B("b0", 0, CW), A.subtract),
+              al("XS") + [("b0", 0, CW)], [("D", CW * q, CW * q + CW)], CW)
+        chunks = [(c, min(VQ, c + 2)) for c in range(0, VQ, 2)]
+        for c, e in chunks:
+            a, b = CW * c, CW * e
+            S(act(B("AB", a, b), B("D", a, b), F.Abs), [("D", a, b)], [("AB", a, b)], b - a)
+        for q in range(VQ, NC):
+            bk = bank()
+            tensor_diff("XS", q, bk)
+            S(act(B("AB", CW * q, CW * q + CW), B(bk, 0, CW), F.Abs), [(bk, 0, CW)], [("AB", CW * q, CW * q + CW)], CW)
+            S(act(B("SG", CW * q, CW * q + CW), B(bk, 0, CW), F.Sign, bias=-0.5), [(bk, 0, CW)], [("SG", CW * q, CW * q + CW)], CW)
+        for c, e in chunks:
+            a, b = CW * c, CW * e
+            if c < 2 * NF:
+                V(ts(B("SG", a, b), B("D", a, b), 0.0, -0.5, A.is_gt, A.add), [("D", a, b)], [("SG", a, b)], b - a, 0.5)
+            else:
+                S(act(B("SG", a, b), B("D", a, b), F.Sign, bias=-0.5), [("D", a, b)], [("SG", a, b)], b - a)
+
+        def piece(buf, q, m, direct):
+            return B(buf, CW * q + I * m, CW * q + I * m + I) if direct else B(buf, CW * q + m, CW * q + CW, NK)
+
+        sq = [(q, m) for q in mixed(NS) for m in range(NK)]
+        for (q, m) in sq:
+            MM(B("b1", 0, I), slide("W1", q + NC * m), piece("AB", q, m, q >= VQ), (q, m) == sq[0], (q, m) == sq[-1], al("W1") + [("AB", CW * q, CW * q + CW)], [("b1", 0, I)], I)
+        gq = sq if NS == 0 else [x for x in sq if x[0] >= VQ] + [x for x in sq if x[0] < VQ]
+        for (q, m) in gq:
+            w = "W2" if q < min(VQ, 2 * NF) else "W1"
+            MM(B("b2", 0, I), slide(w, q + NC * m), piece("SG", q, m, q >= VQ), (q, m) == gq[0], (q, m) == gq[-1], al(w) + [("SG", CW * q, CW * q + CW)], [("b2", 0, I)], I)
+        for q in range(NC - NQ, NC):
+            bk = bank()
+            tensor_diff("XE", q, bk)
+            S(act(B("MX", CW * q, CW * q + CW), B(bk, 0, CW), F.Abs), [(bk, 0, CW)], [("MX", CW * q, CW * q + CW)], CW)
+        for q in range(NC - NQ):
+            V(tt(B("MX", CW * q, CW * q + CW), lambda T, q=q: T.XE[:, q:W:NC], B("b0", 0, CW), A.max),
+              al("XE") + [("b0", 0, CW)], [("MX", CW * q, CW * q + CW)], CW)
+        pq = [(q, m) for q in mixed(NQ) for m in range(NK)]
+        for (q, m) in pq:
+            k = q + NC * m
+            if q < NC - NQ:
+                MM(B("b3", 0, I), slide("W2", k), B("MX", CW * q + m, CW * q + CW, NK), False, (q, m) == pq[-1], al("W2") + [("MX", CW * q, CW * q + CW)], [("b3", 0, I)], I)
+            else:
+                MM(B("b3", 0, I), slide("W1", k), B("MX", CW * q + I * m, CW * q + I * m + I), False, (q, m) == pq[-1], al("W1") + [("MX", CW * q, CW * q + CW)], [("b3", 0, I)], I)
+        V(tt(B("RS"), B("b1", 0, I), B("BND"), A.is_lt), [("b1", 0, I)] + al("BND"), al("RS"), I)
+        MM(B("b1", I, 2 * I), B("Ls"), B("RS"), True, True, al("Ls", "RS"), [("b1", I, 2 * I)], I)
+        V(tt(B("FI"), B("RS"), B("b1", I, 2 * I), A.is_gt), al("RS") + [("b1", I, 2 * I)], al("FI"), I)
+        V(tt(B("FF"), B("FI"), B("b5", s0, s0 + I), A.mult), al("FI") + [("b5", s0, s0 + I)], al("FF"), I)
+        MM(B("b4", I, 2 * I), B("Li"), B("RS"), True, True, al("Li", "RS"), [("b4", I, 2 * I)], I)
+        S(act(B("b1", 0, I), B("b4", I, 2 * I), F.Relu, scale=-1.0, bias=1.0), [("b4", I, 2 * I)], [("b1", 0, I)], I)
+        S(act(B("KK"), B("b2", 0, I), F.Relu, scale=16.0, bias=128.0), [("b2", 0, I)], al("KK"), I)
+        MM(B("b2", I, 2 * I), B("OB"), B("RS"), True, False, al("OB", "RS"), [("b2", I, 2 * I)], I)
+        MM(B("b2", I, 2 * I), B("I100"), B("FI"), False, True, al("I100", "FI"), [("b2", I, 2 * I)], I)
+        V(tt(B("b2", 0, I), B("b2", I, 2 * I), B("KK"), A.is_gt), [("b2", I, 2 * I)] + al("KK"), [("b2", 0, I)], I)
+        V(tt(B("WD"), B("DES"), B("b2", 0, I), A.mult), al("DES") + [("b2", 0, I)], al("WD"), I)
+        V(tt(B("RR"), B("WD"), B("b5", s0, s0 + I), A.add), al("WD") + [("b5", s0, s0 + I)], al("RR"), I)
+        V(tt(B("QQ"), B("RR"), B("b1", 0, I), A.mult), al("RR") + [("b1", 0, I)], al("QQ"), I)
+        V(tt(B("RP"), B("b3", 0, I), B("BND"), A.is_lt), [("b3", 0, I)] + al("BND"), al("RP"), I)
+        MM(B("b3", I, 2 * I), B("OB"), B("RS"), True, False, al("OB", "RS"), [("b3", I, 2 * I)], I)
+        MM(B("b3", I, 2 * I), B("Ls"), B("RP"), False, True, al("Ls", "RP"), [("b3", I, 2 * I)], I)
+        MM(B("b4", 0, I), B("OB"), B("RS"), True, False, al("OB", "RS"), [("b4", 0, I)], I)
+        MM(B("b4", 0, I), B("OB"), B("RP"), False, True, al("OB", "RP"), [("b4", 0, I)], I)
+        V(tt(B("b6", I, 2 * I), B("RP"), B("b3", I, 2 * I), A.is_gt), al("RP") + [("b3", I, 2 * I)], [("b6", I, 2 * I)], I)
+        S(act(B("b4", I, 2 * I), B("b4", 0, I), F.Relu, scale=B("nl0"), bias=B("l0")), [("b4", 0, I)] + al("nl0", "l0"), [("b4", I, 2 * I)], I)
+        V(tt(B("b6", 0, I), B("E16"), B("b6", I, 2 * I), A.mult), al("E16") + [("b6", I, 2 * I)], [("b6", 0, I)], I)
+        V(tt(B("HH"), B("CAND"), B("b4", I, 2 * I), A.mult), al("CAND") + [("b4", I, 2 * I)], al("HH"), I)
+        V(tt(B("GG"), B("HH"), B("b6", 0, I), A.add), al("HH") + [("b6", 0, I)], al("GG"), I)
+        for src in ("FF", "GG"):
+            for r in range(16):
+                MM(B("b7", 16, 28), slide("Wh", r), B(src, r, I, 16), (src, r) == ("FF", 0), (src, r) == ("GG", 15), al("Wh", src), [("b7", 16, 28)], 12)
+        V(ts(B("TU"), B("b7", 16, 28), CEN, None, A.add), [("b7", 16, 28)], al("TU"), 12)
+        V(lambda g, T, f1=f1: g.vector.tensor_tensor(T.YD[:], T.X[:, :].indirect(T.TU[:, 0:12]), T[f1][:], A.subtract), al("X", "TU", f1), al("YD"), I, 1.6)
+        S(act(B(Y), B("YD"), F.Abs), al("YD"), al(Y), I)
+        if t < TURNS - 1:
+            add("G", ("send", t), al(Y), [], 1.2, send=t)
+            Ln = "L%d" % (t + 1)
+            bl = (-t) % N
+            a, b = BLK * bl, BLK * bl + BLK
+            S(act(B(Ln, a, b), B(Y, a, b), F.Copy), al(Y), [(Ln, a, b)], BLK)
+            wr = [(Ln, c, d) for c, d in ((0, a), (b, I)) if d > c]
+            add("R", None, [], wr, 3.8, arr=t)
+        MM(B("b7", 32, 44), B("Ib"), B("c75", 0, 12), True, False, al("Ib", "c75"), [("b7", 32, 44)], 12)
+        for r in range(16):
+            MM(B("b7", 32, 44), slide("W1", r), B(Y, r, I, 16), False, r == 15, al("W1", Y), [("b7", 32, 44)], 12)
+        MM(B("b0", 0, I), B("Ihf"), B(L), True, False, al("Ihf", L), [("b0", 0, I)], I)
+        MM(B("b0", 0, I), B("Ihf"), B("cq"), False, False, al("Ihf", "cq"), [("b0", 0, I)], I)
+        MM(B("b0", 0, I), B("Ihf"), B(Y), False, True, al("Ihf", Y), [("b0", 0, I)], I)
+        V(ts(B("QF"), B("b7", 32, 44), MAGIC16, MAGIC16, A.add, A.subtract), [("b7", 32, 44)], al("QF"), 12)
+        V(tt(B("RF"), B("base"), B("b7", 32, 44), A.add), al("base") + [("b7", 32, 44)], al("RF"), 12)
+        V(tt(B("MF"), B("RF"), B("QF"), A.subtract), al("RF", "QF"), al("MF"), 12)
+        V(tc(B("MU"), B("MF")), al("MF"), al("MU"), 12)
+        V(ts(B("WR"), B("b0", 0, I), MAGIC, MAGIC, A.add, A.subtract), [("b0", 0, I)], al("WR"), I)
+        V(lambda g, T: g.vector.tensor_copy(T.X[:, :].indirect(T.MU[:, 0:12]), T.WR[:]), al("WR", "MU", "X"), al("X"), I, 3.5)
+        o = (B("b5", s1, s1 + I), [("b5", s1, s1 + I)])
+        MM(o[0], B("Ih"), B("RR"), True, False, al("Ih", "RR"), o[1], I)
+        MM(o[0], B("ShI"), B("QQ"), False, False, al("ShI", "QQ"), o[1], I)
+        MM(o[0], B("TpI"), B("FF"), False, False, al("TpI", "FF"), o[1], I)
+        MM(o[0], B("Tp"), B("GG"), False, True, al("Tp", "GG"), o[1], I)
+        last = t == TURNS - 1
+        if last:
+            V(ts(B("OS"), o[0], CEN, None, A.add), o[1], al("OS"), I)
+        else:
+            V(ts(B("SU"), o[0], CEN, None, A.add), o[1], al("SU"), I)
+        S(act(B("CR"), B("b4", 0, I), F.Relu, scale=B("nl0"), bias=B("l0")), [("b4", 0, I)] + al("nl0", "l0"), al("CR"), I)
+        S(act(B("C64"), B("b4", 0, I), F.Relu, scale=-64.0, bias=64.0), [("b4", 0, I)], al("C64"), I)
+        if not last:
+            S(act(B("b3", 0, I), B("b4", 0, I), F.Relu, scale=-1.0, bias=1.0), [("b4", 0, I)], [("b3", 0, I)], I)
+            S(act(B("b3", I, 2 * I), B("b4", 0, I), F.Sign), [("b4", 0, I)], [("b3", I, 2 * I)], I)
+            V(tt(B("b6", 0, I), B("E16"), B("b3", I, 2 * I), A.mult), al("E16") + [("b3", I, 2 * I)], [("b6", 0, I)], I)
+            V(tt(B("HF"), B("CAND"), B("b3", 0, I), A.mult), al("CAND") + [("b3", 0, I)], al("HF"), I)
+            V(tt(B("E16"), B("HF"), B("b6", 0, I), A.add), al("HF") + [("b6", 0, I)], al("E16"), I)
+            V(ts(B("EU"), B("E16"), CEN, None, A.add), al("E16"), al("EU"), I, 0.5)
+        V(tt(B("BND"), B("BND"), B("C64"), A.add), al("BND", "C64"), al("BND"), I, 2)
+        if not last:
+            gathers()
+        for r in range(16):
+            MM(B("b2", 384, 396), slide("W1", r), B("CR", r, I, 16), r == 0, r == 15, al("W1", "CR"), [("b2", 384, 396)], 12)
+        V(tt(B("DP"), B("H7"), B("PF"), A.subtract), al("H7", "PF"), al("DP"), 12)
+        V(tt(B("DQ"), B("DP"), B("b2", 384, 396), A.mult), al("DP") + [("b2", 384, 396)], al("DQ"), 12)
+        V(tt(B("PF"), B("PF"), B("DQ"), A.add), al("PF", "DQ"), al("PF"), 12)
+        if last:
+            V(tt(B("CR"), B("BND"), B("THI"), A.subtract), al("BND", "THI"), al("CR"), I, 2)
+            for r in range(16):
+                MM(B("b2", 384, 396), slide("W1", r), B("CR", r, I, 16), r == 0, r == 15, al("W1", "CR"), [("b2", 384, 396)], 12)
+            def store(dst, src):
+                k = nd[0]
+                nd[0] += 1
+                add("Y", lambda g, T: g.sync.dma_start(T[dst][:], T[src][:]), al(src), [], 2.5, dma=k)
+            store("yf", f1)
+            store("ys", "OS")
+            V(ts(B("MF"), B("b2", 384, 396), PLN / 1024.0, None, A.mult), [("b2", 384, 396)], al("MF"), 12)
+            V(tt(B("YPF"), B("MF"), B("PF"), A.add), al("MF", "PF"), al("YPF"), 12)
+            store("yp", "YPF")
+            for c in range(16):
+                MM(B("b0", 0, I), B("IC", 128 * c, 128 * c + 128), B("X", c, W, 16), c == 0, c == 15, [("IC", 128 * c, 128 * c + 128), ("X",)], [("b0", 0, I)], I)
+            S(act(B("OX"), B("b0", 0, I), F.Copy), [("b0", 0, I)], al("OX"), I)
+            store("yx", "OX")
+    return ops
+
+
+def _deps(ops):
+    data, order = [], []
+    acc = {}
+    banks = {}
+    sends = {}
+    for i, (q, fn, rd, wr, cost, kw) in enumerate(ops):
+        dd, oo = set(), set()
+        seen = {}
+        for lst, w in ((rd, False), (wr, True)):
+            for (n, a, b) in lst:
+                if n[0] == "b" and n[1:].isdigit():
+                    e = seen.get(n)
+                    if e is None:
+                        e = banks.setdefault(n, {"q": q, "cur": [], "prev": []})
+                        if e["q"] != q:
+                            e["prev"], e["cur"], e["q"] = [x[0] for x in e["cur"]], [], q
+                        seen[n] = e
+                        dd.update(e["prev"])
+                    if q == "T":
+                        if e["cur"] and e["cur"][-1][0] != i:
+                            oo.add(e["cur"][-1][0])
+                    else:
+                        for (j, c, d, w2) in e["cur"]:
+                            if j != i and (w or w2) and c < b and a < d:
+                                dd.add(j)
+                    e["cur"].append((i, a, b, w))
+                else:
+                    l = acc.setdefault(n, [])
+                    for (j, c, d, w2) in l:
+                        if j != i and (w or w2) and c < b and a < d:
+                            dd.add(j)
+        for lst, w in ((rd, False), (wr, True)):
+            for (n, a, b) in lst:
+                if n[0] == "b" and n[1:].isdigit():
+                    continue
+                l = acc[n]
+                if w:
+                    l[:] = [x for x in l if not (a <= x[1] and x[2] <= b and x[0] != i)]
+                l.append((i, a, b, w))
+        if "send" in kw:
+            sends[kw["send"]] = i
+        if "arr" in kw:
+            oo.add(sends[kw["arr"]])
+        dd.discard(i)
+        oo -= dd
+        data.append(sorted(dd))
+        order.append(sorted(oo))
+    return data, order
+
+
+def _schedule(ops, data, order):
+    n = len(ops)
+    succ = [[] for _ in range(n)]
+    for i in range(n):
+        for j in data[i] + order[i]:
+            succ[j].append(i)
+    prio = [0.0] * n
+    for i in range(n - 1, -1, -1):
+        prio[i] = ops[i][4] + max([prio[k] + LAT for k in succ[i]], default=0.0)
+    base = list(prio)
+    for i in range(n):
+        if ops[i][3]:
+            w = ops[i][3][0]
+            prio[i] = base[i] + BONUS.get("%s:%s:%d" % (ops[i][0], w[0], w[1]), 0.0)
+    left = [len(data[i]) + len(order[i]) for i in range(n)]
+    ready = [0.0] * n
+    pool = {}
+    free = {}
+    for i in range(n):
+        if left[i] == 0:
+            pool.setdefault(ops[i][0], []).append(i)
+    out = []
+    while True:
+        best = None
+        for q, l in pool.items():
+            if not l:
+                continue
+            st = max(free.get(q, 0.0), min(ready[i] for i in l))
+            if best is None or st < best[0]:
+                best = (st, q)
+        if best is None:
+            break
+        st, q = best
+        i = max((i for i in pool[q] if ready[i] <= st + 1e-9), key=lambda i: (prio[i], -i))
+        if ops[i][4] > 0.3:
+            i = max((k for k in pool[q] if ready[k] <= st + HOLD), key=lambda i: (prio[i], -i))
+            st = max(st, ready[i])
+        pool[q].remove(i)
+        dma = "dma" in ops[i][5] or q == "R"
+        fin = st + ops[i][4]
+        free[q] = st + (0.1 if dma else ops[i][4])
+        out.append((i, st, fin))
+        for k in succ[i]:
+            same = ops[k][0] == q and i in order[k]
+            ready[k] = max(ready[k], fin if same else fin + LAT)
+            left[k] -= 1
+            if left[k] == 0:
+                pool.setdefault(ops[k][0], []).append(k)
+    return out
+
+
+_PLAN = {}
+
+
+def _plan():
+    if not _PLAN:
+        ops = _build()
+        data, order = _deps(ops)
+        _PLAN["ops"], _PLAN["data"], _PLAN["sched"] = ops, data, _schedule(ops, data, order)
+    return _PLAN["ops"], _PLAN["data"], _PLAN["sched"]
+
+
+def rank_program(g, core, T, topo):
+    rank = T.rank_of(core)
+    if rank is None:
+        return
+    ops, data, sched = _plan()
+    eng = {"V": g.vector, "S": g.scalar, "T": g.tensor, "G": g, "Y": g.sync}
+    seq, cnt, clock = {}, {}, {}
+    know = {q: {} for q in eng}
+
+    def send(t):
+        tr = []
+        used = 0
+        for b in range(N):
+            to = (rank + b + t) % N
+            if to == rank:
+                continue
+            dst = T.cores[to]
+            rid, pnc = topo.addr(dst)[:2]
+            e = topo.engines(core, dst)
+            tr.append(RemoteDMATransfer(dst_ids=[DstId(rid=rid, pnc=pnc)], dma_engine_mask=1 << e[used % len(e)], remote_sem=T.sem["arr%d" % t],
+                                        src=T["Y%d" % t][:, BLK * b:BLK * b + BLK], dst=T["L%d" % (t + 1)][:, BLK * b:BLK * b + BLK]))
+            used += 1
+        g.remote_dma_fused(tr, local_sem=T.sem.sent)
+        return used
+
+    sent = 0
+    dmas = []
+    for (i, st, fin) in sched:
+        q, fn, rd, wr, cost, kw = ops[i]
+        if q == "R":
+            seq[i] = ("arr%d" % kw["arr"], N - 1)
+            clock[i] = {}
+            continue
+        kn = know[q]
+        need = {}
+        before = [j for j in data[i] if "send" not in ops[j][5]]
+        for j in before:
+            s, v = seq[j]
+            if kn.get(s, 0) < v:
+                need[s] = max(need.get(s, 0), v)
+        for j in sorted(before, key=lambda j: -j):
+            s, v = seq[j]
+            if s in need and need[s] == v:
+                for s2, v2 in clock[j].items():
+                    if s2 in need and s2 != s and need[s2] <= v2:
+                        del need[s2]
+        for j in before:
+            s, v = seq[j]
+            for s2, v2 in list(clock[j].items()) + [(s, v)]:
+                if kn.get(s2, 0) < v2:
+                    kn[s2] = v2
+        for s, v in need.items():
+            eng[q].wait_ge(T.sem[s], v)
+        if "send" in kw:
+            sent += send(kw["send"])
+            continue
+        ins = fn(g, T)
+        if "dma" in kw:
+            s = "dm%d" % kw["dma"]
+            ins.then_inc(T.sem[s], 16)
+            seq[i] = (s, 16)
+            dmas.append(s)
+            clock[i] = dict(kn)
+        else:
+            s = "q" + q
+            cnt[s] = cnt.get(s, 0) + 1
+            ins.then_inc(T.sem[s], 1)
+            seq[i] = (s, cnt[s])
+            clock[i] = dict(kn)
+    g.wait_ge(T.sem.sent, sent)
+    for s, v in cnt.items():
+        g.wait_ge(T.sem[s], v)
+    for s in dmas:
+        g.wait_ge(T.sem[s], 16)

@@ -5,393 +5,462 @@ from concourse.mybir import dt, AluOpType, AxisListType, ActivationFunctionType
 A = AluOpType
 F = ActivationFunctionType
 I, W, PLN, TURNS, BLK, N = 192, 3072, 2048, 8, 24, 8
-NK = 2
-NQ = 0
-NF = 0
-NS = 2
-CSPL = 152
-XC = 3
-TR = 0.5
-NC = 16 // NK
-CW = NK * I
+NC = 8
+CW = 2 * I
+PA = 64
+PARTS = (0, 1, 2)
+WAYS = "ttbbbm"
+VCUT = (64, 128)
+VCUT0 = (96,)
+HELP, EN = True, 4
+CNT, ATS = True, True
+RPS, FS, WS = True, True, True
+TR = 0.62
 CEN = 1536.0
+BIG = 8192.0
 MAGIC = 12582912.0
 MAGIC16 = 201326592.0
+BF, HF, FL, I32, U16 = "bfloat16", "float16", "float32", "int32", "uint16"
+ORDER = ("yx dx1 xs zp rp xe0 dx3 wr new dx2 hash f2 sp3 sz xe2 sp0 pp0 a dx4 mn pp3 own pp5 dz0 sp5 pp4 u m sx pp1 pp2 f cand rs dz1 dx5 zq sp2 wd dx0 "
+         "sp1 sp4 pre sv wp an yp e sw xe1 set").split()
+HOLDS = "rp an dz1 wr sp1 pre sp4 e new set cand sp3 u m dz0 dx5 pp3 rs own xe0 sp0".split()
+D = {_n: float(_k) for _k, _n in enumerate(ORDER)}
 
-SCRATCH = {
-    "X": ("sbuf", [128, W], "bfloat16"),
-    "XS": ("sbuf", [128, W], "bfloat16"), "XE": ("sbuf", [128, W], "bfloat16"),
-    "D": ("sbuf", [128, W], "bfloat16"), "AB": ("sbuf", [128, W], "bfloat16"),
-    "SG": ("sbuf", [128, W], "bfloat16"), "MX": ("sbuf", [128, W], "bfloat16"),
-    "PLT": ("sbuf", [128, PLN], "int32"), "SI": ("sbuf", [128, I], "int32"), "THI": ("sbuf", [128, I], "int32"),
-    "PI": ("sbuf", [128, 12], "int32"), "PF": ("sbuf", [128, 12], "float32"),
-    "BND": ("sbuf", [128, I], "float32"), "C64": ("sbuf", [128, I], "float32"), "KK": ("sbuf", [128, I], "float32"),
-    "RS": ("sbuf", [128, I], "bfloat16"), "RP": ("sbuf", [128, I], "bfloat16"), "FI": ("sbuf", [128, I], "bfloat16"),
-    "CR": ("sbuf", [128, I], "bfloat16"), "DES": ("sbuf", [128, I], "float32"), "WD": ("sbuf", [128, I], "float32"),
-    "RR": ("sbuf", [128, I], "float16"), "QQ": ("sbuf", [128, I], "float16"), "FF": ("sbuf", [128, I], "float16"),
-    "GG": ("sbuf", [128, I], "float16"), "HH": ("sbuf", [128, I], "float16"), "HF": ("sbuf", [128, I], "float16"),
-    "E16": ("sbuf", [128, I], "float16"), "CAND": ("sbuf", [128, I], "float16"),
-    "SU": ("sbuf", [128, I], "uint16"), "EU": ("sbuf", [128, I], "uint16"),
-    "TU": ("sbuf", [128, 12], "uint16"), "PU": ("sbuf", [128, 12], "uint16"), "MU": ("sbuf", [128, 12], "uint16"),
-    "FA": ("sbuf", [128, I], "bfloat16"), "FB": ("sbuf", [128, I], "bfloat16"),
-    "YD": ("sbuf", [128, I], "bfloat16"), "WR": ("sbuf", [128, I], "bfloat16"),
-    "H1": ("sbuf", [128, 12], "int32"), "H2": ("sbuf", [128, 12], "int32"), "H3": ("sbuf", [128, 12], "int32"),
-    "H4": ("sbuf", [128, 12], "int32"),
-    "H7": ("sbuf", [128, 12], "int32"), "DP": ("sbuf", [128, 12], "float32"), "DQ": ("sbuf", [128, 12], "float32"),
-    "QF": ("sbuf", [128, 12], "float32"), "RF": ("sbuf", [128, 12], "float32"), "MF": ("sbuf", [128, 12], "float32"),
-    "YPF": ("sbuf", [128, 12], "float32"),
-    "ip": ("sbuf", [128, 1], "int32"), "ig": ("sbuf", [128, 1], "int32"), "irow": ("sbuf", [128, 144], "int32"),
-    "igrow": ("sbuf", [128, 128], "int32"), "ibase": ("sbuf", [128, 12], "int32"),
-    "pf": ("sbuf", [128, 1], "float32"), "p1": ("sbuf", [128, 1], "float32"), "gf": ("sbuf", [128, 1], "float32"),
-    "g16": ("sbuf", [128, 1], "float32"), "g15": ("sbuf", [128, 1], "float32"), "lf": ("sbuf", [128, 1], "float32"),
-    "l21": ("sbuf", [128, 1], "float32"), "l0": ("sbuf", [128, 1], "float32"), "nl0": ("sbuf", [128, 1], "float32"),
-    "nl15": ("sbuf", [128, 1], "float32"), "r16": ("sbuf", [128, 1], "float32"),
-    "row": ("sbuf", [128, 144], "float32"), "grow": ("sbuf", [128, 128], "float32"), "base": ("sbuf", [128, 12], "float32"),
-    "W1": ("sbuf", [128, 144], "bfloat16"), "W2": ("sbuf", [128, 144], "bfloat16"), "Wm": ("sbuf", [128, 144], "bfloat16"),
-    "Wu": ("sbuf", [128, 144], "bfloat16"), "Wh": ("sbuf", [128, 144], "float16"),
-    "OB": ("sbuf", [128, 128], "bfloat16"), "OBm": ("sbuf", [128, 128], "bfloat16"), "Ib": ("sbuf", [128, 128], "bfloat16"),
-    "Im": ("sbuf", [128, 128], "bfloat16"), "im8": ("sbuf", [128, 128], "int32"), "mk": ("sbuf", [128, 128], "float32"),
-    "Ihf": ("sbuf", [128, 128], "bfloat16"), "I100": ("sbuf", [128, 128], "bfloat16"), "GT": ("sbuf", [128, 128], "bfloat16"),
-    "Ls": ("sbuf", [128, 128], "bfloat16"), "Li": ("sbuf", [128, 128], "bfloat16"),
-    "Ih": ("sbuf", [128, 128], "float16"), "Sh": ("sbuf", [128, 128], "float16"),
-    "ShI": ("sbuf", [128, 128], "float16"), "Tp": ("sbuf", [128, 128], "float16"), "TpI": ("sbuf", [128, 128], "float16"),
-    "cq": ("sbuf", [128, I], "bfloat16"), "zz": ("sbuf", [128, I], "bfloat16"), "c75": ("sbuf", [128, 16], "bfloat16"),
-    "IC": ("sbuf", [128, 16 * 128], "bfloat16"),
-    "OS": ("sbuf", [128, I], "float32"), "OX": ("sbuf", [128, I], "float32"),
-}
+SCRATCH = {}
+for _n, _w, _d in [
+        ("X", W, BF), ("XS", W, BF), ("XE", W, BF), ("MN", W, HF), ("MX", W, BF),
+        ("PLT", PLN, I32), ("SI", I, I32), ("THI", I, I32), ("PI", 12, I32),
+        ("S16", I, HF), ("E16", I, HF), ("CAND", I, HF), ("TH16", I, HF), ("BND", I, HF), ("AT", I, BF), ("SWH", TURNS * I, BF),
+        ("SU", I, U16), ("EU", I, U16), ("TU", 12, U16), ("PU", 12, U16), ("MU", 12, U16),
+        ("R2", I, I32), ("RS", I, BF), ("RP", I, BF), ("AN", 2 * I, BF), ("SET", I, BF), ("WD", I, FL), ("QQ", I, FL),
+        ("TS", I, HF), ("TP", I, HF), ("TC", I, HF),
+        ("FA", I, BF), ("FB", I, BF), ("YD", I, BF), ("WR", I, BF), ("QF", 12, FL), ("QB", 12, HF),
+        ("HH", 48, I32), ("PH", 12 * TURNS, I32),
+        ("KT", 12 * TURNS, FL), ("PK", 12 * TURNS, FL), ("KK", 180, FL),
+        ("K0", 12, I32), ("PE", 12, I32), ("YPF", 12, FL), ("OS", I, FL), ("OX", I, FL),
+        ("ip", 1, I32), ("ig", 1, I32), ("r4", 128, BF), ("ibase", 12, I32),
+        ("pf", 1, FL), ("gf", 1, FL), ("g16", 1, FL), ("g15", 1, FL), ("lf", 1, FL), ("l21", 1, FL), ("l0", 1, FL),
+        ("r16", 1, FL), ("nB", 5, FL), ("row", 144, FL), ("grow", 128, FL), ("base", 12, FL),
+        ("cv", I, BF), ("FM", I, FL), ("WM", I, FL),
+        ("W1", 144, BF), ("W2", 144, BF), ("Wm", 144, BF), ("Wmh", 144, BF), ("Wu", 144, BF), ("W0", 144, BF),
+        ("Ib", 128, BF), ("Im", 128, BF), ("Ihf", 128, BF), ("I32", 128, BF), ("I64m", 128, BF),
+        ("OB", 128, BF), ("OBh", 128, BF), ("OBB", 128, BF), ("OBm", 128, BF), ("DE", 2048, BF),
+        ("Ls", 128, BF), ("BIL", 128, BF), ("Sh", 128, BF), ("Ihm", 128, BF),
+        ("ShI", 128, BF), ("Ihq", 128, HF), ("R16", I, HF), ("Tp", 128, BF), ("Tp0", 128, BF),
+        ("cq", CW, BF), ("cz", CW, HF), ("ct", I, BF), ("cb", CW, BF), ("IC0", 512, BF), ("IC", 16 * 128, BF)]:
+    SCRATCH[_n] = ("sbuf", [128, _w], _d)
 for _t in range(8):
-    SCRATCH["L%d" % _t] = ("sbuf", [128, I], "bfloat16")
-    SCRATCH["Y%d" % _t] = ("sbuf", [128, I], "bfloat16")
+    SCRATCH["L%d" % _t] = ("sbuf", [128, I], BF)
+    SCRATCH["Y%d" % _t] = ("sbuf", [128, I], BF)
 for _t in range(8):
-    SCRATCH["b%d" % _t] = ("psum", [128, 512], "float32")
+    SCRATCH["b%d" % _t] = ("psum", [128, 512], FL)
 NDMA = 12
 SEMAPHORES = ["qV", "qS", "qT", "qG", "sent"] + ["arr%d" % t for t in range(8)] + ["dm%d" % k for k in range(NDMA)]
 
-LAT = 0.08
-HOLD = 0.15
-BONUS = {}
+LAT, HOLD, FLY = 0.11, 0.15, 3.5
+TO, VS = 0.0, 1.0
+GA = 1.5
 
 
 def _build():
     ops = []
+    CY = 0.00083
+    now = [0.0, ""]
 
     def add(q, fn, rd, wr, cost, **kw):
-        ops.append([q, fn, [(r if len(r) == 3 else (r[0], 0, 1 << 20)) for r in rd], [(r if len(r) == 3 else (r[0], 0, 1 << 20)) for r in wr], cost, kw])
+        ops.append([q, fn, [r for r in rd if r], [r for r in wr if r], cost * (VS if q in "VS" and not kw else 1.0), dict(kw, due=now[0], step=now[1])])
 
-    def al(*names):
-        return [(n,) for n in names]
-
-    CY = 0.00083
-
-    def V(fn, rd, wr, n, f=1.0):
-        add("V", fn, rd, wr, 0.055 + max(64, n * f) * CY)
-
-    def S(fn, rd, wr, n, f=1.0):
-        add("S", fn, rd, wr, 0.15 + n * f * CY)
-
-    def MM(out, lhsT, rhs, start, stop, rd, wr, n):
-        add("T", lambda g, T: g.tensor.matmul(out(T), lhsT(T), rhs(T), start, stop), rd, wr, max(64, n) * CY * TR)
-
-    def tt(o, a, b, op):
-        return lambda g, T: g.vector.tensor_tensor(o(T), a(T), b(T), op)
-
-    def ts(o, a, s1, s2, op0, op1=None):
-        def fn(g, T):
-            x1 = s1(T) if callable_(s1) else s1
-            x2 = s2(T) if callable_(s2) else s2
-            if op1 is None:
-                return g.vector.tensor_scalar(o(T), a(T), x1, x2, op0)
-            return g.vector.tensor_scalar(o(T), a(T), x1, x2, op0, op1)
-        return fn
-
-    def callable_(x):
-        return x is not None and not isinstance(x, (int, float))
-
-    def tc(o, a):
-        return lambda g, T: g.vector.tensor_copy(o(T), a(T))
-
-    def act(o, a, f, **kw):
-        return lambda g, T: g.scalar.activation(o(T), a(T), f, **{k: (v(T) if callable_(v) else v) for k, v in kw.items()})
+    def at(t, step):
+        now[:] = [100.0 * (t + 1) + D[step], step]
 
     def B(name, a=None, b=None, st=None):
         if a is None:
-            return lambda T: T[name][:]
+            return (lambda T: T[name][:]), (name, 0, 1 << 20)
         if st is None:
-            return lambda T: T[name][:, a:b]
-        return lambda T: T[name][:, a:b:st]
+            return (lambda T: T[name][:, a:b]), (name, a, b)
+        return (lambda T: T[name][:, a:b:st]), (name, a, b)
+
+    def IX(win, off, a, b):
+        return (lambda T: T[win][:, :].indirect(T[off][:, a:b])), (win, 0, 1 << 20), (off, a, b)
 
     def slide(name, k):
-        return lambda T: T[name][:, 15 - k:15 - k + 128]
+        return (lambda T: T[name][:, 15 - k:15 - k + 128]), (name, 0, 1 << 20)
+
+    def val(x, T):
+        return x[0](T) if isinstance(x, tuple) else x
+
+    def regs(*xs):
+        return [r for x in xs if isinstance(x, tuple) for r in x[1:]]
+
+    def vcost(n, f):
+        return 0.055 + max(64, n * f) * CY
+
+    def MM(out, lhsT, rhs, start, stop, n, f=1.0):
+        MS([(out, lhsT, rhs)], start, stop, n * f)
+
+    def MS(mm, start, stop, n):
+        fl = [start, stop]
+        add("T", lambda g, T: [g.tensor.matmul(o[0](T), w[0](T), r[0](T), fl[0] and k == 0, fl[1] and k == len(mm) - 1) for k, (o, w, r) in enumerate(mm)],
+            [x for o, w, r in mm for x in regs(w, r)], [x for o, w, r in mm for x in regs(o)], len(mm) * (max(64, n) * CY * TR + TO), fl=fl)
+
+    def tt(o, a, b, op, n, f=1.0):
+        add("V", lambda g, T: g.vector.tensor_tensor(o[0](T), a[0](T), b[0](T), op), regs(a, b), regs(o), vcost(n, f))
+
+    def ts(o, a, s1, s2, op0, op1, n, f=1.0):
+        def fn(g, T):
+            if op1 is None:
+                return g.vector.tensor_scalar(o[0](T), a[0](T), val(s1, T), None, op0)
+            return g.vector.tensor_scalar(o[0](T), a[0](T), val(s1, T), val(s2, T), op0, op1)
+        add("V", fn, regs(a, s1, s2), regs(o), vcost(n, f))
+
+    def tc(o, a, n, f=1.0):
+        add("V", lambda g, T: g.vector.tensor_copy(o[0](T), a[0](T)), regs(a) + list(o[2:]), [o[1]], vcost(n, f))
+
+    def fill(o, c, n):
+        add("V", lambda g, T: g.vector.memset(o[0](T), c), [], regs(o), vcost(n, 0.5))
+
+    def act(o, a, f, n, fc=1.0, **kw):
+        add("S", lambda g, T: g.scalar.activation(o[0](T), a[0](T), f, **{k: val(v, T) for k, v in kw.items()}),
+            regs(a, *kw.values()), regs(o), (0.065 if len(a) > 2 else 0.15) + n * fc * CY)
+
+    def tiny(out, w, src, first, last, n=12, width=I):
+        for h in range(2):
+            MS([(out, slide(w, r), B(src, r, width, 16)) for r in range(8 * h, 8 * h + 8)], first and h == 0, last and h == 1, n)
 
     nd = [0]
 
-    def load(q, dst, src, cost):
+    def dma(q, dst, src, cost, load):
         k = nd[0]
         nd[0] += 1
-        add(q, lambda g, T: (g.sync if q == "Y" else g.scalar).dma_start(T[dst][:], T[src][:]), [], al(dst), cost, dma=k)
+        add(q, lambda g, T: (g.sync if q == "Y" else g.scalar).dma_start(T[dst][:], T[src][:]),
+            [] if load else [(src, 0, 1 << 20)], [(dst, 0, 1 << 20)] if load else [], cost, dma=k)
 
-    load("Y", "SI", "s0", 2.5)
-    load("S", "PI", "p0", 2.5)
-    load("Y", "X", "x0", 6.0)
-    load("S", "PLT", "pl", 6.0)
-    load("Y", "L0", "z0", 6.0)
-    load("Y", "THI", "th", 6.0)
-    load("S", "FA", "f0", 6.0)
+    dma("Y", "X", "x0", 4.0, True)
+    dma("S", "SI", "s0", 2.5, True)
+    dma("S", "L0", "z0", 3.0, True)
+    dma("S", "PI", "p0", 3.0, True)
+    dma("Y", "PLT", "pl", 6.0, True)
+    dma("S", "THI", "th", 4.0, True)
+    dma("S", "FA", "f0", 4.0, True)
 
-    def G(fn, wr, n):
-        add("G", fn, [], wr, 0.15 + 2 * n * CY)
-    G(lambda g, T: g.iota(T.ip[:], [[0, 1]], 0, 1), al("ip"), 1)
-    G(lambda g, T: g.iota(T.irow[:], [[1, 144]], 0, 0), al("irow"), 144)
-    G(lambda g, T: g.iota(T.ibase[:], [[256, 12]], 0, 0), al("ibase"), 12)
-    V(ts(B("ig"), B("ip"), 4, None, A.arith_shift_right), al("ip"), al("ig"), 1)
-    V(tc(B("pf"), B("ip")), al("ip"), al("pf"), 1)
-    V(tc(B("gf"), B("ig")), al("ig"), al("gf"), 1)
-    V(tc(B("row"), B("irow")), al("irow"), al("row"), 144)
-    V(ts(B("igrow"), B("irow", 0, 128), 4, None, A.arith_shift_right), al("irow"), al("igrow"), 128)
-    V(tc(B("grow"), B("igrow")), al("igrow"), al("grow"), 128)
-    V(ts(B("g16"), B("gf"), 16.0, None, A.mult), al("gf"), al("g16"), 1)
-    V(ts(B("g15"), B("gf"), 16.0, 15.0, A.mult, A.add), al("gf"), al("g15"), 1)
-    V(ts(B("p1"), B("pf"), 1.0, None, A.add), al("pf"), al("p1"), 1)
-    V(tt(B("lf"), B("pf"), B("g16"), A.subtract), al("pf", "g16"), al("lf"), 1)
-    V(ts(B("l21"), B("lf"), 2.0, 1.0, A.mult, A.add), al("lf"), al("l21"), 1)
-    V(ts(B("l0"), B("lf"), 0.0, None, A.is_equal), al("lf"), al("l0"), 1)
-    V(ts(B("nl0"), B("l0"), -1.0, None, A.mult), al("l0"), al("nl0"), 1)
-    V(ts(B("nl15"), B("lf"), 15.0, None, A.not_equal), al("lf"), al("nl15"), 1)
-    V(ts(B("r16"), B("lf"), 16.0, 7.5, A.mult, A.add), al("lf"), al("r16"), 1)
-    V(ts(B("base"), B("ibase"), B("r16"), None, A.add), al("ibase", "r16"), al("base"), 12)
-    V(ts(B("W1"), B("row"), B("g15"), None, A.is_equal), al("row", "g15"), al("W1"), 144)
-    V(ts(B("Wm"), B("row"), B("g15"), -1.0, A.is_equal, A.mult), al("row", "g15"), al("Wm"), 144)
-    V(ts(B("W2"), B("row"), B("g15"), 2.0, A.is_equal, A.mult), al("row", "g15"), al("W2"), 144)
-    V(ts(B("Wu"), B("row"), B("g15"), B("l21"), A.is_equal, A.mult), al("row", "g15", "l21"), al("Wu"), 144)
-    V(ts(B("Wh"), B("row"), B("g15"), None, A.is_equal), al("row", "g15"), al("Wh"), 144)
+    def G(fn, rd, wr, n):
+        add("G", fn, regs(*rd), regs(wr), 0.15 + 2 * n * CY)
+    G(lambda g, T: g.iota(T.ip[:], [[0, 1]], 0, 1), [], B("ip"), 1)
+    G(lambda g, T: g.iota(T.r4[:], [[0, 32], [1, 4]], 0, 0, allow_small_or_imprecise_dtypes=True), [], B("r4"), 128)
+    G(lambda g, T: g.iota(T.row[:], [[1, 144]], 0, 0, allow_small_or_imprecise_dtypes=True), [], B("row"), 144)
+    G(lambda g, T: g.iota(T.grow[:], [[1, 8], [0, 16]], 0, 0, allow_small_or_imprecise_dtypes=True), [], B("grow"), 128)
+    G(lambda g, T: g.iota(T.ibase[:], [[-256, 12]], 0, 0), [], B("ibase"), 12)
     R128 = B("row", 0, 128)
-    V(ts(B("Ib"), R128, B("pf"), None, A.is_equal), al("row", "pf"), al("Ib"), 128)
-    V(ts(B("Ihf"), R128, B("pf"), 0.5, A.is_equal, A.mult), al("row", "pf"), al("Ihf"), 128)
-    V(ts(B("I100"), R128, B("pf"), -100.0, A.is_equal, A.mult), al("row", "pf"), al("I100"), 128)
-    V(ts(B("Ih"), R128, B("pf"), None, A.is_equal), al("row", "pf"), al("Ih"), 128)
-    V(ts(B("OB"), B("grow"), B("gf"), None, A.is_equal), al("grow", "gf"), al("OB"), 128)
-    V(ts(B("im8"), B("irow", 0, 128), NC - 1, None, A.bitwise_and), al("irow"), al("im8"), 128)
-    V(ts(B("mk"), B("im8"), NC - NQ - 0.5, -1.0, A.is_lt, A.mult), al("im8"), al("mk"), 128)
-    V(tt(B("OBm"), B("mk"), B("OB"), A.mult), al("mk", "OB"), al("OBm"), 128, 2)
-    V(ts(B("Im"), R128, B("pf"), -1.0, A.is_equal, A.mult), al("row", "pf"), al("Im"), 128)
-    V(ts(B("GT"), R128, B("pf"), None, A.is_gt), al("row", "pf"), al("GT"), 128)
-    V(tt(B("Ls"), B("GT"), B("OB"), A.mult), al("GT", "OB"), al("Ls"), 128, 2)
-    V(tt(B("Li"), B("Ls"), B("Ib"), A.add), al("Ls", "Ib"), al("Li"), 128, 2)
-    V(ts(B("Tp"), R128, B("g16"), None, A.is_equal), al("row", "g16"), al("Tp"), 128)
-    V(tt(B("TpI"), B("Tp"), B("Ih"), A.subtract), al("Tp", "Ih"), al("TpI"), 128, 2)
-    V(ts(B("Sh"), R128, B("p1"), B("nl15"), A.is_equal, A.mult), al("row", "p1", "nl15"), al("Sh"), 128)
-    V(tt(B("ShI"), B("Sh"), B("Ih"), A.subtract), al("Sh", "Ih"), al("ShI"), 128, 2)
-    V(lambda g, T: g.vector.memset(T.zz[:], 0.0), [], al("zz"), I)
-    V(lambda g, T: g.vector.memset(T.cq[:], -0.5), [], al("cq"), I)
-    V(lambda g, T: g.vector.memset(T.c75[:], -7.5), [], al("c75"), 16)
+    ts(B("ig"), B("ip"), 4, None, A.arith_shift_right, None, 1)
+    tc(B("pf"), B("ip"), 1)
+    tc(B("gf"), B("ig"), 1)
+    ts(B("g16"), B("gf"), 16.0, None, A.mult, None, 1)
+    ts(B("g15"), B("gf"), 16.0, 15.0, A.mult, A.add, 1)
+    tt(B("lf"), B("pf"), B("g16"), A.subtract, 1)
+    ts(B("l21"), B("lf"), 2.0, 1.0, A.mult, A.add, 1)
+    ts(B("l0"), B("lf"), 0.0, None, A.is_equal, None, 1)
+    ts(B("W1"), B("row"), B("g15"), None, A.is_equal, None, 144)
+    ts(B("Wu"), B("W1"), B("l21"), None, A.mult, None, 144, 0.5)
+    ts(B("Ib"), R128, B("pf"), None, A.is_equal, None, 128)
+    ts(B("OB"), B("grow"), B("gf"), None, A.is_equal, None, 128)
+    for dst, src, c, n in (("Wmh", "W1", -0.5, 144), ("Wm", "W1", -1.0, 144), ("Im", "Ib", -1.0, 128),
+                           ("I32", "Ib", 32.0, 128), ("I64m", "Ib", -64.0, 128), ("OBh", "OB", 0.5, 128),
+                           ("OBB", "OB", -BIG, 128), ("W2", "W1", 2.0, 144)):
+        act(B(dst), B(src), F.Copy, n, scale=c)
+    if "m" in WAYS:
+        now[0] = -2.0
+        act(B("r4"), B("r4"), F.Sigmoid, 128, 12.0, scale=1000.0, bias=500.0 - 1000.0 * WAYS[2:].index("m"))
+        now[0] = 0.0
+        ts(B("r4"), B("r4"), -1.0, None, A.mult, None, 128, 0.5)
+        tt(B("OBm"), B("r4"), B("OB"), A.mult, 128, 2)
 
-    V(tc(B("PU"), B("PI")), al("PI"), al("PU"), 12)
-    V(tc(B("SU"), B("SI")), al("SI"), al("SU"), I)
-    V(ts(B("E16"), lambda T: T.PLT[:, :].indirect(T.PU[:, 0:12]), -CEN, None, A.add), al("PLT", "PU"), al("E16"), I, 1.6)
-    V(ts(B("EU"), B("E16"), CEN, None, A.add), al("E16"), al("EU"), I)
-    V(ts(B("b5", 0, I), B("SI"), -CEN, None, A.add), al("SI"), [("b5", 0, I)], I)
-    V(tc(B("PF"), B("PI")), al("PI"), al("PF"), 12)
-    V(tc(B("BND"), B("THI")), al("THI"), al("BND"), I)
+    def sel(dst, src, pat, op, fill_, base, cm):
+        G(lambda g, T: g.affine_select(T[dst][:], T[src][:], pat, op, fill_, base, cm), [B(src)], B(dst), 128)
+    col = [[1, 128]]
+    sel("Ls", "OB", col, A.is_gt, 0.0, 0, -1)
+    sel("BIL", "OBB", col, A.is_gt, 0.0, 0, -1)
+    sel("BIL", "BIL", col, A.not_equal, BIG, 0, -1)
+    sel("Sh", "OB", col, A.is_equal, 0.0, -1, -1)
+    sel("ShI", "Sh", col, A.not_equal, -1.0, 0, -1)
+    for x, y in (("Tp0", "Ib"), ("Tp", "OB")):
+        sel(x, y, [[0, 8], [1, 16]], A.is_equal, 0.0, 0, 0)
+    G(lambda g, T: g.iota(T.cb[:, 0:I], [[0, I]], -int(BIG), 0, allow_small_or_imprecise_dtypes=True), [], B("cb", 0, I), I)
+    G(lambda g, T: g.iota(T.ct[:], [[0, I]], int(15 * CEN), 0, allow_small_or_imprecise_dtypes=True), [], B("ct"), I)
+    fill(B("cq"), -0.5, CW)
+    ts(B("cz"), B("cq"), 0.0, -127.9375, A.mult, A.add, CW, 0.5)
+    ts(B("Ihq"), B("Ib"), 0.5 - 2.0 ** -11, None, A.mult, None, 128, 0.5)
+    ts(B("nB", 3, 4), B("lf"), 1.0, 0.28125, A.is_equal, A.mult, 1)
+    ts(B("nB", 4, 5), B("l0"), -2048.0, B("nB", 3, 4), A.mult, A.add, 1)
+    ts(B("cv"), B("cq", 0, I), 0.0, B("nB", 4, 5), A.mult, A.add, I, 0.5)
+    ts(B("nB", 1, 2), B("l0"), -1.0, BIG, A.add, A.mult, 1)
+    ts(B("cb", I, CW), B("cq", 0, I), 0.0, B("nB", 1, 2), A.mult, A.add, I, 0.5)
+    ts(B("W0"), B("W1"), B("l0"), None, A.mult, None, 144, 0.5)
+    if not CNT:
+        ts(B("nB", 2, 3), B("l0"), -0.1 * BIG, 0.15 * BIG, A.mult, A.add, 1)
+    ts(B("r16"), B("lf"), -16.0, 24568.5, A.mult, A.add, 1)
+    ts(B("base"), B("ibase"), B("r16"), None, A.add, None, 12)
 
-    def gathers():
-        cs = CSPL
-        V(lambda g, T: g.vector.tensor_copy(T.XS[:, 0:16 * cs], T.X[:, :].indirect(T.SU[:, 0:cs])), al("X", "SU"), [("XS", 0, 16 * cs)], 16 * cs, 1.5)
-        if cs < I:
-            S(lambda g, T: g.scalar.activation(T.XS[:, 16 * cs:W], T.X[:, :].indirect(T.SU[:, cs:I]), F.Copy), al("X", "SU"), [("XS", 16 * cs, W)], 16 * (I - cs), 1.5)
-        for c in range(XC):
-            a, b = I // XC * c, I // XC * (c + 1)
-            S(lambda g, T, a=a, b=b: g.scalar.activation(T.XE[:, 16 * a:16 * b], T.X[:, :].indirect(T.EU[:, a:b]), F.Copy), al("X", "EU"), [("XE", 16 * a, 16 * b)], 16 * (b - a), 1.5)
+    def late():
+        G(lambda g, T: g.iota(T.KT[:], [[PLN, TURNS], [0, 12]], PLN, 0, allow_small_or_imprecise_dtypes=True), [B("Y0")], B("KT"), 96)
+        for h in range(4):
+            o = 512 * h
+            G(lambda g, T, h=h: g.iota(T.IC0[:], [[1, 4], [0, 128]], 1 + 4 * h, 0, allow_small_or_imprecise_dtypes=True), [B("Y0")], B("IC0"), 512)
+            G(lambda g, T, o=o: g.affine_select(T.IC[:, o:o + 512], T.IC0[:], [[0, 4], [-1, 128]], A.is_equal, 0.0, 0, 1), [B("IC0")], B("IC", o, o + 512), 512)
 
-    gathers()
-
-    def mixed(n):
-        fast, slow = list(range(NC - n)), list(range(NC - n, NC))
-        res = []
-        while fast or slow:
-            if slow and (not fast or len(slow) * (NC - n) >= len(fast) * n):
-                res.append(slow.pop(0))
-            else:
-                res.append(fast.pop(0))
-        return res
-
-    turn_bank = [0]
-
-    def bank():
-        turn_bank[0] += 1
-        return "b4" if turn_bank[0] % 2 else "b6"
+    now[0] = -1.0
+    tc(B("PU"), B("PI"), 12)
+    tc(B("SU"), B("SI"), I)
+    ts(B("E16"), IX("PLT", "PU", 0, 12), -CEN, None, A.add, None, I, GA)
+    ts(B("EU"), B("E16"), CEN, None, A.add, None, I, 0.5)
+    ts(B("S16"), B("SI"), -CEN, None, A.add, None, I)
+    ts(B("BND"), B("THI"), -2048.0, 1.0 / 64, A.add, A.mult, I)
+    now[0] = 0.0
+    if ATS:
+        fill(B("AT"), 0.0, I)
+    else:
+        ts(B("TH16"), B("THI"), -2048.0, 1.0 / 64, A.add, A.mult, I)
 
     for t in range(TURNS):
         L, Y = "L%d" % t, "Y%d" % t
         f0, f1 = ("FA", "FB") if t % 2 == 0 else ("FB", "FA")
-        s0, s1 = (0, I) if t % 2 == 0 else (I, 0)
-        if t == 0:
-            for c in range(16):
-                S(act(B("IC", 128 * c, 128 * c + 128), B("Ib"), F.Copy, scale=float(c + 1)), al("Ib"), [("IC", 128 * c, 128 * c + 128)], 128)
-        MM(B("b3", 0, I), B("Ib"), B("zz"), True, False, al("Ib", "zz"), [("b3", 0, I)], I)
-        for c in range(XC):
-            p, q = I // XC * c, I // XC * (c + 1)
-            for k in [k for k in range(16) if k % NC < NC - NQ]:
-                MM(B("b3", p, q), slide("Wm", k), B("XE", 16 * p + k, 16 * q, 16), False, False, al("Wm") + [("XE", 16 * p, 16 * q)], [("b3", p, q)], q - p)
-        for m in range(NK):
-            MM(B("b0", m, CW, NK), B("Ib"), B(L), True, True, al("Ib", L), [("b0", 0, CW)], I)
-        MM(B("b3", 0, I), B("OBm"), B(L), False, False, al("OBm", L), [("b3", 0, I)], I)
-        for r in range(16):
-            MM(B("b7", 0, 12), slide("Wu", r), B(L, r, I, 16), r == 0, r == 15, al("Wu", L), [("b7", 0, 12)], 12)
-        MM(B("b7", 256, 256 + I), B("Ihf"), B(L), True, False, al("Ihf", L), [("b7", 256, 256 + I)], I)
-        MM(B("b7", 256, 256 + I), B("Ihf"), B(f0), False, False, al("Ihf", f0), [("b7", 256, 256 + I)], I)
-        MM(B("b7", 256, 256 + I), B("Ihf"), B("cq"), False, True, al("Ihf", "cq"), [("b7", 256, 256 + I)], I)
-        V(ts(B(f1), B("b7", 256, 256 + I), MAGIC, MAGIC, A.add, A.subtract), [("b7", 256, 256 + I)], al(f1), I)
-        V(tc(B("H1"), B("b7", 0, 12)), [("b7", 0, 12)], al("H1"), 12)
-        V(ts(B("H2"), B("H1"), 4095, None, A.bitwise_and), al("H1"), al("H2"), 12)
-        V(ts(B("H3"), B("H2"), 1184.0, None, A.add), al("H2"), al("H3"), 12)
-        V(tt(B("H4"), B("H2"), B("H3"), A.mult), al("H2", "H3"), al("H4"), 12)
-        V(ts(B("H7"), B("H4"), 5, PLN - 1, A.arith_shift_right, A.bitwise_and), al("H4"), al("H7"), 12)
-        V(tc(B("PU"), B("H7")), al("H7"), al("PU"), 12)
-        V(ts(B("CAND"), lambda T: T.PLT[:, :].indirect(T.PU[:, 0:12]), -CEN, None, A.add), al("PLT", "PU"), al("CAND"), I, 1.6)
-        V(tt(B("DES"), B("E16"), B("b5", s0, s0 + I), A.subtract), al("E16") + [("b5", s0, s0 + I)], al("DES"), I)
-        def tensor_diff(X, q, bk):
-            for m in range(NK):
-                k = q + NC * m
-                MM(B(bk, I * m, I * m + I), B("Ib"), lambda T, k=k: T[X][:, k:W:16], True, False, al("Ib", X), [(bk, I * m, I * m + I)], I)
-                MM(B(bk, I * m, I * m + I), B("Im"), B(L), False, True, al("Im", L), [(bk, I * m, I * m + I)], I)
+        last = t == TURNS - 1
+        H, VL, UP = ("b2", 0), ("b2", I), ("b3", 0)
 
-        VQ = NC - NS
-        for q in range(VQ):
-            V(tt(B("D", CW * q, CW * q + CW), lambda T, q=q: T.XS[:, q:W:NC], B("b0", 0, CW), A.subtract),
-              al("XS") + [("b0", 0, CW)], [("D", CW * q, CW * q + CW)], CW)
-        chunks = [(c, min(VQ, c + 2)) for c in range(0, VQ, 2)]
-        for c, e in chunks:
-            a, b = CW * c, CW * e
-            S(act(B("AB", a, b), B("D", a, b), F.Abs), [("D", a, b)], [("AB", a, b)], b - a)
-        for q in range(VQ, NC):
-            bk = bank()
-            tensor_diff("XS", q, bk)
-            S(act(B("AB", CW * q, CW * q + CW), B(bk, 0, CW), F.Abs), [(bk, 0, CW)], [("AB", CW * q, CW * q + CW)], CW)
-            S(act(B("SG", CW * q, CW * q + CW), B(bk, 0, CW), F.Sign, bias=-0.5), [(bk, 0, CW)], [("SG", CW * q, CW * q + CW)], CW)
-        for c, e in chunks:
-            a, b = CW * c, CW * e
-            if c < 2 * NF:
-                V(ts(B("SG", a, b), B("D", a, b), 0.0, -0.5, A.is_gt, A.add), [("D", a, b)], [("SG", a, b)], b - a, 0.5)
+        def P(reg, a=0, b=I, st=None):
+            return B(reg[0], reg[1] + a, reg[1] + b, st)
+        vc = VCUT if t else VCUT0
+        cuts = [0] + list(vc) + ([I] if vc[-1] < I else [])
+        at(t, "xs")
+        for a, b in zip(cuts[:-1], cuts[1:]):
+            if b <= vc[-1]:
+                ts(B("XS", 16 * a, 16 * b), IX("X", "SU", a, b), -128.0, None, A.add, None, 16 * (b - a), GA)
             else:
-                S(act(B("SG", a, b), B("D", a, b), F.Sign, bias=-0.5), [("D", a, b)], [("SG", a, b)], b - a)
-
-        def piece(buf, q, m, direct):
-            return B(buf, CW * q + I * m, CW * q + I * m + I) if direct else B(buf, CW * q + m, CW * q + CW, NK)
-
-        sq = [(q, m) for q in mixed(NS) for m in range(NK)]
-        for (q, m) in sq:
-            MM(B("b1", 0, I), slide("W1", q + NC * m), piece("AB", q, m, q >= VQ), (q, m) == sq[0], (q, m) == sq[-1], al("W1") + [("AB", CW * q, CW * q + CW)], [("b1", 0, I)], I)
-        gq = sq if NS == 0 else [x for x in sq if x[0] >= VQ] + [x for x in sq if x[0] < VQ]
-        for (q, m) in gq:
-            w = "W2" if q < min(VQ, 2 * NF) else "W1"
-            MM(B("b2", 0, I), slide(w, q + NC * m), piece("SG", q, m, q >= VQ), (q, m) == gq[0], (q, m) == gq[-1], al(w) + [("SG", CW * q, CW * q + CW)], [("b2", 0, I)], I)
-        for q in range(NC - NQ, NC):
-            bk = bank()
-            tensor_diff("XE", q, bk)
-            S(act(B("MX", CW * q, CW * q + CW), B(bk, 0, CW), F.Abs), [(bk, 0, CW)], [("MX", CW * q, CW * q + CW)], CW)
-        for q in range(NC - NQ):
-            V(tt(B("MX", CW * q, CW * q + CW), lambda T, q=q: T.XE[:, q:W:NC], B("b0", 0, CW), A.max),
-              al("XE") + [("b0", 0, CW)], [("MX", CW * q, CW * q + CW)], CW)
-        pq = [(q, m) for q in mixed(NQ) for m in range(NK)]
-        for (q, m) in pq:
-            k = q + NC * m
-            if q < NC - NQ:
-                MM(B("b3", 0, I), slide("W2", k), B("MX", CW * q + m, CW * q + CW, NK), False, (q, m) == pq[-1], al("W2") + [("MX", CW * q, CW * q + CW)], [("b3", 0, I)], I)
+                act(B("XS", 16 * a, W), IX("X", "SU", a, I), F.Identity, 16 * (I - a), GA, bias=-128.0)
+        for c in PARTS:
+            at(t, "xe%d" % c)
+            if t == 0 and c == PARTS[-1]:
+                tc(B("XE", 16 * PA * c, 16 * PA * (c + 1)), IX("X", "EU", PA * c, PA * (c + 1)), 16 * PA, GA)
             else:
-                MM(B("b3", 0, I), slide("W1", k), B("MX", CW * q + I * m, CW * q + I * m + I), False, (q, m) == pq[-1], al("W1") + [("MX", CW * q, CW * q + CW)], [("b3", 0, I)], I)
-        V(tt(B("RS"), B("b1", 0, I), B("BND"), A.is_lt), [("b1", 0, I)] + al("BND"), al("RS"), I)
-        MM(B("b1", I, 2 * I), B("Ls"), B("RS"), True, True, al("Ls", "RS"), [("b1", I, 2 * I)], I)
-        V(tt(B("FI"), B("RS"), B("b1", I, 2 * I), A.is_gt), al("RS") + [("b1", I, 2 * I)], al("FI"), I)
-        V(tt(B("FF"), B("FI"), B("b5", s0, s0 + I), A.mult), al("FI") + [("b5", s0, s0 + I)], al("FF"), I)
-        MM(B("b4", I, 2 * I), B("Li"), B("RS"), True, True, al("Li", "RS"), [("b4", I, 2 * I)], I)
-        S(act(B("b1", 0, I), B("b4", I, 2 * I), F.Relu, scale=-1.0, bias=1.0), [("b4", I, 2 * I)], [("b1", 0, I)], I)
-        S(act(B("KK"), B("b2", 0, I), F.Relu, scale=16.0, bias=128.0), [("b2", 0, I)], al("KK"), I)
-        MM(B("b2", I, 2 * I), B("OB"), B("RS"), True, False, al("OB", "RS"), [("b2", I, 2 * I)], I)
-        MM(B("b2", I, 2 * I), B("I100"), B("FI"), False, True, al("I100", "FI"), [("b2", I, 2 * I)], I)
-        V(tt(B("b2", 0, I), B("b2", I, 2 * I), B("KK"), A.is_gt), [("b2", I, 2 * I)] + al("KK"), [("b2", 0, I)], I)
-        V(tt(B("WD"), B("DES"), B("b2", 0, I), A.mult), al("DES") + [("b2", 0, I)], al("WD"), I)
-        V(tt(B("RR"), B("WD"), B("b5", s0, s0 + I), A.add), al("WD") + [("b5", s0, s0 + I)], al("RR"), I)
-        V(tt(B("QQ"), B("RR"), B("b1", 0, I), A.mult), al("RR") + [("b1", 0, I)], al("QQ"), I)
-        V(tt(B("RP"), B("b3", 0, I), B("BND"), A.is_lt), [("b3", 0, I)] + al("BND"), al("RP"), I)
-        MM(B("b3", I, 2 * I), B("OB"), B("RS"), True, False, al("OB", "RS"), [("b3", I, 2 * I)], I)
-        MM(B("b3", I, 2 * I), B("Ls"), B("RP"), False, True, al("Ls", "RP"), [("b3", I, 2 * I)], I)
-        MM(B("b4", 0, I), B("OB"), B("RS"), True, False, al("OB", "RS"), [("b4", 0, I)], I)
-        MM(B("b4", 0, I), B("OB"), B("RP"), False, True, al("OB", "RP"), [("b4", 0, I)], I)
-        V(tt(B("b6", I, 2 * I), B("RP"), B("b3", I, 2 * I), A.is_gt), al("RP") + [("b3", I, 2 * I)], [("b6", I, 2 * I)], I)
-        S(act(B("b4", I, 2 * I), B("b4", 0, I), F.Relu, scale=B("nl0"), bias=B("l0")), [("b4", 0, I)] + al("nl0", "l0"), [("b4", I, 2 * I)], I)
-        V(tt(B("b6", 0, I), B("E16"), B("b6", I, 2 * I), A.mult), al("E16") + [("b6", I, 2 * I)], [("b6", 0, I)], I)
-        V(tt(B("HH"), B("CAND"), B("b4", I, 2 * I), A.mult), al("CAND") + [("b4", I, 2 * I)], al("HH"), I)
-        V(tt(B("GG"), B("HH"), B("b6", 0, I), A.add), al("HH") + [("b6", 0, I)], al("GG"), I)
-        for src in ("FF", "GG"):
-            for r in range(16):
-                MM(B("b7", 16, 28), slide("Wh", r), B(src, r, I, 16), (src, r) == ("FF", 0), (src, r) == ("GG", 15), al("Wh", src), [("b7", 16, 28)], 12)
-        V(ts(B("TU"), B("b7", 16, 28), CEN, None, A.add), [("b7", 16, 28)], al("TU"), 12)
-        V(lambda g, T, f1=f1: g.vector.tensor_tensor(T.YD[:], T.X[:, :].indirect(T.TU[:, 0:12]), T[f1][:], A.subtract), al("X", "TU", f1), al("YD"), I, 1.6)
-        S(act(B(Y), B("YD"), F.Abs), al("YD"), al(Y), I)
-        if t < TURNS - 1:
-            add("G", ("send", t), al(Y), [], 1.2, send=t)
+                act(B("XE", 16 * PA * c, 16 * PA * (c + 1)), IX("X", "EU", PA * c, PA * (c + 1)), F.Copy, 16 * PA, GA)
+        at(t, "pre")
+        MM(B("b0", 0, CW), B("Ib"), B("cz"), True, False, CW)
+        MM(P(H), B("I32"), B("BND"), True, False, I)
+        MM(P(VL), B("OB"), B("cv"), False, False, I)
+        MM(P(UP), B("I64m"), B("BND"), True, False, I)
+        if ATS and t:
+            MM(P(H), B("I32"), B("AT"), False, False, I)
+            MM(P(UP), B("I64m"), B("AT"), False, False, I)
+        if not last:
+            MM(B("b3", I, CW), B("Im"), B("E16"), False, False, I)
+        if last:
+            at(t, "yx")
+            for h in range(4):
+                MS([(B("b1", 0, I), B("IC", 128 * c, 128 * c + 128), B("X", c, W, 16)) for c in range(4 * h, 4 * h + 4)], h == 0, False, I)
+            n = 12 * t
+            tiny(B("b1", 256, 256 + n), "W0", "SWH", False, False, n, t * I)
+            if not ATS:
+                tt(B("TH16"), B("BND"), B("TH16"), A.subtract, I, 2)
+            tiny(B("b1", 384, 396), "W0", "AT" if ATS else "TH16", False, True)
+            tc(B("OX"), B("b1", 0, I), I)
+            tt(B("PK", 0, n), B("PH", 0, n), B("KT", 0, n), A.add, n, 2)
+            tc(B("KK", 84, 96), B("PI"), 12)
+            tt(B("KK", 0, n), B("b1", 256, 256 + n), B("PK", 0, n), A.mult, n)
+            tc(B("PE"), B("b1", 384, 396), 12)
+            ts(B("PK", 0, 12), B("PE"), float(PLN), None, A.mult, None, 12)
+            for a, w in ((0, 48), (96, 24)):
+                tt(B("KK", a + 2 * w, a + 3 * w), B("KK", a, a + w), B("KK", a + w, a + 2 * w), A.max, w, 2)
+            tt(B("K0"), B("KK", 144, 156), B("KK", 156, 168), A.max, 12, 2)
+            ts(B("PE"), B("K0"), PLN - 1, None, A.bitwise_and, None, 12)
+            ts(B("PK", 12, 24), B("PK", 0, 12), float(PLN), None, A.add, None, 12)
+            tt(B("YPF"), B("PK", 0, 12), B("PE"), A.add, 12)
+        at(t, "sx")
+        for a, b in zip(cuts[:-1], cuts[1:]):
+            for h in range(4):
+                MS([(P(H, a, b), slide("Wmh", k), B("XS", 16 * a + k, 16 * b, 16)) for k in range(4 * h, 4 * h + 4)], False, False, b - a)
+        at(t, "zp")
+        MS([(B("b0", m, CW, 2), B("Ib"), B(L)) for m in range(2)], False, True, I)
+        at(t, "pre")
+        MM(B("b7", 256, 256 + I), B("Ihq"), B(f0), True, False, I)
+        MM(B("b7", 48, 48 + I), B("Im"), B("S16"), False, False, I)
+        MM(B("b7", 48, 48 + I), B("Ib"), B("E16"), False, False, I)
+        at(t, "u")
+        MM(B("b7", 256, 256 + I), B("Ihq"), B(L), False, False, I)
+        tiny(B("b7", 0, 12), "Wu", L, False, True)
+        at(t, "sz")
+        MM(P(H), B("OBh"), B(L), False, False, I)
+        MM(P(VL), B("OB"), B(L), False, False, I)
+        at(t, "hash")
+        H1, H2, H3, H4 = [B("HH", 12 * k, 12 * k + 12) for k in range(4)]
+        tc(H1, B("b7", 0, 12), 12)
+        ts(H2, H1, 4095, None, A.bitwise_and, None, 12)
+        ts(H3, H2, 1184.0, None, A.add, None, 12)
+        tt(H4, H2, H3, A.mult, 12)
+        ts(B("PH", 12 * t, 12 * t + 12), H4, 5, PLN - 1, A.arith_shift_right, A.bitwise_and, 12)
+        tc(B("PU"), B("PH", 12 * t, 12 * t + 12), 12)
+        at(t, "cand")
+        ts(B("CAND"), IX("PLT", "PU", 0, 12), -CEN, None, A.add, None, I, GA)
+        if not last:
+            MM(B("b3", I, CW), B("Ib"), B("CAND"), False, False, I)
+        for q in range(NC):
+            at(t, "mn")
+            tt(B("MN", CW * q, CW * q + CW), B("XS", q, W, NC), B("b0", 0, CW), A.min, CW)
+            at(t, "sv")
+            MS([(P(VL), slide("Wm", q + NC * m), B("MN", CW * q + m, CW * q + CW, 2)) for m in range(2)], False, q == NC - 1, I)
+        sums = []
+        slow = [x for x in WAYS if x == "t"]
+        ns = 0
+        if len(slow) < 6:
+            at(t, "zq")
+            MS([(B("b1", m, 512, 4), B("Ib"), B(L, PA, I)) for m in range(4)], True, True, I - PA)
+        if "m" in WAYS:
+            MM(P(UP, PA, I), B("OBm"), B(L, PA, I), False, False, I - PA)
+        for n, way in enumerate(WAYS):
+            a, b, st, h = (0, PA, 2, n) if n < 2 else (PA, I, 4, n - 2)
+            d, o = 16 // st, 512 * n
+            xe, mx = B("XE", 16 * a + h, 16 * b, st), B("MX", o, o + 512)
+            if way == "t":
+                bk = "b%d" % (4 + ns % 2)
+                ns += 1
+                at(t, "dx%d" % n)
+                MM(B(bk), B("Ib"), xe, True, False, 512)
+                at(t, "dz%d" % n)
+                MS([(B(bk, m, 512, d), B("Im"), B(L, a, b)) for m in range(d)], False, True, b - a)
+                at(t, "pp%d" % n)
+                act(mx, B(bk), F.Abs, 512)
+            elif way == "m":
+                at(t, "dx%d" % n)
+                MS([(P(UP, a, b), slide("Wm", st * m + h), B("XE", 16 * a + st * m + h, 16 * b, 16)) for m in range(d)], False, False, b - a)
+                at(t, "pp%d" % n)
+                tt(mx, xe, B("b1"), A.max, 512)
+            else:
+                at(t, "dx%d" % n)
+                tt(B("DE", o - 1024, o - 512), xe, B("b1"), A.subtract, 512)
+                at(t, "pp%d" % n)
+                act(mx, B("DE", o - 1024, o - 512), F.Abs, 512)
+            sums.append(([(P(UP, a, b), slide("W2" if way == "m" else "W1", st * m + h), B("MX", o + m, o + 512, d)) for m in range(d)], "sp%d" % n, b - a))
+        for n, (mm, step, w) in enumerate(sums):
+            at(t, step)
+            MS(mm, False, n == len(sums) - 1, w)
+        at(t, "rs")
+        ts(B("R2"), P(VL), -0.65625, 0.1875, A.max, A.add, I)
+        tt(B("RS"), P(H), B("R2"), A.is_gt, I)
+        at(t, "set")
+        tt(B("SET"), P(VL), B("R2"), A.is_le, I)
+        at(t, "pre")
+        MM(B("b6", 0, I), B("Ib"), B("S16"), True, False, I)
+        at(t, "rs")
+        MM(B("b6", 0, I), B("BIL"), B("RS"), False, True, I)
+        ts(B("TS"), B("b6", 0, I), -BIG, -CEN, A.add, A.max, I)
+        at(t, "f")
+        if FS:
+            act(B("FM"), B("b7", 256, 256 + I), F.Identity, I, bias=MAGIC)
+            at(t, "f2")
+            act(B(f1), B("FM"), F.Identity, I, bias=-MAGIC)
+        else:
+            ts(B(f1), B("b7", 256, 256 + I), MAGIC, MAGIC, A.add, A.subtract, I)
+        at(t, "an")
+        MM(B("b0", 0, I), B("Ls"), B("RS"), True, False, I)
+        MM(B("b0", I, CW), B("OBh"), B("RS"), False, False, I)
+        MM(B("b0", I, CW), B("I64m"), B("SET"), False, True, I)
+        act(B("AN"), B("b0", 0, CW), F.Sigmoid, CW, scale=1000.0, bias=-250.0)
+        at(t, "wd")
+        tt(B("b7", 48, 48 + I), B("b7", 48, 48 + I), B("AN", I, CW), A.mult, I)
+        tt(B("R16"), B("b7", 48, 48 + I), B("S16"), A.add, I)
+        MM(B("b6", 0, I), B("ShI"), B("R16"), True, True, I)
+        tt(B("QQ"), B("b6", 0, I), B("AN", 0, I), A.mult, I)
+        SH = B("b2", 0, I)
+        MM(SH, B("Sh"), B("R16"), True, False, I)
+        MM(SH, B("Tp0"), B("ct"), False, False, I)
+        nb, cb = ("b4", "b5") if len(slow) % 2 == 0 else ("b5", "b4")
+        at(t, "wp")
+        MM(B("b1", 0, CW), B("Ib"), B("cb"), True, False, CW)
+        MM(B("b1", 0, I), B("Ib"), B("E16"), False, False, I)
+        MM(B("b1", 0, I), B("OBB"), B("RS"), False, False, I)
+        MM(B("b1", I, CW), B("Tp0"), B("CAND"), False, False, I)
+        MM(B("b1", I, CW), B("OBB"), B("RS"), False, False, I)
+        at(t, "rp")
+        if RPS:
+            act(B("RP"), P(UP), F.Sigmoid, I, scale=-1000.0, bias=2047500.0)
+        else:
+            ts(B("RP"), P(UP), 2048.0, None, A.is_lt, None, I)
+        MM(B("b1", 0, I), B("BIL"), B("RP"), False, False, I)
+        MM(B("b1", I, CW), B("OBB"), B("RP"), False, True, I)
+        tt(B("TP"), B("b1", 0, I), B("TS"), A.max, I)
+        tt(B("TC"), B("b1", I, CW), B("TP"), A.max, I)
+        tiny(B(cb, 16, 28), "W1", "TC", True, True)
+        ts(B("TU"), B(cb, 16, 28), 16 * CEN, None, A.add, None, 12)
+        tt(B("YD"), IX("X", "TU", 0, 12), B(f1), A.subtract, I, GA)
+        act(B(Y), B("YD"), F.Abs, I)
+        if not last:
+            add("G", ("send", t), [(Y, 0, I)], [], 1.2, send=t)
             Ln = "L%d" % (t + 1)
             bl = (-t) % N
             a, b = BLK * bl, BLK * bl + BLK
-            S(act(B(Ln, a, b), B(Y, a, b), F.Copy), al(Y), [(Ln, a, b)], BLK)
-            wr = [(Ln, c, d) for c, d in ((0, a), (b, I)) if d > c]
-            add("R", None, [], wr, 3.8, arr=t)
-        MM(B("b7", 32, 44), B("Ib"), B("c75", 0, 12), True, False, al("Ib", "c75"), [("b7", 32, 44)], 12)
-        for r in range(16):
-            MM(B("b7", 32, 44), slide("W1", r), B(Y, r, I, 16), False, r == 15, al("W1", Y), [("b7", 32, 44)], 12)
-        MM(B("b0", 0, I), B("Ihf"), B(L), True, False, al("Ihf", L), [("b0", 0, I)], I)
-        MM(B("b0", 0, I), B("Ihf"), B("cq"), False, False, al("Ihf", "cq"), [("b0", 0, I)], I)
-        MM(B("b0", 0, I), B("Ihf"), B(Y), False, True, al("Ihf", Y), [("b0", 0, I)], I)
-        V(ts(B("QF"), B("b7", 32, 44), MAGIC16, MAGIC16, A.add, A.subtract), [("b7", 32, 44)], al("QF"), 12)
-        V(tt(B("RF"), B("base"), B("b7", 32, 44), A.add), al("base") + [("b7", 32, 44)], al("RF"), 12)
-        V(tt(B("MF"), B("RF"), B("QF"), A.subtract), al("RF", "QF"), al("MF"), 12)
-        V(tc(B("MU"), B("MF")), al("MF"), al("MU"), 12)
-        V(ts(B("WR"), B("b0", 0, I), MAGIC, MAGIC, A.add, A.subtract), [("b0", 0, I)], al("WR"), I)
-        V(lambda g, T: g.vector.tensor_copy(T.X[:, :].indirect(T.MU[:, 0:12]), T.WR[:]), al("WR", "MU", "X"), al("X"), I, 3.5)
-        o = (B("b5", s1, s1 + I), [("b5", s1, s1 + I)])
-        MM(o[0], B("Ih"), B("RR"), True, False, al("Ih", "RR"), o[1], I)
-        MM(o[0], B("ShI"), B("QQ"), False, False, al("ShI", "QQ"), o[1], I)
-        MM(o[0], B("TpI"), B("FF"), False, False, al("TpI", "FF"), o[1], I)
-        MM(o[0], B("Tp"), B("GG"), False, True, al("Tp", "GG"), o[1], I)
-        last = t == TURNS - 1
-        if last:
-            V(ts(B("OS"), o[0], CEN, None, A.add), o[1], al("OS"), I)
+            add("R", None, [], [(Ln, c, d) for c, d in ((0, a), (b, I)) if d > c], FLY, arr=t)
+            at(t, "own")
+            act(B(Ln, a, b), B("YD", a, b), F.Abs, BLK)
+            if t == 0:
+                late()
+        at(t, "m")
+        MB = B(cb, 32, 44)
+        tiny(MB, "W1", Y, True, True)
+        tt(B("QB"), MB, B("base"), A.add, 12)
+        tt(B("QF"), MB, B("QB"), A.subtract, 12)
+        ts(B("MU"), B("QF"), 24576.0, None, A.add, None, 12)
+        at(t, "wr")
+        MM(B("b0", 0, I), B("Ihq"), B(L), True, False, I)
+        MM(B("b0", 0, I), B("Ihq"), B(Y), False, True, I)
+        if WS:
+            act(B("WM"), B("b0", 0, I), F.Identity, I, bias=MAGIC)
+            act(B("WR"), B("WM"), F.Identity, I, bias=-MAGIC)
         else:
-            V(ts(B("SU"), o[0], CEN, None, A.add), o[1], al("SU"), I)
-        S(act(B("CR"), B("b4", 0, I), F.Relu, scale=B("nl0"), bias=B("l0")), [("b4", 0, I)] + al("nl0", "l0"), al("CR"), I)
-        S(act(B("C64"), B("b4", 0, I), F.Relu, scale=-64.0, bias=64.0), [("b4", 0, I)], al("C64"), I)
+            ts(B("WR"), B("b0", 0, I), MAGIC, MAGIC, A.add, A.subtract, I)
         if not last:
-            S(act(B("b3", 0, I), B("b4", 0, I), F.Relu, scale=-1.0, bias=1.0), [("b4", 0, I)], [("b3", 0, I)], I)
-            S(act(B("b3", I, 2 * I), B("b4", 0, I), F.Sign), [("b4", 0, I)], [("b3", I, 2 * I)], I)
-            V(tt(B("b6", 0, I), B("E16"), B("b3", I, 2 * I), A.mult), al("E16") + [("b3", I, 2 * I)], [("b6", 0, I)], I)
-            V(tt(B("HF"), B("CAND"), B("b3", 0, I), A.mult), al("CAND") + [("b3", 0, I)], al("HF"), I)
-            V(tt(B("E16"), B("HF"), B("b6", 0, I), A.add), al("HF") + [("b6", 0, I)], al("E16"), I)
-            V(ts(B("EU"), B("E16"), CEN, None, A.add), al("E16"), al("EU"), I, 0.5)
-        V(tt(B("BND"), B("BND"), B("C64"), A.add), al("BND", "C64"), al("BND"), I, 2)
+            tc(IX("X", "MU", 0, 12), B("WR"), I, 3.5)
+        else:
+            MM(B("b7", 0, I), B("OB"), B(Y), True, True, I)
+            ts(B("MN", 0, I), B("b7", 0, I), 24568.5, None, A.add, None, I)
+            tt(B("FM"), B("b7", 0, I), B("MN", 0, I), A.subtract, I)
+            ts(B("b7", I, CW), B("FM"), 24577.0, -1.0, A.add, A.mult, I)
+            tt(B("YD"), IX("X", "MU", 0, 12), B("WR"), A.subtract, I, GA)
+            tt(B("b7", 0, I), B("b7", I, CW), B("YD"), A.mult, I)
+            tt(B("OX"), B("b7", 0, I), B("OX"), A.add, I)
+            dma("Y", "yx", "OX", 2.5, False)
+        at(t, "new")
+        MM(SH, B("Tp"), B("TC"), False, True, I)
+        tt(B("S16"), SH, B("QQ"), A.subtract, I)
+        ts(B("OS" if last else "SU"), B("S16"), CEN, None, A.add, None, I, 1 if last else 0.5)
+        at(t, "sw")
+        SW = B("SWH", I * t, I * t + I)
+        if CNT:
+            MM(B(nb, 0, I), B("OB"), B("RS"), True, False, I)
+            MM(B(nb, 0, I), B("OB"), B("RP"), False, True, I)
+            act(SW, B(nb, 0, I), F.Relu, I, scale=-1.0, bias=1.0)
+        else:
+            act(SW, B("b1", I, CW), F.Sigmoid, I, scale=0.1, bias=B("nB", 2, 3))
+        at(t, "e")
         if not last:
-            gathers()
-        for r in range(16):
-            MM(B("b2", 384, 396), slide("W1", r), B("CR", r, I, 16), r == 0, r == 15, al("W1", "CR"), [("b2", 384, 396)], 12)
-        V(tt(B("DP"), B("H7"), B("PF"), A.subtract), al("H7", "PF"), al("DP"), 12)
-        V(tt(B("DQ"), B("DP"), B("b2", 384, 396), A.mult), al("DP") + [("b2", 384, 396)], al("DQ"), 12)
-        V(tt(B("PF"), B("PF"), B("DQ"), A.add), al("PF", "DQ"), al("PF"), 12)
-        if last:
-            V(tt(B("CR"), B("BND"), B("THI"), A.subtract), al("BND", "THI"), al("CR"), I, 2)
-            for r in range(16):
-                MM(B("b2", 384, 396), slide("W1", r), B("CR", r, I, 16), r == 0, r == 15, al("W1", "CR"), [("b2", 384, 396)], 12)
-            def store(dst, src):
-                k = nd[0]
-                nd[0] += 1
-                add("Y", lambda g, T: g.sync.dma_start(T[dst][:], T[src][:]), al(src), [], 2.5, dma=k)
-            store("yf", f1)
-            store("ys", "OS")
-            V(ts(B("MF"), B("b2", 384, 396), PLN / 1024.0, None, A.mult), [("b2", 384, 396)], al("MF"), 12)
-            V(tt(B("YPF"), B("MF"), B("PF"), A.add), al("MF", "PF"), al("YPF"), 12)
-            store("yp", "YPF")
-            for c in range(16):
-                MM(B("b0", 0, I), B("IC", 128 * c, 128 * c + 128), B("X", c, W, 16), c == 0, c == 15, [("IC", 128 * c, 128 * c + 128), ("X",)], [("b0", 0, I)], I)
-            S(act(B("OX"), B("b0", 0, I), F.Copy), [("b0", 0, I)], al("OX"), I)
-            store("yx", "OX")
+            tt(B("b3", 0, I), B("b3", I, CW), SW, A.mult, I)
+            tt(B("E16"), B("b3", 0, I), B("E16"), A.add, I)
+            ts(B("EU"), B("E16"), CEN, None, A.add, None, I, 0.5)
+        at(t, "a")
+        if not last:
+            if ATS:
+                MM(B(nb, I, CW), B("Ib"), B("AT"), True, False, I)
+                MM(B(nb, I, CW), B("Ib"), SW, False, True, I)
+                act(B("AT"), B(nb, I, CW), F.Copy, I)
+            else:
+                tt(B("BND"), B("BND"), SW, A.add, I, 2)
+        else:
+            dma("Y", "yf", f1, 2.5, False)
+            dma("Y", "ys", "OS", 2.5, False)
+            at(t, "yp")
+            for h in range(2):
+                MS([(B("b3", 0, 12), slide("W0", r), B("SWH", I * t + r, I * t + I, 16)) for r in range(8 * h, 8 * h + 8)], h == 0, h == 1, 12)
+            tt(B("PK", 24, 36), B("PK", 12, 24), B("PH", 12 * t, 12 * t + 12), A.add, 12, 2)
+            tt(B("PK", 36, 48), B("b3", 0, 12), B("PK", 24, 36), A.mult, 12)
+            tt(B("YPF"), B("PK", 36, 48), B("YPF"), A.max, 12, 2)
+            dma("Y", "yp", "YPF", 2.5, False)
     return ops
 
 
@@ -400,6 +469,7 @@ def _deps(ops):
     acc = {}
     banks = {}
     sends = {}
+    groups = []
     for i, (q, fn, rd, wr, cost, kw) in enumerate(ops):
         dd, oo = set(), set()
         seen = {}
@@ -414,8 +484,15 @@ def _deps(ops):
                         seen[n] = e
                         dd.update(e["prev"])
                     if q == "T":
-                        if e["cur"] and e["cur"][-1][0] != i:
-                            oo.add(e["cur"][-1][0])
+                        if e["cur"] and e["cur"][-1][0] == i:
+                            continue
+                        if e.get("shut", True):
+                            e["old"], e["grp"] = e.get("grp", []), []
+                            groups.append(e["grp"])
+                        oo.update([j for j in e["grp"] if ops[j][3][0][1] < b and a < ops[j][3][0][2]][:1])
+                        e["grp"].append(i)
+                        e["shut"] = kw["fl"][1]
+                        oo.update(e["old"])
                     else:
                         for (j, c, d, w2) in e["cur"]:
                             if j != i and (w or w2) and c < b and a < d:
@@ -442,27 +519,21 @@ def _deps(ops):
         oo -= dd
         data.append(sorted(dd))
         order.append(sorted(oo))
-    return data, order
+    return data, order, groups
 
 
 def _schedule(ops, data, order):
     n = len(ops)
     succ = [[] for _ in range(n)]
     for i in range(n):
-        for j in data[i] + order[i]:
-            succ[j].append(i)
-    prio = [0.0] * n
-    for i in range(n - 1, -1, -1):
-        prio[i] = ops[i][4] + max([prio[k] + LAT for k in succ[i]], default=0.0)
-    base = list(prio)
-    for i in range(n):
-        if ops[i][3]:
-            w = ops[i][3][0]
-            prio[i] = base[i] + BONUS.get("%s:%s:%d" % (ops[i][0], w[0], w[1]), 0.0)
+        for j in data[i]:
+            succ[j].append((i, LAT))
+        for j in order[i]:
+            succ[j].append((i, 0.0 if ops[i][0] == ops[j][0] else LAT))
+    rank = [(ops[i][5]["due"], i) for i in range(n)]
     left = [len(data[i]) + len(order[i]) for i in range(n)]
     ready = [0.0] * n
-    pool = {}
-    free = {}
+    pool, free = {}, {}
     for i in range(n):
         if left[i] == 0:
             pool.setdefault(ops[i][0], []).append(i)
@@ -470,30 +541,26 @@ def _schedule(ops, data, order):
     while True:
         best = None
         for q, l in pool.items():
-            if not l:
-                continue
-            st = max(free.get(q, 0.0), min(ready[i] for i in l))
-            if best is None or st < best[0]:
-                best = (st, q)
+            if l:
+                st = max(free.get(q, 0.0), min(ready[i] for i in l))
+                if best is None or st < best[0]:
+                    best = (st, q)
         if best is None:
-            break
+            return out
         st, q = best
-        i = max((i for i in pool[q] if ready[i] <= st + 1e-9), key=lambda i: (prio[i], -i))
-        if ops[i][4] > 0.3:
-            i = max((k for k in pool[q] if ready[k] <= st + HOLD), key=lambda i: (prio[i], -i))
+        i = min((k for k in pool[q] if ready[k] <= st + 1e-9), key=lambda k: rank[k])
+        if ops[i][4] > 0.2:
+            i = min((k for k in pool[q] if k == i or (ready[k] <= st + HOLD and ops[k][5]["step"] in HOLDS)), key=lambda k: rank[k])
             st = max(st, ready[i])
         pool[q].remove(i)
-        dma = "dma" in ops[i][5] or q == "R"
         fin = st + ops[i][4]
-        free[q] = st + (0.1 if dma else ops[i][4])
+        free[q] = st + (0.1 if "dma" in ops[i][5] or q == "R" else ops[i][4])
         out.append((i, st, fin))
-        for k in succ[i]:
-            same = ops[k][0] == q and i in order[k]
-            ready[k] = max(ready[k], fin if same else fin + LAT)
+        for k, w in succ[i]:
+            ready[k] = max(ready[k], fin + w)
             left[k] -= 1
             if left[k] == 0:
                 pool.setdefault(ops[k][0], []).append(k)
-    return out
 
 
 _PLAN = {}
@@ -502,42 +569,84 @@ _PLAN = {}
 def _plan():
     if not _PLAN:
         ops = _build()
-        data, order = _deps(ops)
-        _PLAN["ops"], _PLAN["data"], _PLAN["sched"] = ops, data, _schedule(ops, data, order)
+        data, order, groups = _deps(ops)
+        sched = _schedule(ops, data, order)
+        place = {x[0]: k for k, x in enumerate(sched)}
+        ends = {}
+        for grp in groups:
+            begins = ops[grp[0]][5]["fl"][0]
+            grp.sort(key=lambda i: place[i])
+            for i in grp:
+                ops[i][5]["fl"][:] = [begins and i == grp[0], i == grp[-1]]
+            bank = ops[grp[0]][3][0][0]
+            if not begins:
+                ops[ends[bank]][5]["fl"][1] = False
+            ends[bank] = grp[-1]
+        _PLAN["ops"], _PLAN["data"], _PLAN["sched"] = ops, data, sched
     return _PLAN["ops"], _PLAN["data"], _PLAN["sched"]
+
+
+def _helpers(T, topo, core):
+    return [h for h in topo.cores_of(core) if h != core and all(topo.may_write(h, d) for d in T.cores)][:N // 2 - 1]
+
+
+def _transfer(T, topo, dst, engines, t, to, a, n):
+    rid, pnc = topo.addr(dst)[:2]
+    return RemoteDMATransfer(dst_ids=[DstId(rid=rid, pnc=pnc)], dma_engine_mask=sum(1 << e for e in engines), remote_sem=T.sem["arr%d" % t],
+                             src=T["Y%d" % t][:, a:a + n], dst=T[to][:, a:a + n])
+
+
+def _hand_on(g, core, T, topo):
+    home = [c for c in topo.cores_of(core) if T.rank_of(c) is not None]
+    if not HELP or not home or core not in _helpers(T, topo, home[0]):
+        return
+    rank, k = T.rank_of(home[0]), _helpers(T, topo, home[0]).index(core)
+    for t in range(TURNS - 1):
+        p = [p for p in range(N // 2) if p != (-t) % N // 2][k]
+        g.wait_ge(T.sem["arr%d" % t], EN)
+        tr = []
+        for n, b in enumerate((2 * p, 2 * p + 1)):
+            dst = T.cores[(rank + b + t) % N]
+            tr.append(_transfer(T, topo, dst, topo.engines(core, dst)[EN * n:EN * n + EN], t, "L%d" % (t + 1), BLK * b, BLK))
+        g.remote_dma_fused(tr, local_sem=T.sem.sent)
+    g.wait_ge(T.sem.sent, 2 * EN * (TURNS - 1))
 
 
 def rank_program(g, core, T, topo):
     rank = T.rank_of(core)
     if rank is None:
-        return
+        return _hand_on(g, core, T, topo)
     ops, data, sched = _plan()
     eng = {"V": g.vector, "S": g.scalar, "T": g.tensor, "G": g, "Y": g.sync}
     seq, cnt, clock = {}, {}, {}
     know = {q: {} for q in eng}
 
     def send(t):
+        if HELP:
+            own = (-t) % N
+            dst = T.cores[(rank + (own ^ 1) + t) % N]
+            out = topo.engines(core, dst)[:EN]
+            tr = []
+            for k, (h, p) in enumerate(zip(_helpers(T, topo, core), [p for p in range(N // 2) if p != own // 2])):
+                e = [x for x in topo.engines(core, h) if x not in out][EN * k:EN * k + EN]
+                tr.append(_transfer(T, topo, h, e, t, "Y%d" % t, 2 * BLK * p, 2 * BLK))
+            g.remote_dma_fused(tr, local_sem=T.sem.sent)
+            g.remote_dma_fused([_transfer(T, topo, dst, out, t, "L%d" % (t + 1), BLK * (own ^ 1), BLK)], local_sem=T.sem.sent)
+            return EN * (len(tr) + 1)
         tr = []
-        used = 0
         for b in range(N):
-            to = (rank + b + t) % N
-            if to == rank:
-                continue
-            dst = T.cores[to]
-            rid, pnc = topo.addr(dst)[:2]
-            e = topo.engines(core, dst)
-            tr.append(RemoteDMATransfer(dst_ids=[DstId(rid=rid, pnc=pnc)], dma_engine_mask=1 << e[used % len(e)], remote_sem=T.sem["arr%d" % t],
-                                        src=T["Y%d" % t][:, BLK * b:BLK * b + BLK], dst=T["L%d" % (t + 1)][:, BLK * b:BLK * b + BLK]))
-            used += 1
+            dst = T.cores[(rank + b + t) % N]
+            if dst != core:
+                tr.append(_transfer(T, topo, dst, [topo.engines(core, dst)[len(tr)]], t, "L%d" % (t + 1), BLK * b, BLK))
         g.remote_dma_fused(tr, local_sem=T.sem.sent)
-        return used
+        return len(tr)
 
     sent = 0
     dmas = []
     for (i, st, fin) in sched:
         q, fn, rd, wr, cost, kw = ops[i]
         if q == "R":
-            seq[i] = ("arr%d" % kw["arr"], N - 1)
+            seq[i] = ("arr%d" % kw["arr"], (N - 1) * (EN if HELP else 1))
             clock[i] = {}
             continue
         kn = know[q]
@@ -572,8 +681,9 @@ def rank_program(g, core, T, topo):
             clock[i] = dict(kn)
         else:
             s = "q" + q
-            cnt[s] = cnt.get(s, 0) + 1
-            ins.then_inc(T.sem[s], 1)
+            for x in (ins if q == "T" else [ins]):
+                cnt[s] = cnt.get(s, 0) + 1
+                x.then_inc(T.sem[s], 1)
             seq[i] = (s, cnt[s])
             clock[i] = dict(kn)
     g.wait_ge(T.sem.sent, sent)

@@ -8,80 +8,84 @@ I, W, PLN, TURNS, BLK, N = 192, 3072, 2048, 8, 24, 8
 NC = 8
 CW = 2 * I
 PA = 64
-PARTS = (0, 1, 2)
-WAYS = "ttbbbm"
-VCUT = (64, 128)
-VCUT0 = (96,)
-HELP, EN = True, 4
-CNT, ATS = True, True
-RPS, FS, WS = True, True, True
-TR = 0.62
+EN = 4
 CEN = 1536.0
 BIG = 8192.0
 MAGIC = 12582912.0
-MAGIC16 = 201326592.0
+FO = 1280.0
+ROT = 712
 BF, HF, FL, I32, U16 = "bfloat16", "float16", "float32", "int32", "uint16"
-ORDER = ("yx dx1 xs zp rp xe0 dx3 wr new dx2 hash f2 sp3 sz xe2 sp0 pp0 a dx4 mn pp3 own pp5 dz0 sp5 pp4 u m sx pp1 pp2 f cand rs dz1 dx5 zq sp2 wd dx0 "
-         "sp1 sp4 pre sv wp an yp e sw xe1 set").split()
-HOLDS = "rp an dz1 wr sp1 pre sp4 e new set cand sp3 u m dz0 dx5 pp3 rs own xe0 sp0".split()
-D = {_n: float(_k) for _k, _n in enumerate(ORDER)}
+C = dict(
+    ways="ttbbmm",
+    stack=tuple(("VS"[k % 2], 32 * k, 32 * k + 32) for k in range(6)),
+    plan=(("V", 0, 32), ("S", 32, 64), ("S", 64, 128), ("S", 128, 192)),
+    sx=((0, 64), (64, 128), (128, 192)),
+    sq=True, ox="V", t2=True, bm={3: 1, 4: 0},
+    cand="S", tu="V", r2="S", rp="V", su="S", eu="S", f="S", wr="S", h1="V", pu="V",
+    cnt=False, mu2=True,
+    tr=0.62, so=0.15, lat=0.11, hold=0.15, fly=2.5, ga=1.5, sa=3.5,
+    order=("pre pr6 pr7 yx xs0 xs1 xs2 xs3 xs4 xs5 xe0 xe1 xe2 zp mn0 mn1 mn2 mn3 sx0 sx1 sx2 dx0 dz0 dx1 dz1 zq pp0 pp1 dx2 dz2 pp2 dx3 dz3 pp3 dx4 dz4 pp4 "
+           "dx5 dz5 pp5 u h1 h2 h3 sz sv0 sv1 sv2 sv3 r2 sp0 sp1 sp2 sp3 sp4 sp5 cand sc ts wp wc rp f y m es wr set an wd qq sh new su sw ce e eu a own pk yp ex of e0 bs pe pe0 yw s0 pre0 pr60 pr70").split())
+SEQ = """V pk2 xs01 xs41 xs21 e01 yx1 e02 xe01 mn12 h11 mn21 mn31 mn11 mn01 mn22 h12 mn02 dx31 dx21 mn32 pp41 h31 pp51 h32 pk1 r21 set1 rp1 pk3 ts1 bs1 pk4 rp2 pk5 rp3 pk6 wd1 yp1 wd2 y1 yp2 y2 pk7 qq1 e1 pk9 new1 ex1 yp3 pk8 e2 m1 ex2 m2 wr1 ex3 ex4 yp4 ex5 pk10 ex6 yp5 ; cV c1 c4 c5 c7 c18 c8 c6 c3 c10 c2 c11 c19 c17 c16 c12 c14 c20 c22 c9 c13 c21 c15 ; S s01 xs11 s02 xs51 xs31 xe01 xe21 xe11 pp11 h21 pp31 r21 cand1 s03 an1 f1 sw1 of1 y1 a1 own1 wr1 eu1 su1 yp1 ; cS c3 c4 c1 c6 c5 c2 ; T pre03 yx1 pre01 yx3 pre04 pre02 yx2 sx01 sx04 sx02 sx03 yx4 pre05 sx24 sx21 sx23 sx22 u1 sx12 zp1 pr702 u2 zq1 sx14 dx01 sz2 dz01 sx11 pr701 pr601 sv21 dx11 sz3 dz11 sv11 sv12 sz1 sx13 sv22 sv01 pe02 sv02 pe01 sv31 dx51 dx41 sp11 sv32 sp01 pr602 sp41 sp21 sp31 sp51 wp1 wp2 ts1 wc1 an2 rp2 rp1 an1 an3 ce3 yw1 ce4 ce1 ce2 yw2 y1 y2 yw4 a1 sh1 es2 qq1 new1 es1 a2 sh2 yp1 +pre5 ex1 +pr62 m2 m1 wr1 +pre2 +pr72 +pre7 yw7 +pr71 yw5 +pr61 +pe1 +pe2 +pre3 yp2 yw6 yw3 +pre4 +pre1 yw8 +pre6 ; cT  ; cG c1 c2 c3 c14 c4 c15 c7 c18 c5 c6 c17 c11 c16 c13 c8 c21 c12 c10 c9 c20 c19"""
 
 SCRATCH = {}
 for _n, _w, _d in [
         ("X", W, BF), ("XS", W, BF), ("XE", W, BF), ("MN", W, HF), ("MX", W, BF),
-        ("PLT", PLN, I32), ("SI", I, I32), ("THI", I, I32), ("PI", 12, I32),
-        ("S16", I, HF), ("E16", I, HF), ("CAND", I, HF), ("TH16", I, HF), ("BND", I, HF), ("AT", I, BF), ("SWH", TURNS * I, BF),
+        ("PLT", PLN + ROT, I32), ("SI", I, I32), ("THI", I, I32), ("PI", 12, I32),
+        ("S16", I, HF), ("E16", I, HF), ("CAND", I, HF), ("BND", I, HF), ("AT", I, BF), ("SWH", TURNS * I, BF),
         ("SU", I, U16), ("EU", I, U16), ("TU", 12, U16), ("PU", 12, U16), ("MU", 12, U16),
-        ("R2", I, I32), ("RS", I, BF), ("RP", I, BF), ("AN", 2 * I, BF), ("SET", I, BF), ("WD", I, FL), ("QQ", I, FL),
+        ("R2", I, I32), ("RS", I, BF), ("RP", I, BF), ("AN", 2 * I, BF), ("SET", I, BF), ("QQ", I, FL),
         ("TS", I, HF), ("TP", I, HF), ("TC", I, HF),
-        ("FA", I, BF), ("FB", I, BF), ("YD", I, BF), ("WR", I, BF), ("QF", 12, FL), ("QB", 12, HF),
+        ("F0", I, BF), ("FA", I, HF), ("FB", I, HF), ("YD", I, FL), ("WR", I, I32), ("QF", 12, FL), ("QB", 12, HF),
         ("HH", 48, I32), ("PH", 12 * TURNS, I32),
         ("KT", 12 * TURNS, FL), ("PK", 12 * TURNS, FL), ("KK", 180, FL),
-        ("K0", 12, I32), ("PE", 12, I32), ("YPF", 12, FL), ("OS", I, FL), ("OX", I, FL),
-        ("ip", 1, I32), ("ig", 1, I32), ("r4", 128, BF), ("ibase", 12, I32),
-        ("pf", 1, FL), ("gf", 1, FL), ("g16", 1, FL), ("g15", 1, FL), ("lf", 1, FL), ("l21", 1, FL), ("l0", 1, FL),
-        ("r16", 1, FL), ("nB", 5, FL), ("row", 144, FL), ("grow", 128, FL), ("base", 12, FL),
-        ("cv", I, BF), ("FM", I, FL), ("WM", I, FL),
+        ("K0", 12, I32), ("PE", 12, I32), ("YPF", 12, FL), ("OS", I, FL), ("OX", I + 12 * TURNS, FL), ("YX", I, FL),
+        ("ip", 1, I32), ("ig", 1, I32), ("il", 1, I32), ("ibase", 12, I32), ("gf", 1, FL), ("g15", 1, FL), ("l21", 1, FL),
+        ("r16", 1, FL), ("row", 144, FL), ("grow", 128, FL), ("base", 12, FL),
+        ("cv", CW, BF), ("FM", I, FL), ("c24", 12, BF), ("zero", 128, BF), ("NT", 128, BF),
         ("W1", 144, BF), ("W2", 144, BF), ("Wm", 144, BF), ("Wmh", 144, BF), ("Wu", 144, BF), ("W0", 144, BF),
-        ("Ib", 128, BF), ("Im", 128, BF), ("Ihf", 128, BF), ("I32", 128, BF), ("I64m", 128, BF),
-        ("OB", 128, BF), ("OBh", 128, BF), ("OBB", 128, BF), ("OBm", 128, BF), ("DE", 2048, BF),
-        ("Ls", 128, BF), ("BIL", 128, BF), ("Sh", 128, BF), ("Ihm", 128, BF),
-        ("ShI", 128, BF), ("Ihq", 128, HF), ("R16", I, HF), ("Tp", 128, BF), ("Tp0", 128, BF),
-        ("cq", CW, BF), ("cz", CW, HF), ("ct", I, BF), ("cb", CW, BF), ("IC0", 512, BF), ("IC", 16 * 128, BF)]:
+        ("Ib", 128, BF), ("Im", 128, BF), ("Ih", 128, BF), ("I32", 128, BF), ("I64m", 128, BF),
+        ("OB", 128, BF), ("OBh", 128, BF), ("OBB", 128, BF), ("OBm", 128, BF), ("DE", W, BF),
+        ("Ls", 128, BF), ("BIL", 128, BF), ("Sh", 128, BF),
+        ("ShI", 128, BF), ("R16", I, HF), ("Tp", 128, BF), ("Tp0", 128, BF),
+        ("cz", CW, HF), ("ct", I, BF), ("cb", I, BF), ("IC0", 512, BF), ("IC", 16 * 128, BF)]:
     SCRATCH[_n] = ("sbuf", [128, _w], _d)
 for _t in range(8):
     SCRATCH["L%d" % _t] = ("sbuf", [128, I], BF)
     SCRATCH["Y%d" % _t] = ("sbuf", [128, I], BF)
-for _t in range(8):
+for _t in (0, 1, 2, 3, 6, 7):
     SCRATCH["b%d" % _t] = ("psum", [128, 512], FL)
-NDMA = 12
+SCRATCH["b45"] = ("psum", [128, 1024], FL)
+NDMA = 13
 SEMAPHORES = ["qV", "qS", "qT", "qG", "sent"] + ["arr%d" % t for t in range(8)] + ["dm%d" % k for k in range(NDMA)]
-
-LAT, HOLD, FLY = 0.11, 0.15, 3.5
-TO, VS = 0.0, 1.0
-GA = 1.5
 
 
 def _build():
     ops = []
     CY = 0.00083
+    GA = C["ga"]
+    WAYS = C["ways"]
+    D = {n: float(k) for k, n in enumerate(C["order"])}
     now = [0.0, ""]
 
     def add(q, fn, rd, wr, cost, **kw):
-        ops.append([q, fn, [r for r in rd if r], [r for r in wr if r], cost * (VS if q in "VS" and not kw else 1.0), dict(kw, due=now[0], step=now[1])])
+        ops.append([q, fn, [r for r in rd if r], [r for r in wr if r], cost, dict(kw, due=now[0], step=now[1])])
 
     def at(t, step):
         now[:] = [100.0 * (t + 1) + D[step], step]
 
     def B(name, a=None, b=None, st=None):
+        if name in ("b4", "b5"):
+            a, b, o = a or 0, b or 512, 512 * (name == "b5")
+            return (lambda T: T.b45[:, o + a:o + b:st or 1]), (name, a, b)
         if a is None:
             return (lambda T: T[name][:]), (name, 0, 1 << 20)
         if st is None:
             return (lambda T: T[name][:, a:b]), (name, a, b)
         return (lambda T: T[name][:, a:b:st]), (name, a, b)
 
-    def IX(win, off, a, b):
-        return (lambda T: T[win][:, :].indirect(T[off][:, a:b])), (win, 0, 1 << 20), (off, a, b)
+    def IX(win, off, a, b, c=0, d=W):
+        return (lambda T: T[win][:, c:d].indirect(T[off][:, a:b])), (win, c, d), (off, a, b)
 
     def slide(name, k):
         return (lambda T: T[name][:, 15 - k:15 - k + 128]), (name, 0, 1 << 20)
@@ -101,7 +105,7 @@ def _build():
     def MS(mm, start, stop, n):
         fl = [start, stop]
         add("T", lambda g, T: [g.tensor.matmul(o[0](T), w[0](T), r[0](T), fl[0] and k == 0, fl[1] and k == len(mm) - 1) for k, (o, w, r) in enumerate(mm)],
-            [x for o, w, r in mm for x in regs(w, r)], [x for o, w, r in mm for x in regs(o)], len(mm) * (max(64, n) * CY * TR + TO), fl=fl)
+            [x for o, w, r in mm for x in regs(w, r)], [x for o, w, r in mm for x in regs(o)], len(mm) * max(64, n) * CY * C["tr"], fl=fl)
 
     def tt(o, a, b, op, n, f=1.0):
         add("V", lambda g, T: g.vector.tensor_tensor(o[0](T), a[0](T), b[0](T), op), regs(a, b), regs(o), vcost(n, f))
@@ -121,7 +125,18 @@ def _build():
 
     def act(o, a, f, n, fc=1.0, **kw):
         add("S", lambda g, T: g.scalar.activation(o[0](T), a[0](T), f, **{k: val(v, T) for k, v in kw.items()}),
-            regs(a, *kw.values()), regs(o), (0.065 if len(a) > 2 else 0.15) + n * fc * CY)
+            regs(a, *kw.values()), regs(o), (0.065 if len(a) > 2 else C["so"]) + n * fc * CY)
+
+    def plus(q, o, a, c, n, f=1.0):
+        if q == "V":
+            if c:
+                ts(o, a, c, None, A.add, None, n, f)
+            else:
+                tc(o, a, n, f)
+        elif c:
+            act(o, a, F.Identity, n, max(f, 1.0), bias=c)
+        else:
+            act(o, a, F.Copy, n, max(f, 1.0))
 
     def tiny(out, w, src, first, last, n=12, width=I):
         for h in range(2):
@@ -135,73 +150,66 @@ def _build():
         add(q, lambda g, T: (g.sync if q == "Y" else g.scalar).dma_start(T[dst][:], T[src][:]),
             [] if load else [(src, 0, 1 << 20)], [(dst, 0, 1 << 20)] if load else [], cost, dma=k)
 
-    dma("Y", "X", "x0", 4.0, True)
+    dma("Y", "X", "x0", 3.5, True)
     dma("S", "SI", "s0", 2.5, True)
     dma("S", "L0", "z0", 3.0, True)
     dma("S", "PI", "p0", 3.0, True)
-    dma("Y", "PLT", "pl", 6.0, True)
+    for a, b, c, cost in ((ROT, ROT + PLN, 0, 5.5), (0, ROT, PLN - ROT, 6.5)):
+        nd[0] += 1
+        add("Y", lambda g, T, a=a, b=b, c=c: g.sync.dma_start(T.PLT[:, a:b], T.pl[:, c:c + b - a]), [], [("PLT", a, b)], cost, dma=nd[0] - 1)
     dma("S", "THI", "th", 4.0, True)
-    dma("S", "FA", "f0", 4.0, True)
+    dma("S", "F0", "f0", 4.0, True)
 
     def G(fn, rd, wr, n):
         add("G", fn, regs(*rd), regs(wr), 0.15 + 2 * n * CY)
     G(lambda g, T: g.iota(T.ip[:], [[0, 1]], 0, 1), [], B("ip"), 1)
-    G(lambda g, T: g.iota(T.r4[:], [[0, 32], [1, 4]], 0, 0, allow_small_or_imprecise_dtypes=True), [], B("r4"), 128)
     G(lambda g, T: g.iota(T.row[:], [[1, 144]], 0, 0, allow_small_or_imprecise_dtypes=True), [], B("row"), 144)
     G(lambda g, T: g.iota(T.grow[:], [[1, 8], [0, 16]], 0, 0, allow_small_or_imprecise_dtypes=True), [], B("grow"), 128)
-    G(lambda g, T: g.iota(T.ibase[:], [[-256, 12]], 0, 0), [], B("ibase"), 12)
-    R128 = B("row", 0, 128)
+    fill(B("cv"), -11.0 / 512, CW)
+    fill(B("zero"), 0.0, 128)
+    act(B("AT"), B("cv", 0, I), F.Sigmoid, I, 9.0, scale=30000.0)
+    ts(B("cz"), B("cv"), 0.0, -127.9375, A.mult, A.add, CW, 0.5)
     ts(B("ig"), B("ip"), 4, None, A.arith_shift_right, None, 1)
-    tc(B("pf"), B("ip"), 1)
+    ts(B("il"), B("ip"), 15, None, A.bitwise_and, None, 1)
     tc(B("gf"), B("ig"), 1)
-    ts(B("g16"), B("gf"), 16.0, None, A.mult, None, 1)
-    ts(B("g15"), B("gf"), 16.0, 15.0, A.mult, A.add, 1)
-    tt(B("lf"), B("pf"), B("g16"), A.subtract, 1)
-    ts(B("l21"), B("lf"), 2.0, 1.0, A.mult, A.add, 1)
-    ts(B("l0"), B("lf"), 0.0, None, A.is_equal, None, 1)
+    ts(B("g15"), B("ig"), 16.0, 15.0, A.mult, A.add, 1)
+    ts(B("l21"), B("il"), 2.0, 1.0, A.mult, A.add, 1)
+    ts(B("r16"), B("il"), -16.0, -7.5, A.mult, A.add, 1)
     ts(B("W1"), B("row"), B("g15"), None, A.is_equal, None, 144)
-    ts(B("Wu"), B("W1"), B("l21"), None, A.mult, None, 144, 0.5)
-    ts(B("Ib"), R128, B("pf"), None, A.is_equal, None, 128)
     ts(B("OB"), B("grow"), B("gf"), None, A.is_equal, None, 128)
-    for dst, src, c, n in (("Wmh", "W1", -0.5, 144), ("Wm", "W1", -1.0, 144), ("Im", "Ib", -1.0, 128),
-                           ("I32", "Ib", 32.0, 128), ("I64m", "Ib", -64.0, 128), ("OBh", "OB", 0.5, 128),
-                           ("OBB", "OB", -BIG, 128), ("W2", "W1", 2.0, 144)):
-        act(B(dst), B(src), F.Copy, n, scale=c)
+    for dst, src, c, n in (("Wmh", "W1", -0.5, 144), ("OBh", "OB", 0.5, 128), ("Wu", "W1", B("l21"), 144), ("Wm", "W1", -1.0, 144),
+                           ("W2", "W1", 2.0, 144), ("OBB", "OB", -BIG, 128)):
+        ts(B(dst), B(src), c, None, A.mult, None, n, 0.5)
     if "m" in WAYS:
-        now[0] = -2.0
-        act(B("r4"), B("r4"), F.Sigmoid, 128, 12.0, scale=1000.0, bias=500.0 - 1000.0 * WAYS[2:].index("m"))
-        now[0] = 0.0
-        ts(B("r4"), B("r4"), -1.0, None, A.mult, None, 128, 0.5)
-        tt(B("OBm"), B("r4"), B("OB"), A.mult, 128, 2)
+        fill(B("OBm"), 0.0, 128)
+        for k in range(4):
+            if WAYS[2 + k] == "m":
+                ts(B("OBm", k, 128, 4), B("OB", k, 128, 4), -1.0, None, A.mult, None, 32, 0.5)
 
-    def sel(dst, src, pat, op, fill_, base, cm):
-        G(lambda g, T: g.affine_select(T[dst][:], T[src][:], pat, op, fill_, base, cm), [B(src)], B(dst), 128)
-    col = [[1, 128]]
-    sel("Ls", "OB", col, A.is_gt, 0.0, 0, -1)
+    def sel(dst, src, pat, op, fill_, base, cm, n=128):
+        G(lambda g, T: g.affine_select(T[dst][:], T[src][:], pat, op, fill_, base, cm), [B(src)], B(dst), n)
+
+    def const(dst, c, n):
+        G(lambda g, T: g.iota(T[dst][:], [[0, n]], int(c), 0, allow_small_or_imprecise_dtypes=True), [], B(dst), n)
+    col, first = [[1, 128]], [[0, 8], [1, 16]]
+    for x, c in (("Ib", 1.0), ("I32", 32.0), ("I64m", -64.0), ("Ih", 0.5), ("Im", -1.0)):
+        sel(x, "zero", col, A.not_equal, c, 0, -1)
+    const("cb", -BIG, I)
+    sel("NT", "Ih", first, A.not_equal, 0.0, 0, 0)
     sel("BIL", "OBB", col, A.is_gt, 0.0, 0, -1)
     sel("BIL", "BIL", col, A.not_equal, BIG, 0, -1)
+    sel("Tp0", "Ib", first, A.is_equal, 0.0, 0, 0)
+    sel("Ls", "OB", col, A.is_gt, 0.0, 0, -1)
     sel("Sh", "OB", col, A.is_equal, 0.0, -1, -1)
     sel("ShI", "Sh", col, A.not_equal, -1.0, 0, -1)
-    for x, y in (("Tp0", "Ib"), ("Tp", "OB")):
-        sel(x, y, [[0, 8], [1, 16]], A.is_equal, 0.0, 0, 0)
-    G(lambda g, T: g.iota(T.cb[:, 0:I], [[0, I]], -int(BIG), 0, allow_small_or_imprecise_dtypes=True), [], B("cb", 0, I), I)
-    G(lambda g, T: g.iota(T.ct[:], [[0, I]], int(15 * CEN), 0, allow_small_or_imprecise_dtypes=True), [], B("ct"), I)
-    fill(B("cq"), -0.5, CW)
-    ts(B("cz"), B("cq"), 0.0, -127.9375, A.mult, A.add, CW, 0.5)
-    ts(B("Ihq"), B("Ib"), 0.5 - 2.0 ** -11, None, A.mult, None, 128, 0.5)
-    ts(B("nB", 3, 4), B("lf"), 1.0, 0.28125, A.is_equal, A.mult, 1)
-    ts(B("nB", 4, 5), B("l0"), -2048.0, B("nB", 3, 4), A.mult, A.add, 1)
-    ts(B("cv"), B("cq", 0, I), 0.0, B("nB", 4, 5), A.mult, A.add, I, 0.5)
-    ts(B("nB", 1, 2), B("l0"), -1.0, BIG, A.add, A.mult, 1)
-    ts(B("cb", I, CW), B("cq", 0, I), 0.0, B("nB", 1, 2), A.mult, A.add, I, 0.5)
-    ts(B("W0"), B("W1"), B("l0"), None, A.mult, None, 144, 0.5)
-    if not CNT:
-        ts(B("nB", 2, 3), B("l0"), -0.1 * BIG, 0.15 * BIG, A.mult, A.add, 1)
-    ts(B("r16"), B("lf"), -16.0, 24568.5, A.mult, A.add, 1)
-    ts(B("base"), B("ibase"), B("r16"), None, A.add, None, 12)
+    sel("Tp", "OB", first, A.is_equal, 0.0, 0, 0)
+    const("ct", 15 * CEN, I)
+    const("c24", 16 * CEN, 12)
+    G(lambda g, T: g.iota(T.ibase[:], [[-256, 12]], 0, 0), [], B("ibase"), 12)
+    sel("W0", "W1", [[-16, 9], [0, 16]], A.is_equal, 0.0, 0, 1, 144)
 
     def late():
-        G(lambda g, T: g.iota(T.KT[:], [[PLN, TURNS], [0, 12]], PLN, 0, allow_small_or_imprecise_dtypes=True), [B("Y0")], B("KT"), 96)
+        G(lambda g, T: g.iota(T.KT[:], [[PLN, TURNS], [0, 12]], 2 * PLN - ROT, 0, allow_small_or_imprecise_dtypes=True), [B("Y0")], B("KT"), 96)
         for h in range(4):
             o = 512 * h
             G(lambda g, T, h=h: g.iota(T.IC0[:], [[1, 4], [0, 128]], 1 + 4 * h, 0, allow_small_or_imprecise_dtypes=True), [B("Y0")], B("IC0"), 512)
@@ -210,101 +218,97 @@ def _build():
     now[0] = -1.0
     tc(B("PU"), B("PI"), 12)
     tc(B("SU"), B("SI"), I)
-    ts(B("E16"), IX("PLT", "PU", 0, 12), -CEN, None, A.add, None, I, GA)
+    at(0, "s0")
+    plus("S", B("S16"), B("SI"), -CEN, I)
+    act(B("BND"), B("THI"), F.Identity, I, scale=1.0 / 64, bias=-32.0)
+    plus("S", B("FA"), B("F0"), FO, I)
+    at(0, "e0")
+    ts(B("E16"), IX("PLT", "PU", 0, 12, ROT, ROT + PLN), -CEN, None, A.add, None, I, GA)
     ts(B("EU"), B("E16"), CEN, None, A.add, None, I, 0.5)
-    ts(B("S16"), B("SI"), -CEN, None, A.add, None, I)
-    ts(B("BND"), B("THI"), -2048.0, 1.0 / 64, A.add, A.mult, I)
-    now[0] = 0.0
-    if ATS:
-        fill(B("AT"), 0.0, I)
-    else:
-        ts(B("TH16"), B("THI"), -2048.0, 1.0 / 64, A.add, A.mult, I)
+    at(0, "bs")
+    ts(B("base"), B("ibase"), B("r16"), None, A.add, None, 12)
 
     for t in range(TURNS):
         L, Y = "L%d" % t, "Y%d" % t
         f0, f1 = ("FA", "FB") if t % 2 == 0 else ("FB", "FA")
         last = t == TURNS - 1
-        H, VL, UP = ("b2", 0), ("b2", I), ("b3", 0)
+        nb, cb = ("b4", "b5") if WAYS.count("t") % 2 == 0 else ("b5", "b4")
+        H, VL, UP, PC, WC, SC, FS, ES, CE = ("b2", 0), ("b2", I), ("b3", 0), ("b6", 0), ("b6", I), ("b7", 0), ("b1", 0), ("b7", I), ("b1", I)
 
         def P(reg, a=0, b=I, st=None):
             return B(reg[0], reg[1] + a, reg[1] + b, st)
-        vc = VCUT if t else VCUT0
-        cuts = [0] + list(vc) + ([I] if vc[-1] < I else [])
-        at(t, "xs")
-        for a, b in zip(cuts[:-1], cuts[1:]):
-            if b <= vc[-1]:
-                ts(B("XS", 16 * a, 16 * b), IX("X", "SU", a, b), -128.0, None, A.add, None, 16 * (b - a), GA)
-            else:
-                act(B("XS", 16 * a, W), IX("X", "SU", a, I), F.Identity, 16 * (I - a), GA, bias=-128.0)
-        for c in PARTS:
-            at(t, "xe%d" % c)
-            if t == 0 and c == PARTS[-1]:
-                tc(B("XE", 16 * PA * c, 16 * PA * (c + 1)), IX("X", "EU", PA * c, PA * (c + 1)), 16 * PA, GA)
-            else:
-                act(B("XE", 16 * PA * c, 16 * PA * (c + 1)), IX("X", "EU", PA * c, PA * (c + 1)), F.Copy, 16 * PA, GA)
-        at(t, "pre")
+        cuts = C["stack"]
+        for k, (q, a, b) in enumerate(cuts):
+            at(t, "xs%d" % k)
+            plus(q, B("XS", 16 * a, 16 * b), IX("X", "SU", a, b), -128.0, 16 * (b - a), GA)
+        for q, a, b in C["plan"]:
+            at(t, "xe%d" % (a // PA))
+            plus(q, B("XE", 16 * a, 16 * b), IX("X", "EU", a, b), 0.0, 16 * (b - a), GA)
+        at(t, "pre" if t else "pre0")
         MM(B("b0", 0, CW), B("Ib"), B("cz"), True, False, CW)
         MM(P(H), B("I32"), B("BND"), True, False, I)
-        MM(P(VL), B("OB"), B("cv"), False, False, I)
+        MM(P(VL), B("OB"), B("cz", 0, I), False, False, I)
+        MM(P(VL), B("I32"), B("cv", 0, I), False, False, I)
         MM(P(UP), B("I64m"), B("BND"), True, False, I)
-        if ATS and t:
+        if t:
             MM(P(H), B("I32"), B("AT"), False, False, I)
             MM(P(UP), B("I64m"), B("AT"), False, False, I)
-        if not last:
-            MM(B("b3", I, CW), B("Im"), B("E16"), False, False, I)
+        at(t, "pr6" if t else "pr60")
+        MM(P(PC), B("Ib"), B("cb"), True, False, I)
+        MM(P(WC), B("NT"), B("cb"), False, False, I)
+        at(t, "pr7" if t else "pr70")
+        MM(P(SC), B("Ib"), B("S16"), True, False, I)
+        MM(P(ES), B("Im"), B("S16"), False, False, I)
+        at(t, "pe" if t else "pe0")
+        MM(P(PC), B("Ib"), B("E16"), False, False, I)
+        MM(P(ES), B("Ib"), B("E16"), False, False, I)
         if last:
             at(t, "yx")
-            for h in range(4):
-                MS([(B("b1", 0, I), B("IC", 128 * c, 128 * c + 128), B("X", c, W, 16)) for c in range(4 * h, 4 * h + 4)], h == 0, False, I)
             n = 12 * t
-            tiny(B("b1", 256, 256 + n), "W0", "SWH", False, False, n, t * I)
-            if not ATS:
-                tt(B("TH16"), B("BND"), B("TH16"), A.subtract, I, 2)
-            tiny(B("b1", 384, 396), "W0", "AT" if ATS else "TH16", False, True)
-            tc(B("OX"), B("b1", 0, I), I)
+            tiny(B("b1", 0, n), "W0", "SWH", True, False, n, t * I)
+            tiny(B("b1", n, n + 12), "W0", "AT", False, True)
+            plus(C["ox"], B("OX", 0, n + 12), B("b1", 0, n + 12), 0.0, n + 12)
+            at(t, "pk")
             tt(B("PK", 0, n), B("PH", 0, n), B("KT", 0, n), A.add, n, 2)
             tc(B("KK", 84, 96), B("PI"), 12)
-            tt(B("KK", 0, n), B("b1", 256, 256 + n), B("PK", 0, n), A.mult, n)
-            tc(B("PE"), B("b1", 384, 396), 12)
-            ts(B("PK", 0, 12), B("PE"), float(PLN), None, A.mult, None, 12)
+            tt(B("KK", 0, n), B("OX", 0, n), B("PK", 0, n), A.mult, n, 2)
+            ts(B("PK", 0, 12), B("OX", n, n + 12), float(PLN), None, A.mult, None, 12)
             for a, w in ((0, 48), (96, 24)):
                 tt(B("KK", a + 2 * w, a + 3 * w), B("KK", a, a + w), B("KK", a + w, a + 2 * w), A.max, w, 2)
             tt(B("K0"), B("KK", 144, 156), B("KK", 156, 168), A.max, 12, 2)
             ts(B("PE"), B("K0"), PLN - 1, None, A.bitwise_and, None, 12)
             ts(B("PK", 12, 24), B("PK", 0, 12), float(PLN), None, A.add, None, 12)
             tt(B("YPF"), B("PK", 0, 12), B("PE"), A.add, 12)
-        at(t, "sx")
-        for a, b in zip(cuts[:-1], cuts[1:]):
+        for c, (a, b) in enumerate(C["sx"]):
+            at(t, "sx%d" % c)
             for h in range(4):
                 MS([(P(H, a, b), slide("Wmh", k), B("XS", 16 * a + k, 16 * b, 16)) for k in range(4 * h, 4 * h + 4)], False, False, b - a)
         at(t, "zp")
         MS([(B("b0", m, CW, 2), B("Ib"), B(L)) for m in range(2)], False, True, I)
-        at(t, "pre")
-        MM(B("b7", 256, 256 + I), B("Ihq"), B(f0), True, False, I)
-        MM(B("b7", 48, 48 + I), B("Im"), B("S16"), False, False, I)
-        MM(B("b7", 48, 48 + I), B("Ib"), B("E16"), False, False, I)
         at(t, "u")
-        MM(B("b7", 256, 256 + I), B("Ihq"), B(L), False, False, I)
-        tiny(B("b7", 0, 12), "Wu", L, False, True)
+        tiny(B("b5", 0, 12), "Wu", L, True, True)
         at(t, "sz")
         MM(P(H), B("OBh"), B(L), False, False, I)
         MM(P(VL), B("OB"), B(L), False, False, I)
-        at(t, "hash")
+        at(t, "h1")
         H1, H2, H3, H4 = [B("HH", 12 * k, 12 * k + 12) for k in range(4)]
-        tc(H1, B("b7", 0, 12), 12)
+        plus(C["h1"], H1, B("b5", 0, 12), 0.0, 12)
         ts(H2, H1, 4095, None, A.bitwise_and, None, 12)
-        ts(H3, H2, 1184.0, None, A.add, None, 12)
-        tt(H4, H2, H3, A.mult, 12)
+        at(t, "h2")
+        if C["sq"]:
+            act(H4, H2, F.Square, 12, bias=592.0)
+        else:
+            ts(H3, H2, 592.0, None, A.add, None, 12)
+            tt(H4, H3, H3, A.mult, 12)
+        at(t, "h3")
         ts(B("PH", 12 * t, 12 * t + 12), H4, 5, PLN - 1, A.arith_shift_right, A.bitwise_and, 12)
-        tc(B("PU"), B("PH", 12 * t, 12 * t + 12), 12)
+        plus(C["pu"], B("PU"), B("PH", 12 * t, 12 * t + 12), 0.0, 12)
         at(t, "cand")
-        ts(B("CAND"), IX("PLT", "PU", 0, 12), -CEN, None, A.add, None, I, GA)
-        if not last:
-            MM(B("b3", I, CW), B("Ib"), B("CAND"), False, False, I)
+        plus(C["cand"], B("CAND"), IX("PLT", "PU", 0, 12, 0, PLN), -CEN, I, GA)
         for q in range(NC):
-            at(t, "mn")
+            at(t, "mn%d" % (q // 2))
             tt(B("MN", CW * q, CW * q + CW), B("XS", q, W, NC), B("b0", 0, CW), A.min, CW)
-            at(t, "sv")
+            at(t, "sv%d" % (q // 2))
             MS([(P(VL), slide("Wm", q + NC * m), B("MN", CW * q + m, CW * q + CW, 2)) for m in range(2)], False, q == NC - 1, I)
         sums = []
         slow = [x for x in WAYS if x == "t"]
@@ -313,6 +317,7 @@ def _build():
             at(t, "zq")
             MS([(B("b1", m, 512, 4), B("Ib"), B(L, PA, I)) for m in range(4)], True, True, I - PA)
         if "m" in WAYS:
+            at(t, "sz")
             MM(P(UP, PA, I), B("OBm"), B(L, PA, I), False, False, I - PA)
         for n, way in enumerate(WAYS):
             a, b, st, h = (0, PA, 2, n) if n < 2 else (PA, I, 4, n - 2)
@@ -326,7 +331,11 @@ def _build():
                 at(t, "dz%d" % n)
                 MS([(B(bk, m, 512, d), B("Im"), B(L, a, b)) for m in range(d)], False, True, b - a)
                 at(t, "pp%d" % n)
-                act(mx, B(bk), F.Abs, 512)
+                if n > 1 or not C["t2"]:
+                    act(mx, B(bk), F.Abs, 512)
+                elif n == 1:
+                    add("S", lambda g, T: g.scalar.activation(T.MX[:, 0:1024], T.b45[:], F.Abs), regs(B("b4"), B("b5")), regs(B("MX", 0, 1024)),
+                        C["so"] + 1024 * CY)
             elif way == "m":
                 at(t, "dx%d" % n)
                 MS([(P(UP, a, b), slide("Wm", st * m + h), B("XE", 16 * a + st * m + h, 16 * b, 16)) for m in range(d)], False, False, b - a)
@@ -334,133 +343,147 @@ def _build():
                 tt(mx, xe, B("b1"), A.max, 512)
             else:
                 at(t, "dx%d" % n)
-                tt(B("DE", o - 1024, o - 512), xe, B("b1"), A.subtract, 512)
+                tt(B("DE", o, o + 512), xe, B("b1"), A.subtract, 512)
                 at(t, "pp%d" % n)
-                act(mx, B("DE", o - 1024, o - 512), F.Abs, 512)
+                if n in C["bm"]:
+                    p = o - 512 * C["bm"][n]
+                    act(B("MX", p, o + 512), B("DE", p, o + 512), F.Abs, o + 512 - p)
             sums.append(([(P(UP, a, b), slide("W2" if way == "m" else "W1", st * m + h), B("MX", o + m, o + 512, d)) for m in range(d)], "sp%d" % n, b - a))
         for n, (mm, step, w) in enumerate(sums):
             at(t, step)
             MS(mm, False, n == len(sums) - 1, w)
-        at(t, "rs")
-        ts(B("R2"), P(VL), -0.65625, 0.1875, A.max, A.add, I)
+        at(t, "r2")
+        if C["r2"] == "S":
+            act(B("R2"), P(VL), F.Relu, I, bias=0.15625)
+        else:
+            ts(B("R2"), P(VL), 0.15625, 0.0, A.add, A.max, I)
         tt(B("RS"), P(H), B("R2"), A.is_gt, I)
         at(t, "set")
         tt(B("SET"), P(VL), B("R2"), A.is_le, I)
-        at(t, "pre")
-        MM(B("b6", 0, I), B("Ib"), B("S16"), True, False, I)
-        at(t, "rs")
-        MM(B("b6", 0, I), B("BIL"), B("RS"), False, True, I)
-        ts(B("TS"), B("b6", 0, I), -BIG, -CEN, A.add, A.max, I)
-        at(t, "f")
-        if FS:
-            act(B("FM"), B("b7", 256, 256 + I), F.Identity, I, bias=MAGIC)
-            at(t, "f2")
-            act(B(f1), B("FM"), F.Identity, I, bias=-MAGIC)
-        else:
-            ts(B(f1), B("b7", 256, 256 + I), MAGIC, MAGIC, A.add, A.subtract, I)
+        at(t, "ts")
+        MM(P(SC), B("BIL"), B("RS"), False, True, I)
+        ts(B("TS"), P(SC), -BIG, -CEN, A.add, A.max, I)
+        at(t, "wp")
+        MM(P(WC), B("OBB"), B("RS"), False, False, I)
+        MM(P(PC), B("OBB"), B("RS"), False, False, I)
         at(t, "an")
         MM(B("b0", 0, I), B("Ls"), B("RS"), True, False, I)
         MM(B("b0", I, CW), B("OBh"), B("RS"), False, False, I)
         MM(B("b0", I, CW), B("I64m"), B("SET"), False, True, I)
         act(B("AN"), B("b0", 0, CW), F.Sigmoid, CW, scale=1000.0, bias=-250.0)
         at(t, "wd")
-        tt(B("b7", 48, 48 + I), B("b7", 48, 48 + I), B("AN", I, CW), A.mult, I)
-        tt(B("R16"), B("b7", 48, 48 + I), B("S16"), A.add, I)
-        MM(B("b6", 0, I), B("ShI"), B("R16"), True, True, I)
-        tt(B("QQ"), B("b6", 0, I), B("AN", 0, I), A.mult, I)
+        tt(P(ES), P(ES), B("AN", I, CW), A.mult, I)
+        tt(B("R16"), P(ES), B("S16"), A.add, I)
+        at(t, "qq")
+        MM(B("b7", 0, I), B("ShI"), B("R16"), True, True, I)
+        tt(B("QQ"), B("b7", 0, I), B("AN", 0, I), A.mult, I)
+        at(t, "sh")
         SH = B("b2", 0, I)
         MM(SH, B("Sh"), B("R16"), True, False, I)
         MM(SH, B("Tp0"), B("ct"), False, False, I)
-        nb, cb = ("b4", "b5") if len(slow) % 2 == 0 else ("b5", "b4")
-        at(t, "wp")
-        MM(B("b1", 0, CW), B("Ib"), B("cb"), True, False, CW)
-        MM(B("b1", 0, I), B("Ib"), B("E16"), False, False, I)
-        MM(B("b1", 0, I), B("OBB"), B("RS"), False, False, I)
-        MM(B("b1", I, CW), B("Tp0"), B("CAND"), False, False, I)
-        MM(B("b1", I, CW), B("OBB"), B("RS"), False, False, I)
+        at(t, "ce")
+        MM(P(FS), B("Ih"), B(f0), True, False, I)
+        MM(P(FS), B("Ih"), B(L), False, last, I)
+        if not last:
+            MM(P(CE), B("Im"), B("E16"), False, False, I)
+            MM(P(CE), B("Ib"), B("CAND"), False, True, I)
+        at(t, "f")
+        plus(C["f"], B(f1), P(FS), FO / 2 - 0.25, I)
+        at(t, "wc")
+        MM(P(WC), B("Tp0"), B("CAND"), False, False, I)
         at(t, "rp")
-        if RPS:
+        if C["rp"] == "S":
             act(B("RP"), P(UP), F.Sigmoid, I, scale=-1000.0, bias=2047500.0)
         else:
             ts(B("RP"), P(UP), 2048.0, None, A.is_lt, None, I)
-        MM(B("b1", 0, I), B("BIL"), B("RP"), False, False, I)
-        MM(B("b1", I, CW), B("OBB"), B("RP"), False, True, I)
-        tt(B("TP"), B("b1", 0, I), B("TS"), A.max, I)
-        tt(B("TC"), B("b1", I, CW), B("TP"), A.max, I)
+        MM(P(PC), B("BIL"), B("RP"), False, False, I)
+        MM(P(WC), B("OBB"), B("RP"), False, True, I)
+        tt(B("TP"), P(PC), B("TS"), A.max, I)
+        tt(B("TC"), P(WC), B("TP"), A.max, I)
+        at(t, "y")
         tiny(B(cb, 16, 28), "W1", "TC", True, True)
-        ts(B("TU"), B(cb, 16, 28), 16 * CEN, None, A.add, None, 12)
+        plus(C["tu"], B("TU"), B(cb, 16, 28), 16 * CEN, 12)
         tt(B("YD"), IX("X", "TU", 0, 12), B(f1), A.subtract, I, GA)
-        act(B(Y), B("YD"), F.Abs, I)
+        act(B(Y), B("YD"), F.Abs, I, bias=FO)
         if not last:
             add("G", ("send", t), [(Y, 0, I)], [], 1.2, send=t)
             Ln = "L%d" % (t + 1)
             bl = (-t) % N
             a, b = BLK * bl, BLK * bl + BLK
-            add("R", None, [], [(Ln, c, d) for c, d in ((0, a), (b, I)) if d > c], FLY, arr=t)
+            add("R", None, [], [(Ln, c, d) for c, d in ((0, a), (b, I)) if d > c], C["fly"], arr=t)
             at(t, "own")
-            act(B(Ln, a, b), B("YD", a, b), F.Abs, BLK)
+            act(B(Ln, a, b), B("YD", a, b), F.Abs, BLK, bias=FO)
             if t == 0:
                 late()
-        at(t, "m")
         MB = B(cb, 32, 44)
-        tiny(MB, "W1", Y, True, True)
+        if C["mu2"]:
+            at(t, "es")
+            MM(MB, B("Ib"), B("c24"), True, False, 12)
+        at(t, "m")
+        tiny(MB, "W1", Y, not C["mu2"], True)
         tt(B("QB"), MB, B("base"), A.add, 12)
-        tt(B("QF"), MB, B("QB"), A.subtract, 12)
-        ts(B("MU"), B("QF"), 24576.0, None, A.add, None, 12)
+        if C["mu2"]:
+            tt(B("MU"), MB, B("QB"), A.subtract, 12)
+        else:
+            tt(B("QF"), MB, B("QB"), A.subtract, 12)
+            ts(B("MU"), B("QF"), 24576.0, None, A.add, None, 12)
+        at(t, "es")
+        MM(B("b0", 0, I), B("Ih"), B(L), True, False, I)
         at(t, "wr")
-        MM(B("b0", 0, I), B("Ihq"), B(L), True, False, I)
-        MM(B("b0", 0, I), B("Ihq"), B(Y), False, True, I)
-        if WS:
-            act(B("WM"), B("b0", 0, I), F.Identity, I, bias=MAGIC)
-            act(B("WR"), B("WM"), F.Identity, I, bias=-MAGIC)
-        else:
-            ts(B("WR"), B("b0", 0, I), MAGIC, MAGIC, A.add, A.subtract, I)
+        MM(B("b0", 0, I), B("Ih"), B(Y), False, True, I)
+        plus(C["wr"], B("WR"), B("b0", 0, I), -0.25, I)
         if not last:
-            tc(IX("X", "MU", 0, 12), B("WR"), I, 3.5)
+            tc(IX("X", "MU", 0, 12), B("WR"), I, C["sa"])
         else:
-            MM(B("b7", 0, I), B("OB"), B(Y), True, True, I)
-            ts(B("MN", 0, I), B("b7", 0, I), 24568.5, None, A.add, None, I)
-            tt(B("FM"), B("b7", 0, I), B("MN", 0, I), A.subtract, I)
-            ts(B("b7", I, CW), B("FM"), 24577.0, -1.0, A.add, A.mult, I)
+            at(t, "yw")
+            for h in range(8):
+                MS([(B("b3", 0, I), B("IC", 128 * c, 128 * c + 128), B("X", c, W, 16)) for c in range(2 * h, 2 * h + 2)], h == 0, h == 7, I)
+            at(t, "ex")
+            MM(B("b1", 0, I), B("OB"), B(Y), True, True, I)
+            ts(B("MN", 0, I), B("b1", 0, I), 24568.5, None, A.add, None, I)
+            tt(B("FM"), B("b1", 0, I), B("MN", 0, I), A.subtract, I)
+            ts(B("b1", I, CW), B("FM"), 24577.0, -1.0, A.add, A.mult, I)
             tt(B("YD"), IX("X", "MU", 0, 12), B("WR"), A.subtract, I, GA)
-            tt(B("b7", 0, I), B("b7", I, CW), B("YD"), A.mult, I)
-            tt(B("OX"), B("b7", 0, I), B("OX"), A.add, I)
-            dma("Y", "yx", "OX", 2.5, False)
+            tt(B("FM"), B("b1", I, CW), B("YD"), A.mult, I)
+            tt(B("YX"), B("b3", 0, I), B("FM"), A.add, I)
         at(t, "new")
         MM(SH, B("Tp"), B("TC"), False, True, I)
         tt(B("S16"), SH, B("QQ"), A.subtract, I)
-        ts(B("OS" if last else "SU"), B("S16"), CEN, None, A.add, None, I, 1 if last else 0.5)
+        at(t, "su")
+        plus(C["su"], B("OS" if last else "SU"), B("S16"), CEN, I, 1 if last else 0.5)
         at(t, "sw")
         SW = B("SWH", I * t, I * t + I)
-        if CNT:
+        if C["cnt"]:
             MM(B(nb, 0, I), B("OB"), B("RS"), True, False, I)
             MM(B(nb, 0, I), B("OB"), B("RP"), False, True, I)
             act(SW, B(nb, 0, I), F.Relu, I, scale=-1.0, bias=1.0)
         else:
-            act(SW, B("b1", I, CW), F.Sigmoid, I, scale=0.1, bias=B("nB", 2, 3))
-        at(t, "e")
+            act(SW, P(WC), F.Sigmoid, I, scale=0.1, bias=537.5)
         if not last:
-            tt(B("b3", 0, I), B("b3", I, CW), SW, A.mult, I)
-            tt(B("E16"), B("b3", 0, I), B("E16"), A.add, I)
-            ts(B("EU"), B("E16"), CEN, None, A.add, None, I, 0.5)
-        at(t, "a")
-        if not last:
-            if ATS:
-                MM(B(nb, I, CW), B("Ib"), B("AT"), True, False, I)
-                MM(B(nb, I, CW), B("Ib"), SW, False, True, I)
-                act(B("AT"), B(nb, I, CW), F.Copy, I)
-            else:
-                tt(B("BND"), B("BND"), SW, A.add, I, 2)
+            at(t, "e")
+            tt(P(CE), P(CE), SW, A.mult, I)
+            tt(B("E16"), P(CE), B("E16"), A.add, I)
+            at(t, "eu")
+            plus(C["eu"], B("EU"), B("E16"), CEN, I, 0.5)
+            at(t, "a")
+            MM(B(nb, I, CW), B("Ib"), B("AT"), True, False, I)
+            MM(B(nb, I, CW), B("Ib"), SW, False, True, I)
+            act(B("AT"), B(nb, I, CW), F.Copy, I)
         else:
-            dma("Y", "yf", f1, 2.5, False)
+            at(t, "of")
+            act(B("F0"), B(f1), F.Identity, I, bias=-FO)
+            dma("Y", "yf", "F0", 2.5, False)
             dma("Y", "ys", "OS", 2.5, False)
             at(t, "yp")
             for h in range(2):
-                MS([(B("b3", 0, 12), slide("W0", r), B("SWH", I * t + r, I * t + I, 16)) for r in range(8 * h, 8 * h + 8)], h == 0, h == 1, 12)
-            tt(B("PK", 24, 36), B("PK", 12, 24), B("PH", 12 * t, 12 * t + 12), A.add, 12, 2)
-            tt(B("PK", 36, 48), B("b3", 0, 12), B("PK", 24, 36), A.mult, 12)
+                MS([(B(nb, 0, 12), slide("W0", r), B("SWH", I * t + r, I * t + I, 16)) for r in range(8 * h, 8 * h + 8)], h == 0, h == 1, 12)
+            ts(H1, B("PH", 12 * t, 12 * t + 12), float(PLN - ROT), None, A.add, None, 12)
+            ts(H2, H1, PLN - 1, None, A.bitwise_and, None, 12)
+            tt(B("PK", 24, 36), B("PK", 12, 24), H2, A.add, 12, 2)
+            tt(B("PK", 36, 48), B(nb, 0, 12), B("PK", 24, 36), A.mult, 12)
             tt(B("YPF"), B("PK", 36, 48), B("YPF"), A.max, 12, 2)
-            dma("Y", "yp", "YPF", 2.5, False)
+            dma("S", "yp", "YPF", 2.5, False)
+            dma("Y", "yx", "YX", 2.5, False)
     return ops
 
 
@@ -523,44 +546,29 @@ def _deps(ops):
 
 
 def _schedule(ops, data, order):
-    n = len(ops)
-    succ = [[] for _ in range(n)]
-    for i in range(n):
-        for j in data[i]:
-            succ[j].append((i, LAT))
-        for j in order[i]:
-            succ[j].append((i, 0.0 if ops[i][0] == ops[j][0] else LAT))
-    rank = [(ops[i][5]["due"], i) for i in range(n)]
-    left = [len(data[i]) + len(order[i]) for i in range(n)]
-    ready = [0.0] * n
-    pool, free = {}, {}
-    for i in range(n):
-        if left[i] == 0:
-            pool.setdefault(ops[i][0], []).append(i)
-    out = []
-    while True:
-        best = None
-        for q, l in pool.items():
-            if l:
-                st = max(free.get(q, 0.0), min(ready[i] for i in l))
-                if best is None or st < best[0]:
-                    best = (st, q)
-        if best is None:
-            return out
-        st, q = best
-        i = min((k for k in pool[q] if ready[k] <= st + 1e-9), key=lambda k: rank[k])
-        if ops[i][4] > 0.2:
-            i = min((k for k in pool[q] if k == i or (ready[k] <= st + HOLD and ops[k][5]["step"] in HOLDS)), key=lambda k: rank[k])
-            st = max(st, ready[i])
-        pool[q].remove(i)
-        fin = st + ops[i][4]
-        free[q] = st + (0.1 if "dma" in ops[i][5] or q == "R" else ops[i][4])
-        out.append((i, st, fin))
-        for k, w in succ[i]:
-            ready[k] = max(ready[k], fin + w)
-            left[k] -= 1
-            if left[k] == 0:
-                pool.setdefault(ops[k][0], []).append(k)
+    at, seen, turn = {}, {}, []
+    for i, o in enumerate(ops):
+        turn.append(max(int(o[5]["due"] // 100), 0))
+        s = (turn[i], o[0], o[5]["step"] or "c")
+        seen[s] = seen.get(s, 0) + 1
+        at[turn[i], o[0], s[2] + str(seen[s])] = i
+    seq = {w.split()[0]: w.split()[1:] for w in SEQ.split(";")}
+    full = {q: [i for i, o in enumerate(ops) if o[0] == q and (q != "G" or turn[i])] for q in "GYR"}
+    full["G"] = [at[0, "G", k] for k in seq["cG"]] + full["G"]
+    for q in "VST":
+        full[q] = [at[0, q, k] for k in seq["c" + q]]
+        for u in range(TURNS + 1):
+            keys = [(u + (k[0] == "+"), q, k.lstrip("+")) for k in seq[q]]
+            full[q] += [at[k] for k in keys if k[0] and k in at]
+    done, out = set(), []
+    while len(out) < len(ops):
+        n = len(out)
+        for l in full.values():
+            while l and all(j in done for j in data[l[0]] + order[l[0]]):
+                done.add(l[0])
+                out.append((l.pop(0), 0, 0))
+        assert len(out) > n
+    return out
 
 
 _PLAN = {}
@@ -572,16 +580,11 @@ def _plan():
         data, order, groups = _deps(ops)
         sched = _schedule(ops, data, order)
         place = {x[0]: k for k, x in enumerate(sched)}
-        ends = {}
         for grp in groups:
             begins = ops[grp[0]][5]["fl"][0]
             grp.sort(key=lambda i: place[i])
             for i in grp:
                 ops[i][5]["fl"][:] = [begins and i == grp[0], i == grp[-1]]
-            bank = ops[grp[0]][3][0][0]
-            if not begins:
-                ops[ends[bank]][5]["fl"][1] = False
-            ends[bank] = grp[-1]
         _PLAN["ops"], _PLAN["data"], _PLAN["sched"] = ops, data, sched
     return _PLAN["ops"], _PLAN["data"], _PLAN["sched"]
 
@@ -598,7 +601,7 @@ def _transfer(T, topo, dst, engines, t, to, a, n):
 
 def _hand_on(g, core, T, topo):
     home = [c for c in topo.cores_of(core) if T.rank_of(c) is not None]
-    if not HELP or not home or core not in _helpers(T, topo, home[0]):
+    if not home or core not in _helpers(T, topo, home[0]):
         return
     rank, k = T.rank_of(home[0]), _helpers(T, topo, home[0]).index(core)
     for t in range(TURNS - 1):
@@ -622,31 +625,23 @@ def rank_program(g, core, T, topo):
     know = {q: {} for q in eng}
 
     def send(t):
-        if HELP:
-            own = (-t) % N
-            dst = T.cores[(rank + (own ^ 1) + t) % N]
-            out = topo.engines(core, dst)[:EN]
-            tr = []
-            for k, (h, p) in enumerate(zip(_helpers(T, topo, core), [p for p in range(N // 2) if p != own // 2])):
-                e = [x for x in topo.engines(core, h) if x not in out][EN * k:EN * k + EN]
-                tr.append(_transfer(T, topo, h, e, t, "Y%d" % t, 2 * BLK * p, 2 * BLK))
-            g.remote_dma_fused(tr, local_sem=T.sem.sent)
-            g.remote_dma_fused([_transfer(T, topo, dst, out, t, "L%d" % (t + 1), BLK * (own ^ 1), BLK)], local_sem=T.sem.sent)
-            return EN * (len(tr) + 1)
+        own = (-t) % N
+        dst = T.cores[(rank + (own ^ 1) + t) % N]
+        out = topo.engines(core, dst)[:EN]
         tr = []
-        for b in range(N):
-            dst = T.cores[(rank + b + t) % N]
-            if dst != core:
-                tr.append(_transfer(T, topo, dst, [topo.engines(core, dst)[len(tr)]], t, "L%d" % (t + 1), BLK * b, BLK))
+        for k, (h, p) in enumerate(zip(_helpers(T, topo, core), [p for p in range(N // 2) if p != own // 2])):
+            e = [x for x in topo.engines(core, h) if x not in out][EN * k:EN * k + EN]
+            tr.append(_transfer(T, topo, h, e, t, "Y%d" % t, 2 * BLK * p, 2 * BLK))
         g.remote_dma_fused(tr, local_sem=T.sem.sent)
-        return len(tr)
+        g.remote_dma_fused([_transfer(T, topo, dst, out, t, "L%d" % (t + 1), BLK * (own ^ 1), BLK)], local_sem=T.sem.sent)
+        return EN * (len(tr) + 1)
 
     sent = 0
     dmas = []
     for (i, st, fin) in sched:
         q, fn, rd, wr, cost, kw = ops[i]
         if q == "R":
-            seq[i] = ("arr%d" % kw["arr"], (N - 1) * (EN if HELP else 1))
+            seq[i] = ("arr%d" % kw["arr"], (N - 1) * EN)
             clock[i] = {}
             continue
         kn = know[q]

@@ -1,6 +1,5 @@
-import numpy as np
 from concourse.bass import DstId, RemoteDMATransfer
-from concourse.mybir import dt, AluOpType, AxisListType, ActivationFunctionType
+from concourse.mybir import AluOpType, ActivationFunctionType
 
 A = AluOpType
 F = ActivationFunctionType
@@ -11,68 +10,67 @@ PA = 64
 EN = 4
 CEN = 1536.0
 BIG = 8192.0
-MAGIC = 12582912.0
 FO = 1280.0
 ROT = 712
+WAYS = "ttbbmm"
 BF, HF, FL, I32, U16 = "bfloat16", "float16", "float32", "int32", "uint16"
 C = dict(
-    ways="ttbbmm",
-    stack=tuple(("VS"[k % 2], 32 * k, 32 * k + 32) for k in range(6)),
     plan=(("V", 0, 32), ("S", 32, 64), ("S", 64, 128), ("S", 128, 192)),
-    sx=((0, 64), (64, 128), (128, 192)),
-    sq=True, ox="V", t2=True, bm={3: 1, 4: 0},
-    cand="S", tu="V", r2="S", rp="V", su="S", eu="S", f="S", wr="S", h1="V", pu="V",
-    cnt=False, mu2=True,
-    tr=0.62, so=0.15, lat=0.11, hold=0.15, fly=2.5, ga=1.5, sa=3.5,
-    order=("pre pr6 pr7 yx xs0 xs1 xs2 xs3 xs4 xs5 xe0 xe1 xe2 zp mn0 mn1 mn2 mn3 sx0 sx1 sx2 dx0 dz0 dx1 dz1 zq pp0 pp1 dx2 dz2 pp2 dx3 dz3 pp3 dx4 dz4 pp4 "
-           "dx5 dz5 pp5 u h1 h2 h3 sz sv0 sv1 sv2 sv3 r2 sp0 sp1 sp2 sp3 sp4 sp5 cand sc ts wp wc rp f y m es wr set an wd qq sh new su sw ce e eu a own pk yp ex of e0 bs pe pe0 yw s0 pre0 pr60 pr70").split())
-SEQ = """V pk2 xs01 xs41 xs21 e01 yx1 e02 xe01 mn12 h11 mn21 mn31 mn11 mn01 mn22 h12 mn02 dx31 dx21 mn32 pp41 h31 pp51 h32 pk1 r21 set1 rp1 pk3 ts1 bs1 pk4 rp2 pk5 rp3 pk6 wd1 yp1 wd2 y1 yp2 y2 pk7 qq1 e1 pk9 new1 ex1 yp3 pk8 e2 m1 ex2 m2 wr1 ex3 ex4 yp4 ex5 pk10 ex6 yp5 ; cV c1 c4 c5 c7 c18 c8 c6 c3 c10 c2 c11 c19 c17 c16 c12 c14 c20 c22 c9 c13 c21 c15 ; S s01 xs11 s02 xs51 xs31 xe01 xe21 xe11 pp11 h21 pp31 r21 cand1 s03 an1 f1 sw1 of1 y1 a1 own1 wr1 eu1 su1 yp1 ; cS c3 c4 c1 c6 c5 c2 ; T pre03 yx1 pre01 yx3 pre04 pre02 yx2 sx01 sx04 sx02 sx03 yx4 pre05 sx24 sx21 sx23 sx22 u1 sx12 zp1 pr702 u2 zq1 sx14 dx01 sz2 dz01 sx11 pr701 pr601 sv21 dx11 sz3 dz11 sv11 sv12 sz1 sx13 sv22 sv01 pe02 sv02 pe01 sv31 dx51 dx41 sp11 sv32 sp01 pr602 sp41 sp21 sp31 sp51 wp1 wp2 ts1 wc1 an2 rp2 rp1 an1 an3 ce3 yw1 ce4 ce1 ce2 yw2 y1 y2 yw4 a1 sh1 es2 qq1 new1 es1 a2 sh2 yp1 +pre5 ex1 +pr62 m2 m1 wr1 +pre2 +pr72 +pre7 yw7 +pr71 yw5 +pr61 +pe1 +pe2 +pre3 yp2 yw6 yw3 +pre4 +pre1 yw8 +pre6 ; cT  ; cG c1 c2 c3 c14 c4 c15 c7 c18 c5 c6 c17 c11 c16 c13 c8 c21 c12 c10 c9 c20 c19"""
+    plan0=(("S", 0, 64), ("S", 64, 112), ("V", 112, 192)),
+    to=0.0, vo=0.055, tr=0.57, so=0.12, fly=2.5, ga=1.5, sa=3.5, xl=4.0, pl=8.0)
+SEQ = """
+cV c1 c5 c2 c18 c3 c4 c7 c8 c6 c9 c10 c14 c11 c15 c21 c13 c17 c19 c16 c12 c22 c23 c20 ; cS c2 c1 c3 ; cT ;
+cG c1 c18 c4 c2 c14 c3 c5 c9 c13 c16 c19 c10 c8 c12 c6 c17 c7 c11 c15 ;
+V pk1 xs01 xs21 xs41 yx1 xe01 pk2 bs2 mn11 mn32 h11 mn12 mn22 mn21 mn31 e01 s01 xa11 mn02 mn01 dx21 pp41 dx31 pp51 h12 pp52 rs1 h31 set1
+  rp1 ts1 pk3 rp2 yp1 rp3 pk4 wd1 pk5 wd2 bs1 y1 yp2 y2 qq1 pk6 e1 pk7 new1 e2 yp3 ex1 m1 yp4 m2 ex2 ex3 wr1 ex4 ;
+S s01 xs11 xs31 xs51 e01 xe01 xe21 xa01 xa11 xe11 pp11 pp21 r21 ra1 pp31 ha1 h21 s02 h31 cand1 yp1 pk1 an1 pk2 sw1 f1 y1 ex1 of1 a1 own1
+  wr1 ex2 eu1 yp2 su1 ;
+T yx1 yx3 yx4 pre03 pre02 pre01 yx2 sx03 sx01 sx02 sx04 sx14 sx11 sx12 sx13 zp1 pr701 u1 u2 sx24 zq1 pre04 sz1 pr601 dx01 sx21 sv11 sv32
+  dx11 sv12 pr702 dz01 dx42 sx22 sz2 dz11 sv21 sv22 sv31 dx51 pe01 pe02 bn02 ax11 ax01 az11 sm1 az01 ax51 dx41 sx23 dx52 bn01 ax42 ax41 ax52
+  sv02 sv01 sp01 sp41 sp11 sp21 bn03 sp51 sp52 sp31 dt1 ts1 an1 wp2 wp1 rp1 rp2 an2 yw1 wc1 ce3 yw7 ce1 ce4 ce2 y1 y2 qq1 yp1 yp2 a1 qq2
+  sh1 sh3 new1 dm1 sh2 ex1 a2 es1 m2 m1 wr1 yw5 +pr61 +pre3 +pr72 yw6 yw4 +pr71 +pre2 yw3 yw8 +pe1 +pre5 +pre1 +pe2 +pre6 yw2 +pre7 +pre4
+"""
 
 SCRATCH = {}
 for _n, _w, _d in [
-        ("X", W, BF), ("XS", W, BF), ("XE", W, BF), ("MN", W, HF), ("MX", W, BF),
+        ("X", W, BF), ("XS", W, BF), ("XE", W, BF), ("MN", W, HF), ("MX", W, BF), ("DE", 1024, BF),
         ("PLT", PLN + ROT, I32), ("SI", I, I32), ("THI", I, I32), ("PI", 12, I32),
         ("S16", I, HF), ("E16", I, HF), ("CAND", I, HF), ("BND", I, HF), ("AT", I, BF), ("SWH", TURNS * I, BF),
-        ("SU", I, U16), ("EU", I, U16), ("TU", 12, U16), ("PU", 12, U16), ("MU", 12, U16),
-        ("R2", I, I32), ("RS", I, BF), ("RP", I, BF), ("AN", 2 * I, BF), ("SET", I, BF), ("QQ", I, FL),
+        ("SU", I, U16), ("EU", I, U16), ("TU", 12, U16), ("PU", 12, U16), ("P0", 12, U16), ("MU", 12, U16),
+        ("R2", I, I32), ("RS", I, BF), ("RP", I, BF), ("AN", I, BF), ("SET", I, BF), ("R16", I, HF), ("QQ", I, FL),
         ("TS", I, HF), ("TP", I, HF), ("TC", I, HF),
-        ("F0", I, BF), ("FA", I, HF), ("FB", I, HF), ("YD", I, FL), ("WR", I, I32), ("QF", 12, FL), ("QB", 12, HF),
-        ("HH", 48, I32), ("PH", 12 * TURNS, I32),
-        ("KT", 12 * TURNS, FL), ("PK", 12 * TURNS, FL), ("KK", 180, FL),
-        ("K0", 12, I32), ("PE", 12, I32), ("YPF", 12, FL), ("OS", I, FL), ("OX", I + 12 * TURNS, FL), ("YX", I, FL),
+        ("F0", I, BF), ("FA", I, HF), ("FB", I, HF), ("YD", I, FL), ("WR", I, I32), ("QB", 12, HF),
+        ("HH", 36, I32), ("PH", 12 * TURNS, I32), ("KT", 12 * TURNS, FL), ("PK", 12 * TURNS, FL), ("KK", 180, FL),
+        ("K0", 12, I32), ("PE", 12, I32), ("YPF", 12, FL), ("OS", I, FL), ("OX", 12 * TURNS, FL), ("YX", I, FL), ("FM", I, FL),
         ("ip", 1, I32), ("ig", 1, I32), ("il", 1, I32), ("ibase", 12, I32), ("gf", 1, FL), ("g15", 1, FL), ("l21", 1, FL),
         ("r16", 1, FL), ("row", 144, FL), ("grow", 128, FL), ("base", 12, FL),
-        ("cv", CW, BF), ("FM", I, FL), ("c24", 12, BF), ("zero", 128, BF), ("NT", 128, BF),
+        ("cv", CW, BF), ("cz", CW, HF), ("ct", I, BF), ("cb", I, BF), ("c24", 12, BF), ("zero", 128, BF),
         ("W1", 144, BF), ("W2", 144, BF), ("Wm", 144, BF), ("Wmh", 144, BF), ("Wu", 144, BF), ("W0", 144, BF),
         ("Ib", 128, BF), ("Im", 128, BF), ("Ih", 128, BF), ("I32", 128, BF), ("I64m", 128, BF),
-        ("OB", 128, BF), ("OBh", 128, BF), ("OBB", 128, BF), ("OBm", 128, BF), ("DE", W, BF),
-        ("Ls", 128, BF), ("BIL", 128, BF), ("Sh", 128, BF),
-        ("ShI", 128, BF), ("R16", I, HF), ("Tp", 128, BF), ("Tp0", 128, BF),
-        ("cz", CW, HF), ("ct", I, BF), ("cb", I, BF), ("IC0", 512, BF), ("IC", 16 * 128, BF)]:
+        ("OB", 128, BF), ("OBh", 128, BF), ("OBB", 128, BF), ("OBm", 128, BF),
+        ("BL", 128, BF), ("BLm", 128, BF), ("BIL", 128, BF), ("Sh", 128, BF), ("NT", 128, BF), ("Tp", 128, BF), ("Tp0", 128, BF),
+        ("IC0", 512, BF), ("IC", 16 * 128, BF)]:
     SCRATCH[_n] = ("sbuf", [128, _w], _d)
-for _t in range(8):
+for _t in range(TURNS):
     SCRATCH["L%d" % _t] = ("sbuf", [128, I], BF)
     SCRATCH["Y%d" % _t] = ("sbuf", [128, I], BF)
 for _t in (0, 1, 2, 3, 6, 7):
     SCRATCH["b%d" % _t] = ("psum", [128, 512], FL)
 SCRATCH["b45"] = ("psum", [128, 1024], FL)
-NDMA = 13
-SEMAPHORES = ["qV", "qS", "qT", "qG", "sent"] + ["arr%d" % t for t in range(8)] + ["dm%d" % k for k in range(NDMA)]
+SEMAPHORES = ["qV", "qS", "qT", "qG", "sent"] + ["arr%d" % t for t in range(TURNS)] + ["dm%d" % k for k in range(12)]
 
 
 def _build():
     ops = []
     CY = 0.00083
     GA = C["ga"]
-    WAYS = C["ways"]
-    D = {n: float(k) for k, n in enumerate(C["order"])}
     now = [0.0, ""]
 
     def add(q, fn, rd, wr, cost, **kw):
         ops.append([q, fn, [r for r in rd if r], [r for r in wr if r], cost, dict(kw, due=now[0], step=now[1])])
 
     def at(t, step):
-        now[:] = [100.0 * (t + 1) + D[step], step]
+        now[:] = [100.0 * (t + 1), step]
 
     def B(name, a=None, b=None, st=None):
         if name in ("b4", "b5"):
@@ -97,20 +95,20 @@ def _build():
         return [r for x in xs if isinstance(x, tuple) for r in x[1:]]
 
     def vcost(n, f):
-        return 0.055 + max(64, n * f) * CY
+        return C["vo"] + max(64, n * f) * CY
 
-    def MM(out, lhsT, rhs, start, stop, n, f=1.0):
-        MS([(out, lhsT, rhs)], start, stop, n * f)
+    def MM(out, lhsT, rhs, start, stop, n=I):
+        MS([(out, lhsT, rhs)], start, stop, n)
 
     def MS(mm, start, stop, n):
         fl = [start, stop]
         add("T", lambda g, T: [g.tensor.matmul(o[0](T), w[0](T), r[0](T), fl[0] and k == 0, fl[1] and k == len(mm) - 1) for k, (o, w, r) in enumerate(mm)],
-            [x for o, w, r in mm for x in regs(w, r)], [x for o, w, r in mm for x in regs(o)], len(mm) * max(64, n) * CY * C["tr"], fl=fl)
+            [x for o, w, r in mm for x in regs(w, r)], [x for o, w, r in mm for x in regs(o)], len(mm) * (max(64, n) * CY * C["tr"] + C["to"]), fl=fl)
 
-    def tt(o, a, b, op, n, f=1.0):
+    def tt(o, a, b, op, n=I, f=1.0):
         add("V", lambda g, T: g.vector.tensor_tensor(o[0](T), a[0](T), b[0](T), op), regs(a, b), regs(o), vcost(n, f))
 
-    def ts(o, a, s1, s2, op0, op1, n, f=1.0):
+    def ts(o, a, s1, s2, op0, op1, n=I, f=1.0):
         def fn(g, T):
             if op1 is None:
                 return g.vector.tensor_scalar(o[0](T), a[0](T), val(s1, T), None, op0)
@@ -123,48 +121,53 @@ def _build():
     def fill(o, c, n):
         add("V", lambda g, T: g.vector.memset(o[0](T), c), [], regs(o), vcost(n, 0.5))
 
-    def act(o, a, f, n, fc=1.0, **kw):
-        add("S", lambda g, T: g.scalar.activation(o[0](T), a[0](T), f, **{k: val(v, T) for k, v in kw.items()}),
-            regs(a, *kw.values()), regs(o), (0.065 if len(a) > 2 else C["so"]) + n * fc * CY)
+    def act(o, a, f, n=I, fc=1.0, **kw):
+        add("S", lambda g, T: g.scalar.activation(o[0](T), a[0](T), f, **kw), regs(a), regs(o), (0.065 if len(a) > 2 else C["so"]) + n * fc * CY)
 
-    def plus(q, o, a, c, n, f=1.0):
+    def plus(q, o, a, c, n=I, f=1.0):
         if q == "V":
             if c:
                 ts(o, a, c, None, A.add, None, n, f)
             else:
                 tc(o, a, n, f)
         elif c:
-            act(o, a, F.Identity, n, max(f, 1.0), bias=c)
+            act(o, a, F.Identity, n, f, bias=c)
         else:
-            act(o, a, F.Copy, n, max(f, 1.0))
+            act(o, a, F.Copy, n, f)
 
-    def tiny(out, w, src, first, last, n=12, width=I):
+    def tiny(out, w, src, first, last, n=12, a=0, b=I):
         for h in range(2):
-            MS([(out, slide(w, r), B(src, r, width, 16)) for r in range(8 * h, 8 * h + 8)], first and h == 0, last and h == 1, n)
+            MS([(out, slide(w, r), B(src, a + r, b, 16)) for r in range(8 * h, 8 * h + 8)], first and h == 0, last and h == 1, n)
 
     nd = [0]
 
     def dma(q, dst, src, cost, load):
-        k = nd[0]
         nd[0] += 1
-        add(q, lambda g, T: (g.sync if q == "Y" else g.scalar).dma_start(T[dst][:], T[src][:]),
-            [] if load else [(src, 0, 1 << 20)], [(dst, 0, 1 << 20)] if load else [], cost, dma=k)
+        add(q, lambda g, T: (g.sync if q == "Y" else g.scalar).dma_start(dst[0](T), src[0](T)),
+            [] if load else regs(src), regs(dst) if load else [], cost, dma=nd[0] - 1)
 
-    dma("Y", "X", "x0", 3.5, True)
-    dma("S", "SI", "s0", 2.5, True)
-    dma("S", "L0", "z0", 3.0, True)
-    dma("S", "PI", "p0", 3.0, True)
-    for a, b, c, cost in ((ROT, ROT + PLN, 0, 5.5), (0, ROT, PLN - ROT, 6.5)):
-        nd[0] += 1
-        add("Y", lambda g, T, a=a, b=b, c=c: g.sync.dma_start(T.PLT[:, a:b], T.pl[:, c:c + b - a]), [], [("PLT", a, b)], cost, dma=nd[0] - 1)
-    dma("S", "THI", "th", 4.0, True)
-    dma("S", "F0", "f0", 4.0, True)
+    x, p = C["xl"], C["pl"]
+    dma("S", B("SI"), B("s0"), 2.5, True)
+    dma("S", B("PI"), B("p0"), 2.5, True)
+    dma("Y", B("X"), B("x0"), x, True)
+    dma("Y", B("L0"), B("z0"), x + 0.1, True)
+    dma("Y", B("PLT", ROT, ROT + PLN), B("pl"), p, True)
+    dma("Y", B("THI"), B("th"), p + 0.2, True)
+    dma("Y", B("F0"), B("f0"), p + 0.3, True)
+    dma("Y", B("PLT", 0, ROT), B("pl", PLN - ROT, PLN), p + 1.2, True)
 
     def G(fn, rd, wr, n):
         add("G", fn, regs(*rd), regs(wr), 0.15 + 2 * n * CY)
-    G(lambda g, T: g.iota(T.ip[:], [[0, 1]], 0, 1), [], B("ip"), 1)
-    G(lambda g, T: g.iota(T.row[:], [[1, 144]], 0, 0, allow_small_or_imprecise_dtypes=True), [], B("row"), 144)
-    G(lambda g, T: g.iota(T.grow[:], [[1, 8], [0, 16]], 0, 0, allow_small_or_imprecise_dtypes=True), [], B("grow"), 128)
+
+    def iota(dst, pat, base, cm, n, rd=()):
+        kw = {} if SCRATCH[dst][2] == I32 else {"allow_small_or_imprecise_dtypes": True}
+        G(lambda g, T: g.iota(T[dst][:], pat, int(base), cm, **kw), rd, B(dst), n)
+
+    def sel(dst, src, pat, op, fill_, base, cm, n=128):
+        G(lambda g, T: g.affine_select(T[dst][:], T[src][:], pat, op, fill_, base, cm), [B(src)], B(dst), n)
+    iota("ip", [[0, 1]], 0, 1, 1)
+    iota("row", [[1, 144]], 0, 0, 144)
+    iota("grow", [[1, 8], [0, 16]], 0, 0, 128)
     fill(B("cv"), -11.0 / 512, CW)
     fill(B("zero"), 0.0, 128)
     act(B("AT"), B("cv", 0, I), F.Sigmoid, I, 9.0, scale=30000.0)
@@ -180,258 +183,239 @@ def _build():
     for dst, src, c, n in (("Wmh", "W1", -0.5, 144), ("OBh", "OB", 0.5, 128), ("Wu", "W1", B("l21"), 144), ("Wm", "W1", -1.0, 144),
                            ("W2", "W1", 2.0, 144), ("OBB", "OB", -BIG, 128)):
         ts(B(dst), B(src), c, None, A.mult, None, n, 0.5)
-    if "m" in WAYS:
-        fill(B("OBm"), 0.0, 128)
-        for k in range(4):
-            if WAYS[2 + k] == "m":
-                ts(B("OBm", k, 128, 4), B("OB", k, 128, 4), -1.0, None, A.mult, None, 32, 0.5)
-
-    def sel(dst, src, pat, op, fill_, base, cm, n=128):
-        G(lambda g, T: g.affine_select(T[dst][:], T[src][:], pat, op, fill_, base, cm), [B(src)], B(dst), n)
-
-    def const(dst, c, n):
-        G(lambda g, T: g.iota(T[dst][:], [[0, n]], int(c), 0, allow_small_or_imprecise_dtypes=True), [], B(dst), n)
+    fill(B("OBm"), 0.0, 128)
+    for k in range(4):
+        if WAYS[2 + k] == "m":
+            ts(B("OBm", k, 128, 4), B("OB", k, 128, 4), -1.0, None, A.mult, None, 32, 0.5)
     col, first = [[1, 128]], [[0, 8], [1, 16]]
     for x, c in (("Ib", 1.0), ("I32", 32.0), ("I64m", -64.0), ("Ih", 0.5), ("Im", -1.0)):
         sel(x, "zero", col, A.not_equal, c, 0, -1)
-    const("cb", -BIG, I)
-    sel("NT", "Ih", first, A.not_equal, 0.0, 0, 0)
-    sel("BIL", "OBB", col, A.is_gt, 0.0, 0, -1)
-    sel("BIL", "BIL", col, A.not_equal, BIG, 0, -1)
+    iota("cb", [[0, I]], -BIG, 0, I)
+    sel("BLm", "OBB", col, A.is_gt, 0.0, 0, -1)
+    sel("BIL", "BLm", col, A.not_equal, BIG, 0, -1)
     sel("Tp0", "Ib", first, A.is_equal, 0.0, 0, 0)
-    sel("Ls", "OB", col, A.is_gt, 0.0, 0, -1)
     sel("Sh", "OB", col, A.is_equal, 0.0, -1, -1)
-    sel("ShI", "Sh", col, A.not_equal, -1.0, 0, -1)
+    iota("c24", [[0, 12]], 16 * CEN, 0, 12)
+    sel("NT", "Ih", first, A.not_equal, 0.0, 0, 0)
     sel("Tp", "OB", first, A.is_equal, 0.0, 0, 0)
-    const("ct", 15 * CEN, I)
-    const("c24", 16 * CEN, 12)
-    G(lambda g, T: g.iota(T.ibase[:], [[-256, 12]], 0, 0), [], B("ibase"), 12)
+    iota("ct", [[0, I]], 15 * CEN, 0, I)
+    iota("ibase", [[-256, 12]], 0, 0, 12)
     sel("W0", "W1", [[-16, 9], [0, 16]], A.is_equal, 0.0, 0, 1, 144)
 
     def late():
-        G(lambda g, T: g.iota(T.KT[:], [[PLN, TURNS], [0, 12]], 2 * PLN - ROT, 0, allow_small_or_imprecise_dtypes=True), [B("Y0")], B("KT"), 96)
+        iota("KT", [[PLN, TURNS], [0, 12]], 2 * PLN - ROT, 0, 96, [B("Y0")])
         for h in range(4):
             o = 512 * h
-            G(lambda g, T, h=h: g.iota(T.IC0[:], [[1, 4], [0, 128]], 1 + 4 * h, 0, allow_small_or_imprecise_dtypes=True), [B("Y0")], B("IC0"), 512)
+            iota("IC0", [[1, 4], [0, 128]], 1 + 4 * h, 0, 512, [B("Y0")])
             G(lambda g, T, o=o: g.affine_select(T.IC[:, o:o + 512], T.IC0[:], [[0, 4], [-1, 128]], A.is_equal, 0.0, 0, 1), [B("IC0")], B("IC", o, o + 512), 512)
 
-    now[0] = -1.0
-    tc(B("PU"), B("PI"), 12)
+    tc(B("P0"), B("PI"), 12)
     tc(B("SU"), B("SI"), I)
+    tc(B("KK", 84, 96), B("PI"), 12)
     at(0, "s0")
-    plus("S", B("S16"), B("SI"), -CEN, I)
-    act(B("BND"), B("THI"), F.Identity, I, scale=1.0 / 64, bias=-32.0)
-    plus("S", B("FA"), B("F0"), FO, I)
+    plus("S", B("S16"), B("SI"), -CEN)
+    ts(B("BND"), B("THI"), -2048.0, 1.0 / 64, A.add, A.mult)
+    plus("S", B("FA"), B("F0"), FO)
     at(0, "e0")
-    ts(B("E16"), IX("PLT", "PU", 0, 12, ROT, ROT + PLN), -CEN, None, A.add, None, I, GA)
-    ts(B("EU"), B("E16"), CEN, None, A.add, None, I, 0.5)
+    plus("S", B("EU"), IX("PLT", "P0", 0, 12, ROT, ROT + PLN), 0.0, I, GA)
+    plus("V", B("E16"), IX("PLT", "P0", 0, 12, ROT, ROT + PLN), -CEN, I, GA)
     at(0, "bs")
+    ts(B("BL"), B("BLm"), -1.0, None, A.mult, None, 128, 0.5)
     ts(B("base"), B("ibase"), B("r16"), None, A.add, None, 12)
+
+    H, VL, UP, PC, WC, SC, ES = ("b2", 0), ("b2", I), ("b3", 0), ("b6", 0), ("b4", 0), ("b7", 0), ("b7", I)
+    FS, CE, SH = ("b1", 0), ("b1", I), ("b2", 0)
+
+    def P(reg, a=0, b=I):
+        return B(reg[0], reg[1] + a, reg[1] + b)
 
     for t in range(TURNS):
         L, Y = "L%d" % t, "Y%d" % t
         f0, f1 = ("FA", "FB") if t % 2 == 0 else ("FB", "FA")
         last = t == TURNS - 1
-        nb, cb = ("b4", "b5") if WAYS.count("t") % 2 == 0 else ("b5", "b4")
-        H, VL, UP, PC, WC, SC, FS, ES, CE = ("b2", 0), ("b2", I), ("b3", 0), ("b6", 0), ("b6", I), ("b7", 0), ("b1", 0), ("b7", I), ("b1", I)
-
-        def P(reg, a=0, b=I, st=None):
-            return B(reg[0], reg[1] + a, reg[1] + b, st)
-        cuts = C["stack"]
-        for k, (q, a, b) in enumerate(cuts):
+        for k in range(6):
             at(t, "xs%d" % k)
-            plus(q, B("XS", 16 * a, 16 * b), IX("X", "SU", a, b), -128.0, 16 * (b - a), GA)
-        for q, a, b in C["plan"]:
-            at(t, "xe%d" % (a // PA))
+            plus("VS"[k % 2], B("XS", 512 * k, 512 * k + 512), IX("X", "SU", 32 * k, 32 * k + 32), -128.0, 512, GA)
+        for q, a, b in C["plan"] if t else C["plan0"]:
+            at(t, ("xe%d" if t else "xa%d") % (a // PA))
             plus(q, B("XE", 16 * a, 16 * b), IX("X", "EU", a, b), 0.0, 16 * (b - a), GA)
         at(t, "pre" if t else "pre0")
         MM(B("b0", 0, CW), B("Ib"), B("cz"), True, False, CW)
-        MM(P(H), B("I32"), B("BND"), True, False, I)
-        MM(P(VL), B("OB"), B("cz", 0, I), False, False, I)
-        MM(P(VL), B("I32"), B("cv", 0, I), False, False, I)
-        MM(P(UP), B("I64m"), B("BND"), True, False, I)
         if t:
-            MM(P(H), B("I32"), B("AT"), False, False, I)
-            MM(P(UP), B("I64m"), B("AT"), False, False, I)
+            MM(P(H), B("I32"), B("BND"), True, False)
+        else:
+            MM(P(H), B("OBh"), B(L), True, False)
+        MM(P(VL), B("OB"), B("cz", 0, I), False, False)
+        MM(P(VL), B("I32"), B("cv", 0, I), False, False)
+        if not t:
+            at(t, "bn0")
+            MM(P(H), B("I32"), B("BND"), False, False)
+        MM(P(UP), B("I64m"), B("BND"), True, False)
+        if t:
+            MM(P(H), B("I32"), B("AT"), False, False)
+            MM(P(UP), B("I64m"), B("AT"), False, False)
         at(t, "pr6" if t else "pr60")
-        MM(P(PC), B("Ib"), B("cb"), True, False, I)
-        MM(P(WC), B("NT"), B("cb"), False, False, I)
+        MM(P(PC), B("Ib"), B("cb"), True, False)
         at(t, "pr7" if t else "pr70")
-        MM(P(SC), B("Ib"), B("S16"), True, False, I)
-        MM(P(ES), B("Im"), B("S16"), False, False, I)
+        MM(P(SC), B("Ib"), B("S16"), True, False)
+        MM(P(ES), B("Im"), B("S16"), False, False)
         at(t, "pe" if t else "pe0")
-        MM(P(PC), B("Ib"), B("E16"), False, False, I)
-        MM(P(ES), B("Ib"), B("E16"), False, False, I)
+        MM(P(PC), B("Ib"), B("E16"), False, False)
+        MM(P(ES), B("Ib"), B("E16"), False, False)
         if last:
             at(t, "yx")
             n = 12 * t
-            tiny(B("b1", 0, n), "W0", "SWH", True, False, n, t * I)
+            tiny(B("b1", 0, n), "W0", "SWH", True, False, n, 0, t * I)
             tiny(B("b1", n, n + 12), "W0", "AT", False, True)
-            plus(C["ox"], B("OX", 0, n + 12), B("b1", 0, n + 12), 0.0, n + 12)
+            tc(B("OX", 0, n + 12), B("b1", 0, n + 12), n + 12)
             at(t, "pk")
             tt(B("PK", 0, n), B("PH", 0, n), B("KT", 0, n), A.add, n, 2)
-            tc(B("KK", 84, 96), B("PI"), 12)
             tt(B("KK", 0, n), B("OX", 0, n), B("PK", 0, n), A.mult, n, 2)
-            ts(B("PK", 0, 12), B("OX", n, n + 12), float(PLN), None, A.mult, None, 12)
+            act(B("PK", 0, 12), B("OX", n, n + 12), F.Copy, 12, scale=float(PLN))
             for a, w in ((0, 48), (96, 24)):
                 tt(B("KK", a + 2 * w, a + 3 * w), B("KK", a, a + w), B("KK", a + w, a + 2 * w), A.max, w, 2)
             tt(B("K0"), B("KK", 144, 156), B("KK", 156, 168), A.max, 12, 2)
             ts(B("PE"), B("K0"), PLN - 1, None, A.bitwise_and, None, 12)
-            ts(B("PK", 12, 24), B("PK", 0, 12), float(PLN), None, A.add, None, 12)
+            plus("S", B("PK", 12, 24), B("PK", 0, 12), float(PLN), 12)
             tt(B("YPF"), B("PK", 0, 12), B("PE"), A.add, 12)
-        for c, (a, b) in enumerate(C["sx"]):
+        for c in range(3):
             at(t, "sx%d" % c)
+            a, b = PA * c, PA * c + PA
             for h in range(4):
-                MS([(P(H, a, b), slide("Wmh", k), B("XS", 16 * a + k, 16 * b, 16)) for k in range(4 * h, 4 * h + 4)], False, False, b - a)
+                MS([(P(H, a, b), slide("Wmh", k), B("XS", 16 * a + k, 16 * b, 16)) for k in range(4 * h, 4 * h + 4)], False, False, PA)
         at(t, "zp")
         MS([(B("b0", m, CW, 2), B("Ib"), B(L)) for m in range(2)], False, True, I)
         at(t, "u")
         tiny(B("b5", 0, 12), "Wu", L, True, True)
         at(t, "sz")
-        MM(P(H), B("OBh"), B(L), False, False, I)
-        MM(P(VL), B("OB"), B(L), False, False, I)
+        MM(P(VL), B("OB"), B(L), False, False)
+        if t:
+            MM(P(H), B("OBh"), B(L), False, False)
         at(t, "h1")
-        H1, H2, H3, H4 = [B("HH", 12 * k, 12 * k + 12) for k in range(4)]
-        plus(C["h1"], H1, B("b5", 0, 12), 0.0, 12)
+        H1, H2, H3 = [B("HH", 12 * k, 12 * k + 12) for k in range(3)]
+        PH = B("PH", 12 * t, 12 * t + 12)
+        tc(H1, B("b5", 0, 12), 12)
         ts(H2, H1, 4095, None, A.bitwise_and, None, 12)
-        at(t, "h2")
-        if C["sq"]:
-            act(H4, H2, F.Square, 12, bias=592.0)
-        else:
-            ts(H3, H2, 592.0, None, A.add, None, 12)
-            tt(H4, H3, H3, A.mult, 12)
+        at(t, "h2" if t else "ha")
+        act(H3, H2, F.Square, 12, bias=592.0)
         at(t, "h3")
-        ts(B("PH", 12 * t, 12 * t + 12), H4, 5, PLN - 1, A.arith_shift_right, A.bitwise_and, 12)
-        plus(C["pu"], B("PU"), B("PH", 12 * t, 12 * t + 12), 0.0, 12)
+        ts(PH, H3, 5, PLN - 1, A.arith_shift_right, A.bitwise_and, 12)
+        plus("S", B("PU"), PH, 0.0, 12)
         at(t, "cand")
-        plus(C["cand"], B("CAND"), IX("PLT", "PU", 0, 12, 0, PLN), -CEN, I, GA)
+        plus("S", B("CAND"), IX("PLT", "PU", 0, 12, 0, PLN), -CEN, I, GA)
         for q in range(NC):
             at(t, "mn%d" % (q // 2))
             tt(B("MN", CW * q, CW * q + CW), B("XS", q, W, NC), B("b0", 0, CW), A.min, CW)
             at(t, "sv%d" % (q // 2))
             MS([(P(VL), slide("Wm", q + NC * m), B("MN", CW * q + m, CW * q + CW, 2)) for m in range(2)], False, q == NC - 1, I)
         sums = []
-        slow = [x for x in WAYS if x == "t"]
-        ns = 0
-        if len(slow) < 6:
-            at(t, "zq")
-            MS([(B("b1", m, 512, 4), B("Ib"), B(L, PA, I)) for m in range(4)], True, True, I - PA)
-        if "m" in WAYS:
-            at(t, "sz")
-            MM(P(UP, PA, I), B("OBm"), B(L, PA, I), False, False, I - PA)
+        at(t, "zq")
+        MS([(B("b1", m, 512, 4), B("Ib"), B(L, PA, I)) for m in range(4)], True, True, I - PA)
+        at(t, "sm" if t else "bn0")
+        MM(P(UP, PA, I), B("OBm"), B(L, PA, I), False, False, I - PA)
         for n, way in enumerate(WAYS):
             a, b, st, h = (0, PA, 2, n) if n < 2 else (PA, I, 4, n - 2)
             d, o = 16 // st, 512 * n
             xe, mx = B("XE", 16 * a + h, 16 * b, st), B("MX", o, o + 512)
+            parts = [(a, b, o, 512)]
             if way == "t":
-                bk = "b%d" % (4 + ns % 2)
-                ns += 1
-                at(t, "dx%d" % n)
+                bk = "b%d" % (4 + n)
+                at(t, ("dx%d" if t else "ax%d") % n)
                 MM(B(bk), B("Ib"), xe, True, False, 512)
-                at(t, "dz%d" % n)
+                at(t, ("dz%d" if t else "az%d") % n)
                 MS([(B(bk, m, 512, d), B("Im"), B(L, a, b)) for m in range(d)], False, True, b - a)
                 at(t, "pp%d" % n)
-                if n > 1 or not C["t2"]:
-                    act(mx, B(bk), F.Abs, 512)
-                elif n == 1:
+                if n == 1:
                     add("S", lambda g, T: g.scalar.activation(T.MX[:, 0:1024], T.b45[:], F.Abs), regs(B("b4"), B("b5")), regs(B("MX", 0, 1024)),
                         C["so"] + 1024 * CY)
             elif way == "m":
-                at(t, "dx%d" % n)
-                MS([(P(UP, a, b), slide("Wm", st * m + h), B("XE", 16 * a + st * m + h, 16 * b, 16)) for m in range(d)], False, False, b - a)
+                at(t, ("dx%d" if t else "ax%d") % n)
+                for c in range(a, b, PA):
+                    MS([(P(UP, c, c + PA), slide("Wm", st * m + h), B("XE", 16 * c + st * m + h, 16 * (c + PA), 16)) for m in range(d)], False, False, PA)
                 at(t, "pp%d" % n)
-                tt(mx, xe, B("b1"), A.max, 512)
+                if n == 5:
+                    parts = [(a, a + PA, o, 256), (a + PA, b, o + 256, 256)]
+                for c, e, u, w in parts:
+                    tt(B("MX", u, u + w), B("XE", 16 * c + h, 16 * e, st), B("b1", u - o, u - o + w), A.max, w)
             else:
                 at(t, "dx%d" % n)
-                tt(B("DE", o, o + 512), xe, B("b1"), A.subtract, 512)
+                tt(B("DE", o - 1024, o - 512), xe, B("b1"), A.subtract, 512)
                 at(t, "pp%d" % n)
-                if n in C["bm"]:
-                    p = o - 512 * C["bm"][n]
-                    act(B("MX", p, o + 512), B("DE", p, o + 512), F.Abs, o + 512 - p)
-            sums.append(([(P(UP, a, b), slide("W2" if way == "m" else "W1", st * m + h), B("MX", o + m, o + 512, d)) for m in range(d)], "sp%d" % n, b - a))
+                act(mx, B("DE", o - 1024, o - 512), F.Abs, 512)
+            for c, e, u, w in parts:
+                sums.append(([(P(UP, c, e), slide("W2" if way == "m" else "W1", st * m + h), B("MX", u + m, u + w, d)) for m in range(d)], "sp%d" % n, e - c))
         for n, (mm, step, w) in enumerate(sums):
             at(t, step)
             MS(mm, False, n == len(sums) - 1, w)
-        at(t, "r2")
-        if C["r2"] == "S":
-            act(B("R2"), P(VL), F.Relu, I, bias=0.15625)
-        else:
-            ts(B("R2"), P(VL), 0.15625, 0.0, A.add, A.max, I)
-        tt(B("RS"), P(H), B("R2"), A.is_gt, I)
+        at(t, "r2" if t else "ra")
+        act(B("R2"), P(VL), F.Relu, bias=0.15625)
+        at(t, "rs")
+        tt(B("RS"), P(H), B("R2"), A.is_gt)
         at(t, "set")
-        tt(B("SET"), P(VL), B("R2"), A.is_le, I)
+        tt(B("SET"), P(VL), B("R2"), A.is_le)
         at(t, "ts")
-        MM(P(SC), B("BIL"), B("RS"), False, True, I)
-        ts(B("TS"), P(SC), -BIG, -CEN, A.add, A.max, I)
+        MM(P(SC), B("BIL"), B("RS"), False, True)
+        ts(B("TS"), P(SC), -BIG, -CEN, A.add, A.max)
+        at(t, "dt")
+        MM(P(WC), B("NT"), B("cb"), True, False)
         at(t, "wp")
-        MM(P(WC), B("OBB"), B("RS"), False, False, I)
-        MM(P(PC), B("OBB"), B("RS"), False, False, I)
+        MM(P(WC), B("OBB"), B("RS"), False, False)
+        MM(P(PC), B("OBB"), B("RS"), False, False)
         at(t, "an")
-        MM(B("b0", 0, I), B("Ls"), B("RS"), True, False, I)
-        MM(B("b0", I, CW), B("OBh"), B("RS"), False, False, I)
-        MM(B("b0", I, CW), B("I64m"), B("SET"), False, True, I)
-        act(B("AN"), B("b0", 0, CW), F.Sigmoid, CW, scale=1000.0, bias=-250.0)
+        MM(B("b0", I, CW), B("OBh"), B("RS"), True, False)
+        MM(B("b0", I, CW), B("I64m"), B("SET"), False, True)
+        act(B("AN"), B("b0", I, CW), F.Sigmoid, scale=1000.0, bias=-250.0)
         at(t, "wd")
-        tt(P(ES), P(ES), B("AN", I, CW), A.mult, I)
-        tt(B("R16"), P(ES), B("S16"), A.add, I)
+        tt(P(ES), P(ES), B("AN"), A.mult)
+        tt(B("R16"), P(ES), B("S16"), A.add)
         at(t, "qq")
-        MM(B("b7", 0, I), B("ShI"), B("R16"), True, True, I)
-        tt(B("QQ"), B("b7", 0, I), B("AN", 0, I), A.mult, I)
+        MM(B("b0", 0, I), B("Ih"), B("cb"), True, False)
+        MM(B("b0", 0, I), B("BL"), B("RS"), False, True)
+        tt(B("QQ"), B("b0", 0, I), B("R16"), A.min)
         at(t, "sh")
-        SH = B("b2", 0, I)
-        MM(SH, B("Sh"), B("R16"), True, False, I)
-        MM(SH, B("Tp0"), B("ct"), False, False, I)
+        MM(P(SH), B("Sh"), B("R16"), True, False)
+        MM(P(SH), B("BLm"), B("RS"), False, False)
+        MM(P(SH), B("Tp0"), B("ct"), False, False)
         at(t, "ce")
-        MM(P(FS), B("Ih"), B(f0), True, False, I)
-        MM(P(FS), B("Ih"), B(L), False, last, I)
+        MM(P(FS), B("Ih"), B(f0), True, False)
+        MM(P(FS), B("Ih"), B(L), False, last)
         if not last:
-            MM(P(CE), B("Im"), B("E16"), False, False, I)
-            MM(P(CE), B("Ib"), B("CAND"), False, True, I)
+            MM(P(CE), B("Im"), B("E16"), False, False)
+            MM(P(CE), B("Ib"), B("CAND"), False, True)
         at(t, "f")
-        plus(C["f"], B(f1), P(FS), FO / 2 - 0.25, I)
+        plus("S", B(f1), P(FS), FO / 2 - 0.25)
         at(t, "wc")
-        MM(P(WC), B("Tp0"), B("CAND"), False, False, I)
+        MM(P(WC), B("Tp0"), B("CAND"), False, False)
         at(t, "rp")
-        if C["rp"] == "S":
-            act(B("RP"), P(UP), F.Sigmoid, I, scale=-1000.0, bias=2047500.0)
-        else:
-            ts(B("RP"), P(UP), 2048.0, None, A.is_lt, None, I)
-        MM(P(PC), B("BIL"), B("RP"), False, False, I)
-        MM(P(WC), B("OBB"), B("RP"), False, True, I)
-        tt(B("TP"), P(PC), B("TS"), A.max, I)
-        tt(B("TC"), P(WC), B("TP"), A.max, I)
+        ts(B("RP"), P(UP), 2048.0, None, A.is_lt, None)
+        MM(P(PC), B("BIL"), B("RP"), False, True)
+        MM(P(WC), B("OBB"), B("RP"), False, True)
+        tt(B("TP"), P(PC), B("TS"), A.max)
+        tt(B("TC"), P(WC), B("TP"), A.max)
         at(t, "y")
-        tiny(B(cb, 16, 28), "W1", "TC", True, True)
-        plus(C["tu"], B("TU"), B(cb, 16, 28), 16 * CEN, 12)
+        tiny(B("b5", 16, 28), "W1", "TC", True, True)
+        plus("V", B("TU"), B("b5", 16, 28), 16 * CEN, 12)
         tt(B("YD"), IX("X", "TU", 0, 12), B(f1), A.subtract, I, GA)
-        act(B(Y), B("YD"), F.Abs, I, bias=FO)
+        act(B(Y), B("YD"), F.Abs, bias=FO)
         if not last:
             add("G", ("send", t), [(Y, 0, I)], [], 1.2, send=t)
             Ln = "L%d" % (t + 1)
-            bl = (-t) % N
-            a, b = BLK * bl, BLK * bl + BLK
-            add("R", None, [], [(Ln, c, d) for c, d in ((0, a), (b, I)) if d > c], C["fly"], arr=t)
+            a = BLK * ((-t) % N)
+            add("R", None, [], [(Ln, c, d) for c, d in ((0, a), (a + BLK, I)) if d > c], C["fly"], arr=t)
             at(t, "own")
-            act(B(Ln, a, b), B("YD", a, b), F.Abs, BLK, bias=FO)
-            if t == 0:
-                late()
-        MB = B(cb, 32, 44)
-        if C["mu2"]:
-            at(t, "es")
-            MM(MB, B("Ib"), B("c24"), True, False, 12)
+            act(B(Ln, a, a + BLK), B("YD", a, a + BLK), F.Abs, BLK, bias=FO)
+        MB = B("b5", 32, 44)
+        at(t, "dm")
+        MM(MB, B("Ib"), B("c24"), True, False, 12)
         at(t, "m")
-        tiny(MB, "W1", Y, not C["mu2"], True)
+        tiny(MB, "W1", Y, False, True)
         tt(B("QB"), MB, B("base"), A.add, 12)
-        if C["mu2"]:
-            tt(B("MU"), MB, B("QB"), A.subtract, 12)
-        else:
-            tt(B("QF"), MB, B("QB"), A.subtract, 12)
-            ts(B("MU"), B("QF"), 24576.0, None, A.add, None, 12)
+        tt(B("MU"), MB, B("QB"), A.subtract, 12)
         at(t, "es")
-        MM(B("b0", 0, I), B("Ih"), B(L), True, False, I)
+        MM(B("b0", 0, I), B("Ih"), B(L), True, False)
         at(t, "wr")
-        MM(B("b0", 0, I), B("Ih"), B(Y), False, True, I)
-        plus(C["wr"], B("WR"), B("b0", 0, I), -0.25, I)
+        MM(B("b0", 0, I), B("Ih"), B(Y), False, True)
+        plus("S", B("WR"), B("b0", 0, I), -0.25)
         if not last:
             tc(IX("X", "MU", 0, 12), B("WR"), I, C["sa"])
         else:
@@ -439,51 +423,47 @@ def _build():
             for h in range(8):
                 MS([(B("b3", 0, I), B("IC", 128 * c, 128 * c + 128), B("X", c, W, 16)) for c in range(2 * h, 2 * h + 2)], h == 0, h == 7, I)
             at(t, "ex")
-            MM(B("b1", 0, I), B("OB"), B(Y), True, True, I)
-            ts(B("MN", 0, I), B("b1", 0, I), 24568.5, None, A.add, None, I)
-            tt(B("FM"), B("b1", 0, I), B("MN", 0, I), A.subtract, I)
-            ts(B("b1", I, CW), B("FM"), 24577.0, -1.0, A.add, A.mult, I)
+            MM(B("b1", 0, I), B("OB"), B(Y), True, True)
+            plus("S", B("MN", 0, I), B("b1", 0, I), 24568.5)
+            tt(B("FM"), B("b1", 0, I), B("MN", 0, I), A.subtract)
+            act(B("b1", I, CW), B("FM"), F.Identity, scale=-1.0, bias=-24577.0)
             tt(B("YD"), IX("X", "MU", 0, 12), B("WR"), A.subtract, I, GA)
-            tt(B("FM"), B("b1", I, CW), B("YD"), A.mult, I)
-            tt(B("YX"), B("b3", 0, I), B("FM"), A.add, I)
+            tt(B("FM"), B("b1", I, CW), B("YD"), A.mult)
+            tt(B("YX"), B("b3", 0, I), B("FM"), A.add)
         at(t, "new")
-        MM(SH, B("Tp"), B("TC"), False, True, I)
-        tt(B("S16"), SH, B("QQ"), A.subtract, I)
+        MM(P(SH), B("Tp"), B("TC"), False, True)
+        tt(B("S16"), P(SH), B("QQ"), A.max)
         at(t, "su")
-        plus(C["su"], B("OS" if last else "SU"), B("S16"), CEN, I, 1 if last else 0.5)
+        plus("S", B("OS" if last else "SU"), B("S16"), CEN)
         at(t, "sw")
         SW = B("SWH", I * t, I * t + I)
-        if C["cnt"]:
-            MM(B(nb, 0, I), B("OB"), B("RS"), True, False, I)
-            MM(B(nb, 0, I), B("OB"), B("RP"), False, True, I)
-            act(SW, B(nb, 0, I), F.Relu, I, scale=-1.0, bias=1.0)
-        else:
-            act(SW, P(WC), F.Sigmoid, I, scale=0.1, bias=537.5)
+        act(SW, P(WC), F.Sigmoid, scale=0.1, bias=537.5)
         if not last:
             at(t, "e")
-            tt(P(CE), P(CE), SW, A.mult, I)
-            tt(B("E16"), P(CE), B("E16"), A.add, I)
+            tt(P(CE), P(CE), SW, A.mult)
+            tt(B("E16"), P(CE), B("E16"), A.add)
             at(t, "eu")
-            plus(C["eu"], B("EU"), B("E16"), CEN, I, 0.5)
+            plus("S", B("EU"), B("E16"), CEN)
             at(t, "a")
-            MM(B(nb, I, CW), B("Ib"), B("AT"), True, False, I)
-            MM(B(nb, I, CW), B("Ib"), SW, False, True, I)
-            act(B("AT"), B(nb, I, CW), F.Copy, I)
+            MM(B("b6", I, CW), B("Ib"), B("AT"), True, False)
+            MM(B("b6", I, CW), B("Ib"), SW, False, True)
+            act(B("AT"), B("b6", I, CW), F.Copy)
+            if t == 0:
+                late()
         else:
             at(t, "of")
-            act(B("F0"), B(f1), F.Identity, I, bias=-FO)
-            dma("Y", "yf", "F0", 2.5, False)
-            dma("Y", "ys", "OS", 2.5, False)
+            plus("S", B("F0"), B(f1), -FO)
+            dma("Y", B("yf"), B("F0"), 2.5, False)
+            dma("Y", B("ys"), B("OS"), 2.5, False)
             at(t, "yp")
-            for h in range(2):
-                MS([(B(nb, 0, 12), slide("W0", r), B("SWH", I * t + r, I * t + I, 16)) for r in range(8 * h, 8 * h + 8)], h == 0, h == 1, 12)
-            ts(H1, B("PH", 12 * t, 12 * t + 12), float(PLN - ROT), None, A.add, None, 12)
+            tiny(B("b4", 0, 12), "W0", "SWH", True, True, 12, I * t, I * t + I)
+            plus("S", H1, PH, float(PLN - ROT), 12)
             ts(H2, H1, PLN - 1, None, A.bitwise_and, None, 12)
             tt(B("PK", 24, 36), B("PK", 12, 24), H2, A.add, 12, 2)
-            tt(B("PK", 36, 48), B(nb, 0, 12), B("PK", 24, 36), A.mult, 12)
+            tt(B("PK", 36, 48), B("b4", 0, 12), B("PK", 24, 36), A.mult, 12)
             tt(B("YPF"), B("PK", 36, 48), B("YPF"), A.max, 12, 2)
-            dma("S", "yp", "YPF", 2.5, False)
-            dma("Y", "yx", "YX", 2.5, False)
+            dma("S", B("yp"), B("YPF"), 2.5, False)
+            dma("Y", B("yx"), B("YX"), 2.5, False)
     return ops
 
 
@@ -548,7 +528,7 @@ def _deps(ops):
 def _schedule(ops, data, order):
     at, seen, turn = {}, {}, []
     for i, o in enumerate(ops):
-        turn.append(max(int(o[5]["due"] // 100), 0))
+        turn.append(int(o[5]["due"] // 100))
         s = (turn[i], o[0], o[5]["step"] or "c")
         seen[s] = seen.get(s, 0) + 1
         at[turn[i], o[0], s[2] + str(seen[s])] = i
@@ -566,7 +546,7 @@ def _schedule(ops, data, order):
         for l in full.values():
             while l and all(j in done for j in data[l[0]] + order[l[0]]):
                 done.add(l[0])
-                out.append((l.pop(0), 0, 0))
+                out.append(l.pop(0))
         assert len(out) > n
     return out
 
@@ -579,12 +559,11 @@ def _plan():
         ops = _build()
         data, order, groups = _deps(ops)
         sched = _schedule(ops, data, order)
-        place = {x[0]: k for k, x in enumerate(sched)}
+        place = {i: k for k, i in enumerate(sched)}
         for grp in groups:
-            begins = ops[grp[0]][5]["fl"][0]
             grp.sort(key=lambda i: place[i])
             for i in grp:
-                ops[i][5]["fl"][:] = [begins and i == grp[0], i == grp[-1]]
+                ops[i][5]["fl"][:] = [i == grp[0], i == grp[-1]]
         _PLAN["ops"], _PLAN["data"], _PLAN["sched"] = ops, data, sched
     return _PLAN["ops"], _PLAN["data"], _PLAN["sched"]
 
@@ -638,7 +617,7 @@ def rank_program(g, core, T, topo):
 
     sent = 0
     dmas = []
-    for (i, st, fin) in sched:
+    for i in sched:
         q, fn, rd, wr, cost, kw = ops[i]
         if q == "R":
             seq[i] = ("arr%d" % kw["arr"], (N - 1) * EN)
@@ -673,14 +652,13 @@ def rank_program(g, core, T, topo):
             ins.then_inc(T.sem[s], 16)
             seq[i] = (s, 16)
             dmas.append(s)
-            clock[i] = dict(kn)
         else:
             s = "q" + q
             for x in (ins if q == "T" else [ins]):
                 cnt[s] = cnt.get(s, 0) + 1
                 x.then_inc(T.sem[s], 1)
             seq[i] = (s, cnt[s])
-            clock[i] = dict(kn)
+        clock[i] = dict(kn)
     g.wait_ge(T.sem.sent, sent)
     for s, v in cnt.items():
         g.wait_ge(T.sem[s], v)

from concourse.bass import DstId, RemoteDMATransfer
from concourse.mybir import AluOpType, ActivationFunctionType

A = AluOpType
F = ActivationFunctionType
I, W, PLN, TURNS, BLK, N = 192, 3072, 2048, 8, 24, 8
NC = 8
CW = 2 * I
PA = 64
EN = 4
CEN = 1536.0
BIG = 8192.0
FO = 1280.0
ROT = 712
WAYS = "ttbbmm"
BF, HF, FL, I32, U16 = "bfloat16", "float16", "float32", "int32", "uint16"
C = dict(
    plan=(("V", 0, 32), ("S", 32, 64), ("S", 64, 128), ("S", 128, 192)),
    plan0=(("S", 0, 64), ("S", 64, 112), ("V", 112, 192)),
    to=0.0, vo=0.055, tr=0.57, so=0.12, fly=2.5, ga=1.5, sa=3.5, xl=4.0, pl=8.0)
SEQ = """
cV c1 c5 c2 c18 c3 c4 c7 c8 c6 c9 c10 c14 c11 c15 c21 c13 c17 c19 c16 c12 c22 c23 c20 ; cS c2 c1 c3 ; cT ;
cG c1 c18 c4 c2 c14 c3 c5 c9 c13 c16 c19 c10 c8 c12 c6 c17 c7 c11 c15 ;
V pk1 xs01 xs21 xs41 yx1 xe01 pk2 bs2 mn11 mn32 h11 mn12 mn22 mn21 mn31 e01 s01 xa11 mn02 mn01 dx21 pp41 dx31 pp51 h12 pp52 rs1 h31 set1
  rp1 ts1 pk3 rp2 yp1 rp3 pk4 wd1 pk5 wd2 bs1 y1 yp2 y2 qq1 pk6 e1 pk7 new1 e2 yp3 ex1 m1 yp4 m2 ex2 ex3 wr1 ex4 ;
S s01 xs11 xs31 xs51 e01 xe01 xe21 xa01 xa11 xe11 pp11 pp21 r21 ra1 pp31 ha1 h21 s02 h31 cand1 yp1 pk1 an1 pk2 sw1 f1 y1 ex1 of1 a1 own1
  wr1 ex2 eu1 yp2 su1 ;
T yx1 yx3 yx4 pre03 pre02 pre01 yx2 sx03 sx01 sx02 sx04 sx14 sx11 sx12 sx13 zp1 pr701 u1 u2 sx24 zq1 pre04 sz1 pr601 dx01 sx21 sv11 sv32
  dx11 sv12 pr702 dz01 dx42 sx22 sz2 dz11 sv21 sv22 sv31 dx51 pe01 pe02 bn02 ax11 ax01 az11 sm1 az01 ax51 dx41 sx23 dx52 bn01 ax42 ax41 ax52
  sv02 sv01 sp01 sp41 sp11 sp21 bn03 sp51 sp52 sp31 dt1 ts1 an1 wp2 wp1 rp1 rp2 an2 yw1 wc1 ce3 yw7 ce1 ce4 ce2 y1 y2 qq1 yp1 yp2 a1 qq2
  sh1 sh3 new1 dm1 sh2 ex1 a2 es1 m2 m1 wr1 yw5 +pr61 +pre3 +pr72 yw6 yw4 +pr71 +pre2 yw3 yw8 +pe1 +pre5 +pre1 +pe2 +pre6 yw2 +pre7 +pre4
"""

SCRATCH = {}
for _n, _w, _d in [
        ("X", W, BF), ("XS", W, BF), ("XE", W, BF), ("MN", W, HF), ("MX", W, BF), ("DE", 1024, BF),
        ("PLT", PLN + ROT, I32), ("SI", I, I32), ("THI", I, I32), ("PI", 12, I32),
        ("S16", I, HF), ("E16", I, HF), ("CAND", I, HF), ("BND", I, HF), ("AT", I, BF), ("SWH", TURNS * I, BF),
        ("SU", I, U16), ("EU", I, U16), ("TU", 12, U16), ("PU", 12, U16), ("P0", 12, U16), ("MU", 12, U16),
        ("R2", I, I32), ("RS", I, BF), ("RP", I, BF), ("AN", I, BF), ("SET", I, BF), ("R16", I, HF), ("QQ", I, FL),
        ("TS", I, HF), ("TP", I, HF), ("TC", I, HF),
        ("F0", I, BF), ("FA", I, HF), ("FB", I, HF), ("YD", I, FL), ("WR", I, I32), ("QB", 12, HF),
        ("HH", 36, I32), ("PH", 12 * TURNS, I32), ("KT", 12 * TURNS, FL), ("PK", 12 * TURNS, FL), ("KK", 180, FL),
        ("K0", 12, I32), ("PE", 12, I32), ("YPF", 12, FL), ("OS", I, FL), ("OX", 12 * TURNS, FL), ("YX", I, FL), ("FM", I, FL),
        ("ip", 1, I32), ("ig", 1, I32), ("il", 1, I32), ("ibase", 12, I32), ("gf", 1, FL), ("g15", 1, FL), ("l21", 1, FL),
        ("r16", 1, FL), ("row", 144, FL), ("grow", 128, FL), ("base", 12, FL),
        ("cv", CW, BF), ("cz", CW, HF), ("ct", I, BF), ("cb", I, BF), ("c24", 12, BF), ("zero", 128, BF),
        ("W1", 144, BF), ("W2", 144, BF), ("Wm", 144, BF), ("Wmh", 144, BF), ("Wu", 144, BF), ("W0", 144, BF),
        ("Ib", 128, BF), ("Im", 128, BF), ("Ih", 128, BF), ("I32", 128, BF), ("I64m", 128, BF),
        ("OB", 128, BF), ("OBh", 128, BF), ("OBB", 128, BF), ("OBm", 128, BF),
        ("BL", 128, BF), ("BLm", 128, BF), ("BIL", 128, BF), ("Sh", 128, BF), ("NT", 128, BF), ("Tp", 128, BF), ("Tp0", 128, BF),
        ("IC0", 512, BF), ("IC", 16 * 128, BF)]:
    SCRATCH[_n] = ("sbuf", [128, _w], _d)
for _t in range(TURNS):
    SCRATCH["L%d" % _t] = ("sbuf", [128, I], BF)
    SCRATCH["Y%d" % _t] = ("sbuf", [128, I], BF)
for _t in (0, 1, 2, 3, 6, 7):
    SCRATCH["b%d" % _t] = ("psum", [128, 512], FL)
SCRATCH["b45"] = ("psum", [128, 1024], FL)
SEMAPHORES = ["qV", "qS", "qT", "qG", "sent"] + ["arr%d" % t for t in range(TURNS)] + ["dm%d" % k for k in range(12)]


def _build():
    ops = []
    CY = 0.00083
    GA = C["ga"]
    now = [0.0, ""]

    def add(q, fn, rd, wr, cost, **kw):
        ops.append([q, fn, [r for r in rd if r], [r for r in wr if r], cost, dict(kw, due=now[0], step=now[1])])

    def at(t, step):
        now[:] = [100.0 * (t + 1), step]

    def B(name, a=None, b=None, st=None):
        if name in ("b4", "b5"):
            a, b, o = a or 0, b or 512, 512 * (name == "b5")
            return (lambda T: T.b45[:, o + a:o + b:st or 1]), (name, a, b)
        if a is None:
            return (lambda T: T[name][:]), (name, 0, 1 << 20)
        if st is None:
            return (lambda T: T[name][:, a:b]), (name, a, b)
        return (lambda T: T[name][:, a:b:st]), (name, a, b)

    def IX(win, off, a, b, c=0, d=W):
        return (lambda T: T[win][:, c:d].indirect(T[off][:, a:b])), (win, c, d), (off, a, b)

    def slide(name, k):
        return (lambda T: T[name][:, 15 - k:15 - k + 128]), (name, 0, 1 << 20)

    def val(x, T):
        return x[0](T) if isinstance(x, tuple) else x

    def regs(*xs):
        return [r for x in xs if isinstance(x, tuple) for r in x[1:]]

    def vcost(n, f):
        return C["vo"] + max(64, n * f) * CY

    def MM(out, lhsT, rhs, start, stop, n=I):
        MS([(out, lhsT, rhs)], start, stop, n)

    def MS(mm, start, stop, n):
        fl = [start, stop]
        add("T", lambda g, T: [g.tensor.matmul(o[0](T), w[0](T), r[0](T), fl[0] and k == 0, fl[1] and k == len(mm) - 1) for k, (o, w, r) in enumerate(mm)],
            [x for o, w, r in mm for x in regs(w, r)], [x for o, w, r in mm for x in regs(o)], len(mm) * (max(64, n) * CY * C["tr"] + C["to"]), fl=fl)

    def tt(o, a, b, op, n=I, f=1.0):
        add("V", lambda g, T: g.vector.tensor_tensor(o[0](T), a[0](T), b[0](T), op), regs(a, b), regs(o), vcost(n, f))

    def ts(o, a, s1, s2, op0, op1, n=I, f=1.0):
        def fn(g, T):
            if op1 is None:
                return g.vector.tensor_scalar(o[0](T), a[0](T), val(s1, T), None, op0)
            return g.vector.tensor_scalar(o[0](T), a[0](T), val(s1, T), val(s2, T), op0, op1)
        add("V", fn, regs(a, s1, s2), regs(o), vcost(n, f))

    def tc(o, a, n, f=1.0):
        add("V", lambda g, T: g.vector.tensor_copy(o[0](T), a[0](T)), regs(a) + list(o[2:]), [o[1]], vcost(n, f))

    def fill(o, c, n):
        add("V", lambda g, T: g.vector.memset(o[0](T), c), [], regs(o), vcost(n, 0.5))

    def act(o, a, f, n=I, fc=1.0, **kw):
        add("S", lambda g, T: g.scalar.activation(o[0](T), a[0](T), f, **kw), regs(a), regs(o), (0.065 if len(a) > 2 else C["so"]) + n * fc * CY)

    def plus(q, o, a, c, n=I, f=1.0):
        if q == "V":
            if c:
                ts(o, a, c, None, A.add, None, n, f)
            else:
                tc(o, a, n, f)
        elif c:
            act(o, a, F.Identity, n, f, bias=c)
        else:
            act(o, a, F.Copy, n, f)

    def tiny(out, w, src, first, last, n=12, a=0, b=I):
        for h in range(2):
            MS([(out, slide(w, r), B(src, a + r, b, 16)) for r in range(8 * h, 8 * h + 8)], first and h == 0, last and h == 1, n)

    nd = [0]

    def dma(q, dst, src, cost, load):
        nd[0] += 1
        add(q, lambda g, T: (g.sync if q == "Y" else g.scalar).dma_start(dst[0](T), src[0](T)),
            [] if load else regs(src), regs(dst) if load else [], cost, dma=nd[0] - 1)

    x, p = C["xl"], C["pl"]
    dma("S", B("SI"), B("s0"), 2.5, True)
    dma("S", B("PI"), B("p0"), 2.5, True)
    dma("Y", B("X"), B("x0"), x, True)
    dma("Y", B("L0"), B("z0"), x + 0.1, True)
    dma("Y", B("PLT", ROT, ROT + PLN), B("pl"), p, True)
    dma("Y", B("THI"), B("th"), p + 0.2, True)
    dma("Y", B("F0"), B("f0"), p + 0.3, True)
    dma("Y", B("PLT", 0, ROT), B("pl", PLN - ROT, PLN), p + 1.2, True)

    def G(fn, rd, wr, n):
        add("G", fn, regs(*rd), regs(wr), 0.15 + 2 * n * CY)

    def iota(dst, pat, base, cm, n, rd=()):
        kw = {} if SCRATCH[dst][2] == I32 else {"allow_small_or_imprecise_dtypes": True}
        G(lambda g, T: g.iota(T[dst][:], pat, int(base), cm, **kw), rd, B(dst), n)

    def sel(dst, src, pat, op, fill_, base, cm, n=128):
        G(lambda g, T: g.affine_select(T[dst][:], T[src][:], pat, op, fill_, base, cm), [B(src)], B(dst), n)
    iota("ip", [[0, 1]], 0, 1, 1)
    iota("row", [[1, 144]], 0, 0, 144)
    iota("grow", [[1, 8], [0, 16]], 0, 0, 128)
    fill(B("cv"), -11.0 / 512, CW)
    fill(B("zero"), 0.0, 128)
    act(B("AT"), B("cv", 0, I), F.Sigmoid, I, 9.0, scale=30000.0)
    ts(B("cz"), B("cv"), 0.0, -127.9375, A.mult, A.add, CW, 0.5)
    ts(B("ig"), B("ip"), 4, None, A.arith_shift_right, None, 1)
    ts(B("il"), B("ip"), 15, None, A.bitwise_and, None, 1)
    tc(B("gf"), B("ig"), 1)
    ts(B("g15"), B("ig"), 16.0, 15.0, A.mult, A.add, 1)
    ts(B("l21"), B("il"), 2.0, 1.0, A.mult, A.add, 1)
    ts(B("r16"), B("il"), -16.0, -7.5, A.mult, A.add, 1)
    ts(B("W1"), B("row"), B("g15"), None, A.is_equal, None, 144)
    ts(B("OB"), B("grow"), B("gf"), None, A.is_equal, None, 128)
    for dst, src, c, n in (("Wmh", "W1", -0.5, 144), ("OBh", "OB", 0.5, 128), ("Wu", "W1", B("l21"), 144), ("Wm", "W1", -1.0, 144),
                           ("W2", "W1", 2.0, 144), ("OBB", "OB", -BIG, 128)):
        ts(B(dst), B(src), c, None, A.mult, None, n, 0.5)
    fill(B("OBm"), 0.0, 128)
    for k in range(4):
        if WAYS[2 + k] == "m":
            ts(B("OBm", k, 128, 4), B("OB", k, 128, 4), -1.0, None, A.mult, None, 32, 0.5)
    col, first = [[1, 128]], [[0, 8], [1, 16]]
    for x, c in (("Ib", 1.0), ("I32", 32.0), ("I64m", -64.0), ("Ih", 0.5), ("Im", -1.0)):
        sel(x, "zero", col, A.not_equal, c, 0, -1)
    iota("cb", [[0, I]], -BIG, 0, I)
    sel("BLm", "OBB", col, A.is_gt, 0.0, 0, -1)
    sel("BIL", "BLm", col, A.not_equal, BIG, 0, -1)
    sel("Tp0", "Ib", first, A.is_equal, 0.0, 0, 0)
    sel("Sh", "OB", col, A.is_equal, 0.0, -1, -1)
    iota("c24", [[0, 12]], 16 * CEN, 0, 12)
    sel("NT", "Ih", first, A.not_equal, 0.0, 0, 0)
    sel("Tp", "OB", first, A.is_equal, 0.0, 0, 0)
    iota("ct", [[0, I]], 15 * CEN, 0, I)
    iota("ibase", [[-256, 12]], 0, 0, 12)
    sel("W0", "W1", [[-16, 9], [0, 16]], A.is_equal, 0.0, 0, 1, 144)

    def late():
        iota("KT", [[PLN, TURNS], [0, 12]], 2 * PLN - ROT, 0, 96, [B("Y0")])
        for h in range(4):
            o = 512 * h
            iota("IC0", [[1, 4], [0, 128]], 1 + 4 * h, 0, 512, [B("Y0")])
            G(lambda g, T, o=o: g.affine_select(T.IC[:, o:o + 512], T.IC0[:], [[0, 4], [-1, 128]], A.is_equal, 0.0, 0, 1), [B("IC0")], B("IC", o, o + 512), 512)

    tc(B("P0"), B("PI"), 12)
    tc(B("SU"), B("SI"), I)
    tc(B("KK", 84, 96), B("PI"), 12)
    at(0, "s0")
    plus("S", B("S16"), B("SI"), -CEN)
    ts(B("BND"), B("THI"), -2048.0, 1.0 / 64, A.add, A.mult)
    plus("S", B("FA"), B("F0"), FO)
    at(0, "e0")
    plus("S", B("EU"), IX("PLT", "P0", 0, 12, ROT, ROT + PLN), 0.0, I, GA)
    plus("V", B("E16"), IX("PLT", "P0", 0, 12, ROT, ROT + PLN), -CEN, I, GA)
    at(0, "bs")
    ts(B("BL"), B("BLm"), -1.0, None, A.mult, None, 128, 0.5)
    ts(B("base"), B("ibase"), B("r16"), None, A.add, None, 12)

    H, VL, UP, PC, WC, SC, ES = ("b2", 0), ("b2", I), ("b3", 0), ("b6", 0), ("b4", 0), ("b7", 0), ("b7", I)
    FS, CE, SH = ("b1", 0), ("b1", I), ("b2", 0)

    def P(reg, a=0, b=I):
        return B(reg[0], reg[1] + a, reg[1] + b)

    for t in range(TURNS):
        L, Y = "L%d" % t, "Y%d" % t
        f0, f1 = ("FA", "FB") if t % 2 == 0 else ("FB", "FA")
        last = t == TURNS - 1
        for k in range(6):
            at(t, "xs%d" % k)
            plus("VS"[k % 2], B("XS", 512 * k, 512 * k + 512), IX("X", "SU", 32 * k, 32 * k + 32), -128.0, 512, GA)
        for q, a, b in C["plan"] if t else C["plan0"]:
            at(t, ("xe%d" if t else "xa%d") % (a // PA))
            plus(q, B("XE", 16 * a, 16 * b), IX("X", "EU", a, b), 0.0, 16 * (b - a), GA)
        at(t, "pre" if t else "pre0")
        MM(B("b0", 0, CW), B("Ib"), B("cz"), True, False, CW)
        if t:
            MM(P(H), B("I32"), B("BND"), True, False)
        else:
            MM(P(H), B("OBh"), B(L), True, False)
        MM(P(VL), B("OB"), B("cz", 0, I), False, False)
        MM(P(VL), B("I32"), B("cv", 0, I), False, False)
        if not t:
            at(t, "bn0")
            MM(P(H), B("I32"), B("BND"), False, False)
        MM(P(UP), B("I64m"), B("BND"), True, False)
        if t:
            MM(P(H), B("I32"), B("AT"), False, False)
            MM(P(UP), B("I64m"), B("AT"), False, False)
        at(t, "pr6" if t else "pr60")
        MM(P(PC), B("Ib"), B("cb"), True, False)
        at(t, "pr7" if t else "pr70")
        MM(P(SC), B("Ib"), B("S16"), True, False)
        MM(P(ES), B("Im"), B("S16"), False, False)
        at(t, "pe" if t else "pe0")
        MM(P(PC), B("Ib"), B("E16"), False, False)
        MM(P(ES), B("Ib"), B("E16"), False, False)
        if last:
            at(t, "yx")
            n = 12 * t
            tiny(B("b1", 0, n), "W0", "SWH", True, False, n, 0, t * I)
            tiny(B("b1", n, n + 12), "W0", "AT", False, True)
            tc(B("OX", 0, n + 12), B("b1", 0, n + 12), n + 12)
            at(t, "pk")
            tt(B("PK", 0, n), B("PH", 0, n), B("KT", 0, n), A.add, n, 2)
            tt(B("KK", 0, n), B("OX", 0, n), B("PK", 0, n), A.mult, n, 2)
            act(B("PK", 0, 12), B("OX", n, n + 12), F.Copy, 12, scale=float(PLN))
            for a, w in ((0, 48), (96, 24)):
                tt(B("KK", a + 2 * w, a + 3 * w), B("KK", a, a + w), B("KK", a + w, a + 2 * w), A.max, w, 2)
            tt(B("K0"), B("KK", 144, 156), B("KK", 156, 168), A.max, 12, 2)
            ts(B("PE"), B("K0"), PLN - 1, None, A.bitwise_and, None, 12)
            plus("S", B("PK", 12, 24), B("PK", 0, 12), float(PLN), 12)
            tt(B("YPF"), B("PK", 0, 12), B("PE"), A.add, 12)
        for c in range(3):
            at(t, "sx%d" % c)
            a, b = PA * c, PA * c + PA
            for h in range(4):
                MS([(P(H, a, b), slide("Wmh", k), B("XS", 16 * a + k, 16 * b, 16)) for k in range(4 * h, 4 * h + 4)], False, False, PA)
        at(t, "zp")
        MS([(B("b0", m, CW, 2), B("Ib"), B(L)) for m in range(2)], False, True, I)
        at(t, "u")
        tiny(B("b5", 0, 12), "Wu", L, True, True)
        at(t, "sz")
        MM(P(VL), B("OB"), B(L), False, False)
        if t:
            MM(P(H), B("OBh"), B(L), False, False)
        at(t, "h1")
        H1, H2, H3 = [B("HH", 12 * k, 12 * k + 12) for k in range(3)]
        PH = B("PH", 12 * t, 12 * t + 12)
        tc(H1, B("b5", 0, 12), 12)
        ts(H2, H1, 4095, None, A.bitwise_and, None, 12)
        at(t, "h2" if t else "ha")
        act(H3, H2, F.Square, 12, bias=592.0)
        at(t, "h3")
        ts(PH, H3, 5, PLN - 1, A.arith_shift_right, A.bitwise_and, 12)
        plus("S", B("PU"), PH, 0.0, 12)
        at(t, "cand")
        plus("S", B("CAND"), IX("PLT", "PU", 0, 12, 0, PLN), -CEN, I, GA)
        for q in range(NC):
            at(t, "mn%d" % (q // 2))
            tt(B("MN", CW * q, CW * q + CW), B("XS", q, W, NC), B("b0", 0, CW), A.min, CW)
            at(t, "sv%d" % (q // 2))
            MS([(P(VL), slide("Wm", q + NC * m), B("MN", CW * q + m, CW * q + CW, 2)) for m in range(2)], False, q == NC - 1, I)
        sums = []
        at(t, "zq")
        MS([(B("b1", m, 512, 4), B("Ib"), B(L, PA, I)) for m in range(4)], True, True, I - PA)
        at(t, "sm" if t else "bn0")
        MM(P(UP, PA, I), B("OBm"), B(L, PA, I), False, False, I - PA)
        for n, way in enumerate(WAYS):
            a, b, st, h = (0, PA, 2, n) if n < 2 else (PA, I, 4, n - 2)
            d, o = 16 // st, 512 * n
            xe, mx = B("XE", 16 * a + h, 16 * b, st), B("MX", o, o + 512)
            parts = [(a, b, o, 512)]
            if way == "t":
                bk = "b%d" % (4 + n)
                at(t, ("dx%d" if t else "ax%d") % n)
                MM(B(bk), B("Ib"), xe, True, False, 512)
                at(t, ("dz%d" if t else "az%d") % n)
                MS([(B(bk, m, 512, d), B("Im"), B(L, a, b)) for m in range(d)], False, True, b - a)
                at(t, "pp%d" % n)
                if n == 1:
                    add("S", lambda g, T: g.scalar.activation(T.MX[:, 0:1024], T.b45[:], F.Abs), regs(B("b4"), B("b5")), regs(B("MX", 0, 1024)),
                        C["so"] + 1024 * CY)
            elif way == "m":
                at(t, ("dx%d" if t else "ax%d") % n)
                for c in range(a, b, PA):
                    MS([(P(UP, c, c + PA), slide("Wm", st * m + h), B("XE", 16 * c + st * m + h, 16 * (c + PA), 16)) for m in range(d)], False, False, PA)
                at(t, "pp%d" % n)
                if n == 5:
                    parts = [(a, a + PA, o, 256), (a + PA, b, o + 256, 256)]
                for c, e, u, w in parts:
                    tt(B("MX", u, u + w), B("XE", 16 * c + h, 16 * e, st), B("b1", u - o, u - o + w), A.max, w)
            else:
                at(t, "dx%d" % n)
                tt(B("DE", o - 1024, o - 512), xe, B("b1"), A.subtract, 512)
                at(t, "pp%d" % n)
                act(mx, B("DE", o - 1024, o - 512), F.Abs, 512)
            for c, e, u, w in parts:
                sums.append(([(P(UP, c, e), slide("W2" if way == "m" else "W1", st * m + h), B("MX", u + m, u + w, d)) for m in range(d)], "sp%d" % n, e - c))
        for n, (mm, step, w) in enumerate(sums):
            at(t, step)
            MS(mm, False, n == len(sums) - 1, w)
        at(t, "r2" if t else "ra")
        act(B("R2"), P(VL), F.Relu, bias=0.15625)
        at(t, "rs")
        tt(B("RS"), P(H), B("R2"), A.is_gt)
        at(t, "set")
        tt(B("SET"), P(VL), B("R2"), A.is_le)
        at(t, "ts")
        MM(P(SC), B("BIL"), B("RS"), False, True)
        ts(B("TS"), P(SC), -BIG, -CEN, A.add, A.max)
        at(t, "dt")
        MM(P(WC), B("NT"), B("cb"), True, False)
        at(t, "wp")
        MM(P(WC), B("OBB"), B("RS"), False, False)
        MM(P(PC), B("OBB"), B("RS"), False, False)
        at(t, "an")
        MM(B("b0", I, CW), B("OBh"), B("RS"), True, False)
        MM(B("b0", I, CW), B("I64m"), B("SET"), False, True)
        act(B("AN"), B("b0", I, CW), F.Sigmoid, scale=1000.0, bias=-250.0)
        at(t, "wd")
        tt(P(ES), P(ES), B("AN"), A.mult)
        tt(B("R16"), P(ES), B("S16"), A.add)
        at(t, "qq")
        MM(B("b0", 0, I), B("Ih"), B("cb"), True, False)
        MM(B("b0", 0, I), B("BL"), B("RS"), False, True)
        tt(B("QQ"), B("b0", 0, I), B("R16"), A.min)
        at(t, "sh")
        MM(P(SH), B("Sh"), B("R16"), True, False)
        MM(P(SH), B("BLm"), B("RS"), False, False)
        MM(P(SH), B("Tp0"), B("ct"), False, False)
        at(t, "ce")
        MM(P(FS), B("Ih"), B(f0), True, False)
        MM(P(FS), B("Ih"), B(L), False, last)
        if not last:
            MM(P(CE), B("Im"), B("E16"), False, False)
            MM(P(CE), B("Ib"), B("CAND"), False, True)
        at(t, "f")
        plus("S", B(f1), P(FS), FO / 2 - 0.25)
        at(t, "wc")
        MM(P(WC), B("Tp0"), B("CAND"), False, False)
        at(t, "rp")
        ts(B("RP"), P(UP), 2048.0, None, A.is_lt, None)
        MM(P(PC), B("BIL"), B("RP"), False, True)
        MM(P(WC), B("OBB"), B("RP"), False, True)
        tt(B("TP"), P(PC), B("TS"), A.max)
        tt(B("TC"), P(WC), B("TP"), A.max)
        at(t, "y")
        tiny(B("b5", 16, 28), "W1", "TC", True, True)
        plus("V", B("TU"), B("b5", 16, 28), 16 * CEN, 12)
        tt(B("YD"), IX("X", "TU", 0, 12), B(f1), A.subtract, I, GA)
        act(B(Y), B("YD"), F.Abs, bias=FO)
        if not last:
            add("G", ("send", t), [(Y, 0, I)], [], 1.2, send=t)
            Ln = "L%d" % (t + 1)
            a = BLK * ((-t) % N)
            add("R", None, [], [(Ln, c, d) for c, d in ((0, a), (a + BLK, I)) if d > c], C["fly"], arr=t)
            at(t, "own")
            act(B(Ln, a, a + BLK), B("YD", a, a + BLK), F.Abs, BLK, bias=FO)
        MB = B("b5", 32, 44)
        at(t, "dm")
        MM(MB, B("Ib"), B("c24"), True, False, 12)
        at(t, "m")
        tiny(MB, "W1", Y, False, True)
        tt(B("QB"), MB, B("base"), A.add, 12)
        tt(B("MU"), MB, B("QB"), A.subtract, 12)
        at(t, "es")
        MM(B("b0", 0, I), B("Ih"), B(L), True, False)
        at(t, "wr")
        MM(B("b0", 0, I), B("Ih"), B(Y), False, True)
        plus("S", B("WR"), B("b0", 0, I), -0.25)
        if not last:
            tc(IX("X", "MU", 0, 12), B("WR"), I, C["sa"])
        else:
            at(t, "yw")
            for h in range(8):
                MS([(B("b3", 0, I), B("IC", 128 * c, 128 * c + 128), B("X", c, W, 16)) for c in range(2 * h, 2 * h + 2)], h == 0, h == 7, I)
            at(t, "ex")
            MM(B("b1", 0, I), B("OB"), B(Y), True, True)
            plus("S", B("MN", 0, I), B("b1", 0, I), 24568.5)
            tt(B("FM"), B("b1", 0, I), B("MN", 0, I), A.subtract)
            act(B("b1", I, CW), B("FM"), F.Identity, scale=-1.0, bias=-24577.0)
            tt(B("YD"), IX("X", "MU", 0, 12), B("WR"), A.subtract, I, GA)
            tt(B("FM"), B("b1", I, CW), B("YD"), A.mult)
            tt(B("YX"), B("b3", 0, I), B("FM"), A.add)
        at(t, "new")
        MM(P(SH), B("Tp"), B("TC"), False, True)
        tt(B("S16"), P(SH), B("QQ"), A.max)
        at(t, "su")
        plus("S", B("OS" if last else "SU"), B("S16"), CEN)
        at(t, "sw")
        SW = B("SWH", I * t, I * t + I)
        act(SW, P(WC), F.Sigmoid, scale=0.1, bias=537.5)
        if not last:
            at(t, "e")
            tt(P(CE), P(CE), SW, A.mult)
            tt(B("E16"), P(CE), B("E16"), A.add)
            at(t, "eu")
            plus("S", B("EU"), B("E16"), CEN)
            at(t, "a")
            MM(B("b6", I, CW), B("Ib"), B("AT"), True, False)
            MM(B("b6", I, CW), B("Ib"), SW, False, True)
            act(B("AT"), B("b6", I, CW), F.Copy)
            if t == 0:
                late()
        else:
            at(t, "of")
            plus("S", B("F0"), B(f1), -FO)
            dma("Y", B("yf"), B("F0"), 2.5, False)
            dma("Y", B("ys"), B("OS"), 2.5, False)
            at(t, "yp")
            tiny(B("b4", 0, 12), "W0", "SWH", True, True, 12, I * t, I * t + I)
            plus("S", H1, PH, float(PLN - ROT), 12)
            ts(H2, H1, PLN - 1, None, A.bitwise_and, None, 12)
            tt(B("PK", 24, 36), B("PK", 12, 24), H2, A.add, 12, 2)
            tt(B("PK", 36, 48), B("b4", 0, 12), B("PK", 24, 36), A.mult, 12)
            tt(B("YPF"), B("PK", 36, 48), B("YPF"), A.max, 12, 2)
            dma("S", B("yp"), B("YPF"), 2.5, False)
            dma("Y", B("yx"), B("YX"), 2.5, False)
    return ops


def _deps(ops):
    data, order = [], []
    acc = {}
    banks = {}
    sends = {}
    groups = []
    for i, (q, fn, rd, wr, cost, kw) in enumerate(ops):
        dd, oo = set(), set()
        seen = {}
        for lst, w in ((rd, False), (wr, True)):
            for (n, a, b) in lst:
                if n[0] == "b" and n[1:].isdigit():
                    e = seen.get(n)
                    if e is None:
                        e = banks.setdefault(n, {"q": q, "cur": [], "prev": []})
                        if e["q"] != q:
                            e["prev"], e["cur"], e["q"] = [x[0] for x in e["cur"]], [], q
                        seen[n] = e
                        dd.update(e["prev"])
                    if q == "T":
                        if e["cur"] and e["cur"][-1][0] == i:
                            continue
                        if e.get("shut", True):
                            e["old"], e["grp"] = e.get("grp", []), []
                            groups.append(e["grp"])
                        oo.update([j for j in e["grp"] if ops[j][3][0][1] < b and a < ops[j][3][0][2]][:1])
                        e["grp"].append(i)
                        e["shut"] = kw["fl"][1]
                        oo.update(e["old"])
                    else:
                        for (j, c, d, w2) in e["cur"]:
                            if j != i and (w or w2) and c < b and a < d:
                                dd.add(j)
                    e["cur"].append((i, a, b, w))
                else:
                    l = acc.setdefault(n, [])
                    for (j, c, d, w2) in l:
                        if j != i and (w or w2) and c < b and a < d:
                            dd.add(j)
        for lst, w in ((rd, False), (wr, True)):
            for (n, a, b) in lst:
                if n[0] == "b" and n[1:].isdigit():
                    continue
                l = acc[n]
                if w:
                    l[:] = [x for x in l if not (a <= x[1] and x[2] <= b and x[0] != i)]
                l.append((i, a, b, w))
        if "send" in kw:
            sends[kw["send"]] = i
        if "arr" in kw:
            oo.add(sends[kw["arr"]])
        dd.discard(i)
        oo -= dd
        data.append(sorted(dd))
        order.append(sorted(oo))
    return data, order, groups


def _schedule(ops, data, order):
    at, seen, turn = {}, {}, []
    for i, o in enumerate(ops):
        turn.append(int(o[5]["due"] // 100))
        s = (turn[i], o[0], o[5]["step"] or "c")
        seen[s] = seen.get(s, 0) + 1
        at[turn[i], o[0], s[2] + str(seen[s])] = i
    seq = {w.split()[0]: w.split()[1:] for w in SEQ.split(";")}
    full = {q: [i for i, o in enumerate(ops) if o[0] == q and (q != "G" or turn[i])] for q in "GYR"}
    full["G"] = [at[0, "G", k] for k in seq["cG"]] + full["G"]
    for q in "VST":
        full[q] = [at[0, q, k] for k in seq["c" + q]]
        for u in range(TURNS + 1):
            keys = [(u + (k[0] == "+"), q, k.lstrip("+")) for k in seq[q]]
            full[q] += [at[k] for k in keys if k[0] and k in at]
    done, out = set(), []
    while len(out) < len(ops):
        n = len(out)
        for l in full.values():
            while l and all(j in done for j in data[l[0]] + order[l[0]]):
                done.add(l[0])
                out.append(l.pop(0))
        assert len(out) > n
    return out


_PLAN = {}


def _plan():
    if not _PLAN:
        ops = _build()
        data, order, groups = _deps(ops)
        sched = _schedule(ops, data, order)
        place = {i: k for k, i in enumerate(sched)}
        for grp in groups:
            grp.sort(key=lambda i: place[i])
            for i in grp:
                ops[i][5]["fl"][:] = [i == grp[0], i == grp[-1]]
        _PLAN["ops"], _PLAN["data"], _PLAN["sched"] = ops, data, sched
    return _PLAN["ops"], _PLAN["data"], _PLAN["sched"]


def _helpers(T, topo, core):
    return [h for h in topo.cores_of(core) if h != core and all(topo.may_write(h, d) for d in T.cores)][:N // 2 - 1]


def _transfer(T, topo, dst, engines, t, to, a, n):
    rid, pnc = topo.addr(dst)[:2]
    return RemoteDMATransfer(dst_ids=[DstId(rid=rid, pnc=pnc)], dma_engine_mask=sum(1 << e for e in engines), remote_sem=T.sem["arr%d" % t],
                             src=T["Y%d" % t][:, a:a + n], dst=T[to][:, a:a + n])


def _hand_on(g, core, T, topo):
    home = [c for c in topo.cores_of(core) if T.rank_of(c) is not None]
    if not home or core not in _helpers(T, topo, home[0]):
        return
    rank, k = T.rank_of(home[0]), _helpers(T, topo, home[0]).index(core)
    for t in range(TURNS - 1):
        p = [p for p in range(N // 2) if p != (-t) % N // 2][k]
        g.wait_ge(T.sem["arr%d" % t], EN)
        tr = []
        for n, b in enumerate((2 * p, 2 * p + 1)):
            dst = T.cores[(rank + b + t) % N]
            tr.append(_transfer(T, topo, dst, topo.engines(core, dst)[EN * n:EN * n + EN], t, "L%d" % (t + 1), BLK * b, BLK))
        g.remote_dma_fused(tr, local_sem=T.sem.sent)
    g.wait_ge(T.sem.sent, 2 * EN * (TURNS - 1))


def rank_program(g, core, T, topo):
    rank = T.rank_of(core)
    if rank is None:
        return _hand_on(g, core, T, topo)
    ops, data, sched = _plan()
    eng = {"V": g.vector, "S": g.scalar, "T": g.tensor, "G": g, "Y": g.sync}
    seq, cnt, clock = {}, {}, {}
    know = {q: {} for q in eng}

    def send(t):
        own = (-t) % N
        dst = T.cores[(rank + (own ^ 1) + t) % N]
        out = topo.engines(core, dst)[:EN]
        tr = []
        for k, (h, p) in enumerate(zip(_helpers(T, topo, core), [p for p in range(N // 2) if p != own // 2])):
            e = [x for x in topo.engines(core, h) if x not in out][EN * k:EN * k + EN]
            tr.append(_transfer(T, topo, h, e, t, "Y%d" % t, 2 * BLK * p, 2 * BLK))
        g.remote_dma_fused(tr, local_sem=T.sem.sent)
        g.remote_dma_fused([_transfer(T, topo, dst, out, t, "L%d" % (t + 1), BLK * (own ^ 1), BLK)], local_sem=T.sem.sent)
        return EN * (len(tr) + 1)

    sent = 0
    dmas = []
    for i in sched:
        q, fn, rd, wr, cost, kw = ops[i]
        if q == "R":
            seq[i] = ("arr%d" % kw["arr"], (N - 1) * EN)
            clock[i] = {}
            continue
        kn = know[q]
        need = {}
        before = [j for j in data[i] if "send" not in ops[j][5]]
        for j in before:
            s, v = seq[j]
            if kn.get(s, 0) < v:
                need[s] = max(need.get(s, 0), v)
        for j in sorted(before, key=lambda j: -j):
            s, v = seq[j]
            if s in need and need[s] == v:
                for s2, v2 in clock[j].items():
                    if s2 in need and s2 != s and need[s2] <= v2:
                        del need[s2]
        for j in before:
            s, v = seq[j]
            for s2, v2 in list(clock[j].items()) + [(s, v)]:
                if kn.get(s2, 0) < v2:
                    kn[s2] = v2
        for s, v in need.items():
            eng[q].wait_ge(T.sem[s], v)
        if "send" in kw:
            sent += send(kw["send"])
            continue
        ins = fn(g, T)
        if "dma" in kw:
            s = "dm%d" % kw["dma"]
            ins.then_inc(T.sem[s], 16)
            seq[i] = (s, 16)
            dmas.append(s)
        else:
            s = "q" + q
            for x in (ins if q == "T" else [ins]):
                cnt[s] = cnt.get(s, 0) + 1
                x.then_inc(T.sem[s], 1)
            seq[i] = (s, cnt[s])
        clock[i] = dict(kn)
    g.wait_ge(T.sem.sent, sent)
    for s, v in cnt.items():
        g.wait_ge(T.sem[s], v)
    for s in dmas:
        g.wait_ge(T.sem[s], 16)
